import numpy as np, ml_dtypes
CORES = [8,136,40,168]
N = 4
BF = ml_dtypes.bfloat16
def gentries(a):
    return np.ascontiguousarray(a.reshape(8, 16, -1).transpose(0, 2, 1)).reshape(8, -1)
def gtable(e):
    e = np.asarray(e); return np.ascontiguousarray(e.reshape(8, -1, 16).transpose(0, 2, 1)).reshape(128, -1).astype(np.int32)
W, C, T, S = 2560, 128, 4, 5
K = 16 * C; H = 8 * C
EX = np.exp(-0.015625 * np.arange(256))
def pack(Y, R, L, D, F):
    return {"wl": np.ascontiguousarray(Y.reshape(N, 128, W)).astype(np.float32).astype(BF), "rc": np.ascontiguousarray(R.reshape(N, 128, K)).astype(np.float32).astype(BF),
            "nm": np.stack([gtable(a) for a in L]), "dn": np.ascontiguousarray(D).astype(np.int32), "pl": np.ascontiguousarray(F).astype(np.int32)}
def names(rng):
    return np.ascontiguousarray(np.argsort(rng.random((N, 8, 2, W)), axis=-1)[..., :H]).reshape(N, 8, K)
def flows(rng):
    return np.argsort(rng.random((N, 8, W)), axis=-1)
def records(rng, k):
    v = rng.integers(0, 256, (N, 8, 16, k)); v[:, :, :15] = v[:, :, :15] >> rng.integers(0, 2, (N, 8, 1, k)); v[:, :, 15] = rng.integers(0, 160, (N, 8, k))
    return v * (rng.random((N, 8, 1, k)) > 0.125)
def thin(rng, R):
    share = rng.choice(np.array([0.0, 0.0, 0.25, 0.5]), (N, 8, 1, C, 1))
    return (R.reshape(N, 8, 16, C, 16) * (rng.random((N, 8, 1, C, 16)) >= share)).reshape(N, 8, 16, K)
def steady(rng, size, lo, hi):
    v = np.zeros((N, 8, 16, K), np.int64); v[:, :, :15] = size * (1 + np.argsort(rng.random((N, 8, 15, K)), axis=2)); v[:, :, 15] = rng.integers(lo, hi, (N, 8, K))
    return v
def alive(rng, m):
    return (np.argsort(rng.random((N, 8, C, 16)), axis=3) < m[..., None]).reshape(N, 8, 1, K)
def lanes(a):
    return np.repeat(a, 16, axis=2)[:, :, None, :]
def mixed(rng, k):
    v = 255 * rng.integers(0, 2, (N, 8, 16, k)); t = rng.integers(0, 5, (N, 8, 1, k))
    v = np.where(t == 0, 0, np.where((t == 1) | (t == 2), 255, v)); t = t[:, :, 0]
    v[:, :, 15] = np.where(t == 2, 0, np.where(t == 4, 255, v[:, :, 15]))
    return v
def strong(rng):
    a = rng.integers(130, 231, (N, 8, C)); c = np.repeat(a, 16, axis=2) + (rng.random((N, 8, K)) < 0.25).astype(np.int64)
    b = (16 * c + rng.integers(0, 9, (N, 8, K)))[:, :, None, :]; e = rng.integers(0, 4, (N, 8, 15, K)); o = np.argsort(rng.random((N, 8, 15, K)), axis=2)
    v = np.zeros((N, 8, 16, K), np.int64); v[:, :, :15] = b // 15 + (o < b % 15).astype(np.int64) + e - np.roll(e, 1, axis=2); v[:, :, 15] = c
    F = 256 * a + rng.integers(-1, 2, (N, 8, C)); F[..., C - 1] = 256 * a[..., C - 1] + 1
    return v, F
def setup_inputs(rng):
    return pack(records(rng, W), thin(rng, records(rng, K)), names(rng), flows(rng), rng.integers(0, 14001, (N, 8, C)))
def setup_inputs_spread(rng):
    def uneven(k):
        v = np.exp2(2 + 6 * rng.random((N, 8, 1, k))) * rng.random((N, 8, 16, k)); v[:, :, 15] = np.exp2(3 + 5 * rng.random((N, 8, k))) * rng.random((N, 8, k))
        return np.minimum(np.floor(v), 255)
    F = np.minimum(np.floor(np.exp2(16 * rng.random((N, 8, C)))), 61200)
    return pack(uneven(W), uneven(K), names(rng), flows(rng), F)
def setup_inputs_ends(rng):
    mid = 1 + rng.permutation(W - 2); P = np.concatenate([np.array([0, W - 1]), mid[:W // 2 - 2]]); Q = mid[W // 2 - 2:]
    fc = np.zeros(C, bool)
    fc[np.concatenate([np.array([0]), 1 + rng.permutation(C // 2 - 1)])[:C // 4]] = True
    fc[C - 1 - np.concatenate([np.array([0]), 1 + rng.permutation(C // 2 - 1)])[:C // 4]] = True
    fl = np.repeat(fc, 16); L = np.zeros((N, 8, K), np.int64); D = np.zeros((N, 8, W), np.int64)
    for q in range(N):
        for g in range(8):
            D[q, g, P] = rng.permutation(P); D[q, g, Q] = rng.permutation(Q)
            for h in range(2):
                a = np.flatnonzero(fl[h * H:(h + 1) * H]) + h * H; b = np.flatnonzero(~fl[h * H:(h + 1) * H]) + h * H
                p = np.concatenate([P[:2], rng.permutation(P[2:])])[:len(a)]
                L[q, g, a] = p if h == 0 else p[::-1]
                if h == 1:
                    L[q, g, a[-1]] = W - 1; L[q, g, a[-2]] = 0
                L[q, g, b] = rng.permutation(Q)[:len(b)]
    Y = mixed(rng, W); Y[..., P] = 255
    R = np.where(fl[None, None, None, :], 255, mixed(rng, K))
    short = (rng.random((N, 8, C)) < 0.3) & fc[None, None, :]; short[..., 0] = False; short[..., C - 1] = False
    hole = (np.arange(16) == rng.integers(0, 16, (N, 8, C, 1))) & short[..., None]
    R = np.where(hole.reshape(N, 8, 1, K), 0, R)
    near = (rng.random((N, 8, C)) < 0.25) & fc[None, None, :] & ~short; near[..., 0] = False; near[..., C - 1] = False
    R = np.where(lanes(near), 255 - (rng.random((N, 8, 16, K)) < 0.3).astype(np.int64), R)
    F = np.where(fc[None, None, :], np.where(near, 0, 61200), 61200 * rng.integers(0, 2, (N, 8, C)))
    far = int(rng.integers(1, N - 1)); m = rng.integers(1, 17, (8, C)); m[:, 0] = 3; m[:, C - 1] = 16
    live = (np.argsort(rng.random((8, C, 16)), axis=2) < m[..., None]).reshape(8, 1, K)
    z = ((np.arange(16)[None, :, None] == rng.integers(0, 15, (8, 1, K))) & live).astype(np.int64)
    R[far] = np.where(fl[None, None, :], z, R[far]); F[far] = np.where(fc[None, :], 0, 61200)
    return pack(Y, R, L, D, F)
def setup_inputs_corners(rng):
    s = np.arange(W); L = np.zeros((N, 8, K), np.int64); D = np.zeros((N, 8, W), np.int64)
    for q in range(N):
        for g in range(8):
            o = rng.permutation(W); cyc = np.zeros(W, np.int64); cyc[o] = np.roll(o, -1)
            D[q, g] = (s, (s + 1) % W, W - 1 - s, (s - 1) % W, cyc)[(q + g) % 5]
            A, B = ((s[:H], s[W - H:]), (s[0:2 * H:2], s[1:2 * H:2]), (s[W - H:], s[W - H:]), (rng.permutation(W)[:H], rng.permutation(W)[:H]))[(q + 3 * g) % 4]
            L[q, g, :H] = rng.permutation(A); L[q, g, H:] = rng.permutation(B)
    Y = rng.integers(30, 256, (N, 8, 16, W))
    Y[:, :, 15] = np.where(rng.random((N, 8, W)) < 0.7, rng.integers(14, 17, (N, 8, W)), rng.integers(0, 256, (N, 8, W)))
    Y = Y * (rng.random((N, 8, 1, W)) > 0.03125)
    kc = rng.integers(0, 4, (N, 8, C)); m = rng.choice(np.array([0, 1, 2, 15, 16, 16]), (N, 8, C))
    R = np.where(lanes(kc) < 2, steady(rng, 2, 14, 17) * alive(rng, m), records(rng, K))
    F = m * rng.choice(np.array([224, 240]), (N, 8, C)) + rng.integers(0, 2, (N, 8, C))
    F = np.where(kc < 2, F, np.where(kc == 2, rng.integers(0, 14001, (N, 8, C)), 61200 * rng.integers(0, 2, (N, 8, C))))
    return pack(Y, R, L, D, F)
def setup_inputs_crowd(rng):
    o = rng.permutation(W); L = np.zeros((N, 8, K), np.int64)
    for q in range(N):
        for g in range(8):
            L[q, g, :H] = rng.permutation(o[:H]); j = H + rng.integers(0, H)
            if q % 2 == 0:
                L[q, g, H:] = rng.permutation(o[:H])
                if g % 2 == 1: L[q, g, j] = o[rng.integers(H, W)]
            else:
                L[q, g, H:] = rng.permutation(o[H:])[:H]
                if g % 2 == 1: L[q, g, j] = o[rng.integers(0, H)]
    Y = records(rng, W); R = thin(rng, records(rng, K)); F = rng.integers(0, 14001, (N, 8, C))
    high = rng.integers(250, 256, (N, 8, 16, W - H)); high[:, :, 15] = rng.integers(232, 256, (N, 8, W - H)); Y[..., o[H:]] = high
    v, u = strong(rng); R[1::2, :, :, H:] = v[1::2, :, :, H:]; F[1::2, :, C // 2:] = u[1::2, :, C // 2:]
    return pack(Y, R, L, flows(rng), F)
def setup_inputs_calm(rng):
    Y = rng.integers(64, 256, (N, 8, 16, W)); Y[:, :, 15] = rng.integers(60, 256, (N, 8, W))
    m = rng.integers(0, 4, (N, 8, C)); pc = rng.random((N, 8, C)) < 0.25
    R = np.where(lanes(pc), records(rng, K), steady(rng, 4, 60, 256) * alive(rng, m))
    F = np.where(pc, rng.integers(0, 14001, (N, 8, C)), 480 * m + rng.integers(0, 2, (N, 8, C)))
    return pack(Y, R, names(rng), flows(rng), F)
def check_ranges(d):
    bad = []
    for k, lo, hi in (("wl", 0, 255), ("rc", 0, 255), ("nm", 0, W - 1), ("dn", 0, W - 1), ("pl", 0, 61200)):
        v = np.asarray(d[k]).astype(np.float64)
        if not (np.min(v) >= lo and np.max(v) <= hi): bad.append("range of " + k)
        elif np.any(v != np.floor(v)): bad.append("whole numbers of " + k)
    if not bad:
        if np.any(np.sort(d["dn"], axis=-1) != np.arange(W)): bad.append("a row of dn doesn't hold every site once")
        s = np.sort(np.stack([gentries(a) for a in d["nm"]]).reshape(N, 8, 2, H), axis=-1)
        if np.any(s[..., 1:] == s[..., :-1]): bad.append("names of a half in nm repeat")
    return bad
def turn(a, t):
    b = np.roll(a, t, axis=0); h = b.shape[-1] // 2
    b[..., h:] = np.roll(b[..., h:], S * t, axis=1)
    return b
def reference(wl, rc, nm, dn, pl):
    Y = wl.astype(np.float32).astype(np.int32).reshape(N, 8, 16, W); R = rc.astype(np.float32).astype(np.int32).reshape(N, 8, 16, K)
    L = np.stack([gentries(a) for a in nm]).astype(np.int64); D = dn.astype(np.int64); F = np.repeat(pl.astype(np.int64), 16, axis=2)
    E = np.zeros((N, 8, 16, C))
    for t in range(1, T + 1):
        R = turn(R, t); L = turn(L, t); pull = turn(F, t)
        ca = np.zeros((N, 8, W), np.int32); cb = np.zeros((N, 8, W), np.int32)
        np.put_along_axis(ca, L[..., :H], 1, 2); np.put_along_axis(cb, L[..., H:], 1, 2); cnt = ca + cb
        y = np.take_along_axis(Y, L[:, :, None, :], 3)
        b = np.add.reduce(np.minimum(R, y)[:, :, :15], axis=2).astype(np.int64); bond = b > 0
        n = np.repeat(np.add.reduce(bond.reshape(N, 8, C, 16).astype(np.int64), axis=3), 16, axis=2)
        ly = 16 * y[:, :, 15].astype(np.int64); lr = 16 * R[:, :, 15].astype(np.int64); la = np.minimum(ly, lr)
        fail = bond & (n * np.minimum(b, la) < pull); hold = bond & ~fail
        x = np.where(hold[:, :, None, :], EX[np.abs(R - y)], 0.0)
        E = E + turn(np.add.reduce(x.reshape(N, 8, 16, C, 16), axis=4), -t)
        swap = fail & (np.take_along_axis(cnt, L, 2) == 1) & (b > la)
        lig = (swap & (ly <= lr))[:, :, None, :]; rec = (swap & (ly > lr))[:, :, None, :]
        v = np.where(lig, 0, np.where(rec, R, y)); R = np.where(lig, y, np.where(rec, 0, R))
        np.put_along_axis(Y, L[:, :, None, :], v, 3)
        if t < T:
            d = np.take_along_axis(D, L, 2)
            L = np.where(~hold & (np.take_along_axis(cnt, d, 2) == 0), d, L)
        R = turn(R, -t); L = turn(L, -t)
    a = Y.reshape(N, 128, 4, W // 4); r = R.reshape(N, 128, 4, K // 4)
    return {"ye": E.reshape(N, 128, C).astype(np.float32),
            "yw": (a[:, :, 0] - a[:, :, 1] + 2 * a[:, :, 2] - 2 * a[:, :, 3]).astype(np.float32),
            "yr": (r[:, :, 0] - r[:, :, 1] + 2 * r[:, :, 2] - 2 * r[:, :, 3]).astype(np.float32)}

def check_inputs(d):
    bad = list(check_ranges(d))
    if not bad:
        for name, y in reference(**d).items():
            for q in range(N):
                v = np.abs(np.asarray(y[q], np.float64)); s = np.sqrt(np.mean(v * v))
                if v.max() > 10 * s or s < 2.0 ** -3: bad.append('%s of rank %d is uneven or too small' % (name, q))
    return bad

@@ -1,0 +1,634 @@
+from concourse.mybir import AluOpType, ActivationFunctionType
+
+ALU = AluOpType
+FN = ActivationFunctionType
+W, K, H, NT, GS = 2560, 2048, 1024, 4, 5
+ZZ = 3 * H
+SLOT = ZZ + 16
+W0 = NT * SLOT
+NP = W0 + W + NT * K
+SH = (16 * GS) % 128
+LW = K + 16
+CH = 512
+
+
+def SL(t):
+    return (NT - t) * SLOT
+
+
+def BX(t):
+    return W + (t - 1) * K
+
+
+F32, BF, I32, U16 = "float32", "bfloat16", "int32", "uint16"
+SCRATCH = {}
+for _n, _c, _d in [
+        ("pool", NP, BF), ("tab", W, BF), ("c0", K, BF), ("gg", K, BF), ("src", K, BF), ("hh", H, BF), ("oo", K, BF),
+        ("ab", 2 * K + 32, BF), ("xx", 2 * K, F32), ("rout", 2 * K, BF), ("wout", W, BF),
+        ("land", 6 * LW, BF), ("hop", 6 * H, BF), ("hq", 6 * H, BF), ("ui", 512, U16), ("dq", 384, F32),
+        ("nmi", 128, I32), ("nout", NT * 128, U16), ("nin", NT * 128, U16), ("pli", 128, I32), ("plf", 128, F32),
+        ("fout", 512, F32), ("fin", 384, F32), ("eout", 512, F32), ("ein", 384, F32),
+        ("t320", 320, I32), ("t640", 640, I32), ("zb", 640, BF), ("zc", 256, BF), ("pci", 8, I32), ("col", 32, F32),
+        ("xi", 160, F32), ("xw", 256, F32), ("xb", 128, F32), ("xf", 256, F32), ("wf", 256, F32), ("idf", 256, F32),
+        ("idb", 896, BF), ("sel", 5 * 144, BF), ("blk", 128, BF), ("bond", 128, BF), ("nh", 128, BF),
+        ("pu", 160, U16), ("du", 128, U16), ("ur", 384, U16), ("uv", 128, U16), ("ux", 128, U16),
+        ("ow", 640, F32), ("orr", 512, F32), ("jj", 128, F32), ("dl", 128, F32), ("lr", 128, F32),
+        ("la", 128, F32), ("ww", 128, F32), ("s1", 128, F32), ("n0", 256, F32), ("n1", 256, F32), ("ln", 256, F32),
+        ("d0", 384, F32), ("dr", 384, F32), ("dv", 384, F32), ("sr", 384, F32), ("sv", 384, F32)]:
+    SCRATCH[_n] = ("sbuf", [128, _c], _d)
+for _n in ("pd", "pa", "pb", "pc", "pv", "pe", "pn"):
+    SCRATCH[_n] = ("psum", [128, 1024 if _n == "pd" else 512], F32)
+NDMA = 24
+SEMAPHORES = (["ev", "ea", "ep", "eg", "sent"] + ["d%d" % i for i in range(NDMA)]
+              + [a + str(t) for a in ("an", "am", "au", "af", "ae") for t in range(1, NT + 1)] + ["ar1"]
+              + ["l%d%d%d" % (t, h, m) for t in range(2, NT + 1) for h in range(2) for m in range(2)]
+              + ["h%d" % m for m in range(6)] + ["o%d%d" % (h, m) for h in range(2) for m in range(6)])
+
+EST = dict(g=1.5, s=3.5, cyc=1.0e-3, fix=0.06, pcyc=0.5e-3, dfix=1.6, dbw=4e5, rbw=1e5, rfix=2.0, first=3.0, wake=0.1)
+SEED, ROUNDS, NOISE = [0], [1], [1.5, 10.0, 0.7, 0.5, 0.3]
+ORDER = {}
+PLAN = ["1M1T20261P1Q1W1Y24282A2C22363J1U332E312I3X2G3Z2K5H2O6T48636V3U6X2S654H3O4J2Q4L693Q386B2Y3L3B676D3D3F3H4N3S342U4P2M446N2W4A4F6P3M6G4C6R4652424Q40506I4Y5Q546K004U4S73744W5I777A827E7C7H787Z868O8M8157968B580290707J7K6Y5A949B7Q925C7S8I88048E8L8H8W0M8S8Z148Q8V9E989Z9C5S0G7U5E9K8C9H84A19S9I7M9M9OATA29Q9WBQA4AVA6A87O0EAA7W5KAFAWB0BS9UAYADB2BEBVBGAG0IB4AIB608AKCZB8D0AMBJBAD2D6BCDABND4AOD80KAQBPBL0CDH0ADFCMDJE6EM5UEE5WCQDLEOCSCPDMDUDODRCWE2EIDWDYCUF0EHDSELESE1F2FBE8EBEWEVEQEZF4DCGFF8E4FYF6FHG1FC0YFKFIFMGDG2FOFQFWHQGVG4GGG6G8GT6EGAH0ECFEGI0WFSBXGWGKFU5MGMGYBZH2GOH4GQC1HEH610H80QJ0IZCAHGHAC8HPJ6HCJ2J80SHJCEJA12HLC4HNC20UCCINC6KBCG5YJLJIIRJ4JUHSJQJMJFJGIPJOKEK6JSKOITKMKHL0JZL2K1IUKIJCCJK8LZM0CKL4KSK2KLJWN0KCM2KVMCKWLBMSKQKZL6IWMVM460L8K406LELHLCHXLKLIMWLM1GLSHVLOLQLUNQHZLWMYM6I1M8N2MANEMFI2NG1EN4NINLN6N8MGNANNICMINCMK18NSOWOVMMI6MONPOYP2MQ1KI4P0NVP4IG1CP9IAI8P71AIEON1IQ6Q4PTIJPRIKPBPCPWOPOQPEOTPGQ0PIPKPNQI0OPPQKPZQONZQAQ3QMQSQDQEREQ8QHQWRHQUQQRM5OPUR2RIRAQZNXRKR0R4R6TEO1R8RCROS2OAS4RQO2S9SERSS6O6RXO4SGTGSDSAOCRVO8S0OESLRYOGSJTKUAOITJTMOKSSTPU0U3TQTYSPTWSQTSU4SNTUSWUD16T8U7SYU8T6UET4T0T2SUTBTC"]
+
+
+def overlap(hist, reads, writes):
+    for regs, wr in ((reads, False), (writes, True)):
+        for name, lo, hi in regs:
+            for x in hist.get(name, []):
+                if x[0] < hi and lo < x[1] and (wr or x[3]):
+                    yield x[2]
+
+
+def note(hist, key, reads, writes, keep=False):
+    for name, lo, hi in writes:
+        hist[name] = [x for x in hist.get(name, []) if keep or not (lo <= x[0] and x[1] <= hi)] + [(lo, hi, key, True)]
+    for name, lo, hi in reads:
+        hist.setdefault(name, []).append((lo, hi, key, False))
+
+
+def banks(o):
+    return set((nm, b) for nm, lo, hi in o["r"] + o["w"] if SCRATCH[nm][0] == "psum" for b in range(lo // 512, (hi + 511) // 512))
+
+
+def arrange(ops, seed):
+    n = len(ops)
+    hist, pred, sent = {}, [], {}
+    for i, o in enumerate(ops):
+        grp = o.get("group")
+        pred.append(set(p for p in overlap(hist, o["r"], o["w"]) if grp is None or ops[p].get("group") != grp))
+        note(hist, i, o["r"], o["w"], grp is not None)
+        if o["kind"] == "send":
+            sent[o["sem"]] = i
+    succ = [[] for _ in ops]
+    for i, o in enumerate(ops):
+        if o["kind"] == "land":
+            pred[i].add(sent[o["sem"]])
+        if o["kind"] == "send" and o["sem"] != "an1":
+            pred[i].add(sent["an1"] - 1)
+        for p in pred[i]:
+            succ[p].append(i)
+    left = [len(p) for p in pred]
+    topo_ = [i for i in range(n) if not left[i]]
+    for i in topo_:
+        for s in succ[i]:
+            left[s] -= 1
+            if not left[s]:
+                topo_.append(s)
+    ways = []
+    for o in ops:
+        w = []
+        for e, (busy, lat) in o["cost"].items():
+            use = [(e, 0.0, busy)] if e != "-" else []
+            use += [(b, 0.0, busy + EST["wake"]) for b in banks(o)]
+            if o["kind"] == "dma":
+                use.append(("dma", busy + EST["dfix"], busy + lat))
+            if o["kind"] == "send":
+                way = EST["rfix"] + (0 if o["via"] is None else EST["rfix"] + 1.5 + 2.5 * o["via"])
+                use.append((("link", o["via"]), busy + way, busy + way + lat))
+                lat += way
+            w.append((e, busy + lat + (EST["wake"] if o["kind"] != "send" else 0.0), use))
+        ways.append(w)
+    back = [[(e, d, [(r, d - b, d - a) for r, a, b in use]) for e, d, use in w] for w in ways]
+
+    pen = []
+
+    def place(prio, before, after, ways_):
+        line, end, got = {}, [0.0] * n, [None] * n
+        left = [len(p) for p in before]
+        ready = [i for i in range(n) if not left[i]]
+        while ready:
+            i = min(ready, key=lambda k: prio[k])
+            ready.remove(i)
+            t0 = max([end[p] for p in before[i]] + [0.0])
+            best = None
+            for e, d, use in ways_[i]:
+                t, moved = t0, True
+                while moved:
+                    moved = False
+                    for r, a, b in use:
+                        ln = line.get(r, ())
+                        k = len(ln)
+                        while k and ln[k - 1][1] > t + a + 1e-9:
+                            k -= 1
+                        while k < len(ln) and ln[k][0] < t + b - 1e-9:
+                            t, moved = ln[k][1] - a, True
+                            k += 1
+                if best is None or t + d + (pen[i] if e == "v" else 0) < best[4]:
+                    best = (t + d, t, e, use, t + d + (pen[i] if e == "v" else 0))
+            end[i], got[i] = best[0], (best[1], best[2])
+            for r, a, b in best[3]:
+                line.setdefault(r, []).append((best[1] + a, best[1] + b))
+                line[r].sort()
+            for s in after[i]:
+                left[s] -= 1
+                if not left[s]:
+                    ready.append(s)
+        return end, got
+
+    x = seed * 7919 + 1
+    prio = [0.0] * n
+    for i in reversed(topo_):
+        prio[i] = min([prio[s] for s in succ[i]] + [0]) - min(w[1] for w in ways[i])
+    keep, cur, rnd = None, None, [x]
+    marks = [i for i in range(n) if ops[i]["kind"] == "send"]
+    ORDER["path"] = -min(prio)
+
+    def draw():
+        rnd[0] = (rnd[0] * 1103515245 + 12345) % 2147483648
+        return rnd[0] / 2147483648
+
+    pen[:] = [NOISE[2]] * n
+    if len(PLAN[0]) == 2 * n:
+        for k in range(n):
+            v = int(PLAN[0][2 * k:2 * k + 2], 36)
+            prio[v // 2], pen[v // 2] = k, 99 if v % 2 else -99
+    for it in range(ROUNDS[0]):
+        end, got = place(prio, pred, succ, ways)
+        if it % 2:
+            endb, gotb = place([-v for v in end], succ, pred, back)
+            end, got = place([-v for v in endb], pred, succ, ways)
+        val = max(end) + NOISE[3] * sum(end[i] for i in marks) / len(marks)
+        if keep is None or val <= keep[3]:
+            keep = (max(end), got, list(pen), val)
+        if cur is None or val <= cur[3] + NOISE[4] * (1 - it / ROUNDS[0]) * draw():
+            cur = (max(end), got, list(pen), val)
+        pen[:] = cur[2]
+        lo = draw() * cur[0] - 5
+        hi = lo + NOISE[1] * draw()
+        prio = [cur[1][i][0] for i in range(n)]
+        for i in range(n):
+            if lo <= prio[i] <= hi:
+                prio[i] += NOISE[0] * draw() if it % 3 else (6 * NOISE[0] * (draw() - 0.5) if draw() < 0.1 else 0)
+                if draw() < 0.15:
+                    pen[i] = 2 * NOISE[2] * draw()
+    rank_ = {i: k for k, i in enumerate(topo_)}
+    return [(i, keep[1][i][1]) for i in sorted(range(n), key=lambda k: (round(keep[1][k][0], 6), rank_[k]))], keep[0]
+
+
+def rank_program(g, core, T, topo):
+    n = len(T.cores)
+
+    def helper(r, h):
+        c = T.cores[r % n]
+        return [x for x in topo.cores_of(c) if x != c and (topo.die(x) != topo.die(c)) == bool(h)][0]
+
+    rank, role = T.rank_of(core), None
+    for r in range(n):
+        for h in range(2):
+            if helper(r, h) == core:
+                rank, role = r, h
+    if rank is None:
+        return
+    Q = {"v": g.vector, "a": g.scalar, "p": g.tensor, "g": g, "s": g.sync}
+    ops = []
+
+    def V(name, a=0, b=None, st=1, p=None):
+        if b is None:
+            b = SCRATCH[name][1][1]
+        ps = slice(0, 128) if p is None else slice(*p)
+        return (T[name][ps, a:b:st] if st > 1 else T[name][ps, a:b], [(name, a, b)], len(range(a, b, st)), SCRATCH[name][2], SCRATCH[name][0])
+
+    def IND(win, off):
+        return (win[0].indirect(off[0]), win[1] + off[1], 16 * off[2], win[3], "ind")
+
+    def X(*at):
+        return (at, [], 0, "", "dram")
+
+    def ap(x):
+        return T[x[0][0]][x[0][1]:x[0][2], x[0][3]:x[0][4]] if x[4] == "dram" else x[0]
+
+    def aps(*xs):
+        return [x for x in xs if isinstance(x, tuple)]
+
+    def val(x):
+        return x[0] if isinstance(x, tuple) else x
+
+    def cyc(out, ins, k):
+        if out[4] == "ind":
+            k = EST["s"]
+        elif ins and ins[0][4] == "ind":
+            k = EST["g"]
+        return (EST["fix"] + max(64, k * out[2]) * EST["cyc"], 0.0)
+
+    def half(*xs):
+        return 0.5 if all(x[3] in (BF, U16) for x in xs) else 1
+
+    def op(calls, out, ins):
+        reads = [r for x in ins for r in x[1]]
+        writes = out[1]
+        if out[4] == "ind":
+            reads, writes = reads + out[1][1:], out[1][:1]
+        ops.append(dict(kind="op", r=reads, w=writes, calls=calls, cost={e: cyc(out, ins, k) for e, (c, k) in calls.items()}))
+
+    def cp(out, a, both=False):
+        calls = {"v": (lambda: g.vector.tensor_copy(out[0], a[0]), half(out, a))}
+        if both:
+            calls["a"] = (lambda: g.scalar.activation(out[0], a[0], FN.Identity), 1)
+        op(calls, out, [a])
+
+    def tt(out, a, b, o):
+        op({"v": (lambda: g.vector.tensor_tensor(out[0], a[0], b[0], o), 2 if a[4] == b[4] else 1)}, out, [a, b])
+
+    def ts(out, a, s1, o0, s2=None, o1=None, alt=None):
+        if o1 is None:
+            calls = {"v": (lambda: g.vector.tensor_scalar(out[0], a[0], val(s1), None, o0), half(out, a))}
+        else:
+            calls = {"v": (lambda: g.vector.tensor_scalar(out[0], a[0], val(s1), val(s2), o0, o1), half(out, a))}
+        if alt:
+            calls["a"] = (lambda: g.scalar.activation(out[0], a[0], alt[0], bias=val(alt[2]), scale=val(alt[1])), 1)
+        op(calls, out, aps(a, s1, s2))
+
+    def lin(out, a, scale, bias):
+        ts(out, a, scale, ALU.mult, bias, ALU.add, alt=(FN.Identity, scale, bias))
+
+    def scan(out, a, b):
+        op({"v": (lambda: g.vector.tensor_tensor_scan(out[0], a[0], b[0], 0.0, ALU.mult, ALU.add), 1)}, out, [a, b])
+
+    def fill(out, c):
+        op({"v": (lambda: g.vector.memset(out[0], c), half(out))}, out, [])
+
+    def act(out, a, f, scale=1.0):
+        op({"a": (lambda: g.scalar.activation(out[0], a[0], f, scale=scale), 1)}, out, [a])
+
+    def gather(buf, a, win, obuf, oa, cnt):
+        for c in range(0, cnt, CH):
+            m = min(CH, cnt - c)
+            cp(V(buf, a + c, a + c + m), IND(win, V(obuf, oa + c // 16, oa + (c + m) // 16)), True)
+
+    def iota(out, pat, cm, fl=True):
+        if fl:
+            op({"g": (lambda: g.iota(out[0], pat, 0, cm, allow_small_or_imprecise_dtypes=True), 2)}, out, [])
+        else:
+            op({"g": (lambda: g.iota(out[0], pat, 0, cm), 2)}, out, [])
+
+    runs, seen = {}, {}
+
+    def mm(items, group=None, whole=None):
+        runs[group] = runs.get(group, 0) + 1
+
+        def call():
+            seen[group] = seen.get(group, 0) + 1
+            start, stop = group is None or seen[group] == 1, group is None or seen[group] == runs[group]
+            for i, (o, l, r) in enumerate(items):
+                ins = g.tensor.matmul(o[0], l[0], r[0], start and i == 0, stop and i == len(items) - 1)
+            return ins
+        c = sum(max(64, r[2]) * (4 if r[3] == F32 else 1) for o, l, r in items) * EST["pcyc"]
+        ops.append(dict(kind="op", r=[r for it in items for x in it[1:] for r in x[1]], calls={"p": (call, 0)}, cost={"p": (c, 0.0)},
+                        w=whole[1] if whole else sorted(set(r for it in items for r in it[0][1])), group=group))
+
+    def wrap(out, s, buf, a, cnt):
+        return [(out, V("sel", 144 * s + 15 - k, 144 * s + 143 - k), V(buf, a + k, a + cnt, 16)) for k in range(16)]
+
+    def dma(e, pairs, kb):
+        ops.append(dict(kind="dma", r=[r for o, i in pairs for r in i[1]], w=[r for o, i in pairs for r in o[1]], pairs=pairs,
+                        cost={e: (0.1 * len(pairs), EST["dfix"] + kb * 1024 / EST["dbw"])}))
+
+    def send(d, out, a, sem, via=None, slot=0):
+        by = 128 * a[2] * (4 if a[3] == F32 else 2)
+        ops.append(dict(kind="send", r=a[1], w=[], d=d, out=out, a=a, sem=sem, via=via, slot=slot,
+                        cost={"g": (0.3 + (EST["first"] if sem == "an1" else 0), 0.3 + by / EST["rbw"])}))
+
+    def lands(d, out, sem, via=None):
+        ops.append(dict(kind="land", r=[], w=out[1], d=d, sem=sem, via=via, cost={"-": (0.0, 0.0)}))
+
+    def LD(t, h, m):
+        a = (2 * (t - 2) + h) * LW + H * m
+        return V("land", a, a + H)
+
+    def col(i):
+        return V("col", i, i + 1)
+
+    PT, DS, HP, HN, A15 = 0, 1, 2, 3, 4
+    IDB, NID, P2, N2, BIG = 0, 128, 256, 512, 768
+
+    def mat(m):
+        return V("idb", m, m + 128)
+
+    def turn(o):
+        return V("idf", o, o + 128)
+
+    for t in range(1, NT + 1):
+        n0 = 128 * (t - 1)
+        if t == 1:
+            lands(1, V("nin", 0, 128), "an1")
+            lands(1, V("pool", SL(1), SL(1) + K), "ar1")
+        else:
+            lands(1, V("nin", n0, n0 + 64), "an%d" % t)
+            lands(1, V("nin", n0 + 64, n0 + 128), "am%d" % t)
+            lands(1, V("ui", n0, n0 + 128), "au%d" % t)
+            for h in range(2):
+                for m in range(2):
+                    lands(1, LD(t, h, m), "l%d%d%d" % (t, h, m), h)
+        if t < NT:
+            lands(t, V("fin", n0, n0 + 128), "af%d" % t)
+            lands(-t, V("ein", n0, n0 + 128), "ae%d" % t)
+
+    dma("s", [(V("nmi", 0, 64), X("nm", 0, 128, 0, 64)), (V("nmi", 64, 128, p=(SH, 128)), X("nm", 0, 128 - SH, 64, 128)),
+              (V("nmi", 64, 128, p=(0, SH)), X("nm", 128 - SH, 128, 64, 128))], 64)
+    dma("a", [(V("t320", 0, 160), X("dn", 0, 8, 0, W))], 80)
+    dma("s", [(V("rout", 0, H), X("rc", 0, 128, 0, H)), (V("rout", H, K, p=(SH, 128)), X("rc", 0, 128 - SH, H, K)),
+              (V("rout", H, K, p=(0, SH)), X("rc", 128 - SH, 128, H, K))], 512)
+    dma("a", [(V("pli", p=(0, 8)), X("pl", 0, 8, 0, 128))], 4)
+    dma("s", [(V("pool", W0, W0 + W), X("wl", 0, 128, 0, W))], 640)
+
+    iota(V("pci", 0, 1), [[0, 1]], 1, False)
+    iota(V("xi"), [[1, 160]], -1)
+    iota(V("xw"), [[0, 2], [1, 128]], -1)
+    iota(V("xb"), [[16, 8], [0, 16]], -1)
+    iota(V("xf", p=(0, 8)), [[0, 2], [1, 8], [0, 16]], -1)
+    fill(V("tab"), 0.0)
+    ts(V("pci", 4, 5), V("pci", 0, 1), 15, ALU.bitwise_and)
+    cp(col(0), V("pci", 0, 1))
+    cp(col(1), V("pci", 4, 5))
+    ts(col(2), col(1), 160.0, ALU.mult, col(0), ALU.add)
+    ts(V("t320", 160, 320), V("xi"), col(2), ALU.add)
+    cp(V("nout", 0, 128), V("nmi"))
+    send(1, V("nin", 0, 128), V("nout", 0, 128), "an1")
+    send(1, V("pool", SL(1), SL(1) + K), V("rout", 0, K), "ar1")
+    ts(V("t640", 0, 320), V("t320"), 7, ALU.arith_shift_right)
+    ts(V("t640", 320, 640), V("t320"), 127, ALU.bitwise_and)
+    cp(V("zb", 0, 320), V("t640", 0, 320))
+    cp(V("zb", 320, 640), V("t640", 320, 640))
+    dma("s", [(V("tab", p=(r, 128, 16)), V("zb", c, c + 160)) for r, c in ((0, 0), (8, 160), (4, 320), (12, 480))], 100)
+    fill(V("c0"), 0.0)
+    lin(V("zc", 0, 128), V("xi", 0, 128), 0.0, col(1))
+    lin(V("zc", 128, 256), V("xi", 0, 128), 1.0, col(0))
+    dma("s", [(V("c0", p=(r, 128, 16)), V("zc", c, c + 128)) for r, c in ((8, 0), (12, 128))], 64)
+    ts(col(3), col(1), 8.0, ALU.is_lt)
+    ts(col(4), col(1), 8.0, ALU.is_equal)
+    for t in range(1, NT + 1):
+        lin(col(19 + t), col(4), float(BX(t) // 128), 0.0)
+    lin(col(5), col(1), -1.0, 15.0)
+    lin(col(6), col(4), 128.0, 0.0)
+    ts(col(7), col(1), 12.0, ALU.is_equal, col(6), ALU.add)
+    ts(col(8), col(1), 0.0, ALU.is_equal, 128.0, ALU.mult)
+    ts(col(9), col(1), 4.0, ALU.is_equal, col(8), ALU.add)
+    ts(col(10), col(1), 15.0, ALU.is_lt, 0.5, ALU.mult)
+    ts(col(11), col(1), 15.0, ALU.is_equal, 16.0, ALU.mult)
+    lin(col(12), col(1), -1.0, 0.0)
+    lin(col(13), col(0), 16.0, col(1))
+    for s, c in ((PT, 7), (DS, 9), (HP, 10), (A15, 11)):
+        ts(V("sel", 144 * s, 144 * s + 144), V("xi", 0, 144), col(5), ALU.is_equal, col(c), ALU.mult)
+    ts(V("idf"), V("xw"), 0.0, ALU.is_equal)
+    ts(V("wf", p=(0, 8)), V("xf", p=(0, 8)), 0.0, ALU.is_equal)
+    cp(V("plf", p=(0, 8)), V("pli", p=(0, 8)))
+    lin(V("sel", 144 * HN, 144 * HN + 144), V("sel", 144 * HP, 144 * HP + 144), -1.0, 0.0)
+    for m, w, c in ((IDB, 128, 1.0), (NID, 128, -1.0), (BIG, 128, 4096.0), (P2, 256, 2.0), (N2, 256, -2.0)):
+        lin(V("idb", m, m + w), V("idf", 0, w), c, 0.0)
+    for t in range(1, NT + 1):
+        o = (-SH * t) % 128
+        mm([(V("pn", 128 * (t - 1), 128 * (t - 1) + 64), V("wf", 0, 128, p=(0, 8)), V("plf", 0, 64, p=(0, 8)))])
+        mm([(V("pn", 128 * (t - 1) + 64, 128 * t), V("wf", o, o + 128, p=(0, 8)), V("plf", 64, 128, p=(0, 8)))])
+    cp(V("fout"), V("pn"), True)
+    for t in range(1, NT):
+        send(t, V("fin", 128 * (t - 1), 128 * t), V("fout", 128 * (t - 1), 128 * t), "af%d" % t)
+    ts(V("blk"), V("xb"), col(12), ALU.is_equal)
+    lin(V("jj"), V("xi", 0, 128), 16.0, col(13))
+    for t in range(1, NT + 1):
+        fill(V("pool", SL(t) + ZZ, SL(t) + SLOT), 0.0)
+    for u in range(6):
+        fill(V("land", LW * u + K, LW * u + LW), 0.0)
+    for h in range(2):
+        for u, (a, b) in enumerate(((1.0, -H), (-1.0, K), (1.0, 0))):
+            lin(V("dq", 192 * h + u, 192 * h + 192, 3), V("jj", 64 * h, 64 * h + 64), a, float(b - a * H * h))
+    fill(V("ab", K, K + 16), 16384.0)
+    fill(V("ab", 2 * K + 16, 2 * K + 32), 16384.0)
+    fill(V("n0"), 0.0)
+    fill(V("d0"), 0.0)
+    lin(V("dr", 1, 384, 3), V("jj"), -1.0, float(ZZ))
+    lin(V("dr", 2, 384, 3), V("jj"), 1.0, 0.0)
+    lin(V("dr", 192, 384, 3), V("jj", 64, 128), 1.0, float(H - ZZ))
+    lin(V("dv", 0, 384, 3), V("jj"), -1.0, float(ZZ))
+    lin(V("dv", 193, 384, 3), V("jj", 64, 128), 0.0, -float(H))
+    lin(V("dv", 194, 384, 3), V("jj", 64, 128), 1.0, float(H))
+
+    tab = V("tab")
+
+    def ypos(t, h):
+        return W0 + BX(t) if h == 0 else SL(t) + K
+
+    for t in range(1, NT + 1):
+        last = t == NT
+        n0 = 128 * (t - 1)
+        pull = V("fout", 384, 512) if last else V("fin", n0, n0 + 128)
+        old = V("pool", SL(t), W0 + BX(t))
+        if t > 1:
+            for h in range(2):
+                a = (2 * (t - 2) + h) * LW
+                gather("pool", SL(t) + H * h, V("land", a, a + LW), "ui", n0 + 64 * h, H)
+        if not last:
+            for h in range(2):
+                send(1, LD(t + 1, h, 0), V("pool", SL(t) + H * h, SL(t) + H * h + H), "l%d%d0" % (t + 1, h), h, 2 * t - 2)
+        for h in range(2):
+            c, a = 64 * h, H * h
+            gather("gg", a, tab, "nin", n0 + c, H)
+            if t > 1 or h:
+                mm(wrap(V("pa", c, c + 64), PT, "gg", a, H))
+                cp(V("pu", c, c + 64), V("pa", c, c + 64))
+            lin(V("src", a, a + H), V("gg", a, a + H), col(3), col(19 + t))
+            tt(IND(tab, V("nin", n0 + c, n0 + c + 64)), V("src", a, a + H), V("c0", a, a + H), ALU.add)
+            if not last:
+                mm(wrap(V("pb", c, c + 64), DS, "gg", a, H))
+                cp(V("du", c, c + 64), V("pb", c, c + 64))
+            if t == 1:
+                gather("pool", ypos(t, h), V("pool", W0, W0 + W), "nin", c, H)
+            else:
+                gather("pool", ypos(t, h), V("pool", W0, W0 + BX(t) + a), "pu", c, H)
+        lf = V("n1", 1, 256, 2)
+        if not last:
+            cp(lf, V("nin", n0, n0 + 128))
+            tt(V("dl"), V("pb", 0, 128), lf, ALU.subtract)
+        u1 = V("pa", 0, 64) if t > 1 else V("n1", 1, 128, 2)
+        if last:
+            lin(V("dr", 0, 192, 3), u1, 1.0, float(W0 - SL(t) - ZZ))
+        else:
+            for h in range(2):
+                send(1, LD(t + 1, h, 1), V("pool", ypos(t, h), ypos(t, h) + H), "l%d%d1" % (t + 1, h), h, 2 * t - 1)
+        lin(V("dv", 2, 192, 3), u1, 1.0, float(W0 - SL(t)))
+        tt(V("dv", 1, 192, 3), V("jj", 0, 64), V("dv", 2, 192, 3), ALU.subtract)
+        bb = V("pc", 0, 128)
+        a0, x0 = (K + 16) * (t % 2), K * (t % 2)
+        for h in range(2):
+            for q in range(2):
+                a = H * h + 512 * q
+                pd = V("pd", 512 * q, 512 * q + 512)
+                mm([(pd, mat(IDB), V("pool", SL(t) + a, SL(t) + a + 512)), (pd, mat(NID), V("pool", ypos(t, h) + 512 * q, ypos(t, h) + 512 * q + 512))])
+                act(V("ab", a0 + a, a0 + a + 512), pd, FN.Abs)
+            out = V("pc", 64 * h, 64 * h + 64)
+            if h:
+                mm(wrap(V("pb", 384, 512), A15, "pool", SL(t), K))
+                mm(wrap(V("pc", 0, 64), HP, "pool", SL(t), H) + wrap(out, HP, "pool", SL(t) + H, H), "b%d" % t, bb)
+            mm(wrap(out, HP, "pool", ypos(t, h), H), "b%d" % t, bb)
+            mm(wrap(V("pb", 256 + 64 * h, 320 + 64 * h), A15, "pool", ypos(t, h), H))
+            mm(wrap(out, HN, "ab", a0 + H * h, H), "b%d" % t, bb)
+        cp(V("lr"), V("pb", 384, 512), True)
+        ly = V("pb", 256, 384)
+        tt(V("la"), ly, V("lr"), ALU.min)
+        tt(V("d0", 1, 384, 3), ly, V("lr"), ALU.is_le)
+        ts(V("bond"), bb, 0.0, ALU.is_gt, alt=(FN.Sign, 1.0, 0.0))
+        mm([(V("pb", 128, 256), V("blk"), V("bond"))])
+        tt(V("ww"), bb, V("la"), ALU.min)
+        tt(V("pv", 0, 128), V("pb", 128, 256), V("ww"), ALU.mult)
+        tt(V("pv", 128, 256), V("pv", 0, 128), pull, ALU.is_lt)
+        tt(V("nh"), V("pv", 128, 256), V("bond"), ALU.is_ge)
+        tt(V("pv", 256, 384), bb, V("la"), ALU.is_gt)
+        tt(V("s1"), V("pv", 256, 384), V("nh"), ALU.mult)
+        if not last:
+            tt(V("n1", 0, 256, 2), V("nh"), V("dl"), ALU.mult)
+            for h in range(2):
+                c = 64 * h
+                gather("oo", H * h, tab, "du", c, H)
+                mm(wrap(V("pa", 192 + c, 256 + c), PT, "oo", H * h, H))
+                ts(V("n0", 2 * c + 1, 2 * c + 128, 2), V("pa", 192 + c, 256 + c), float(BX(t)), ALU.is_lt)
+                scan(V("ln", 2 * c, 2 * c + 128), V("n0", 2 * c, 2 * c + 128), V("n1", 2 * c, 2 * c + 128))
+                new = V("ln", 2 * c + 1, 2 * c + 128, 2)
+                if h:
+                    mm([(V("pn", 0, 64), turn(128 - SH), new)])
+                    new = V("pn", 0, 64)
+                out = V("nout", 128 * t + c, 128 * t + c + 64)
+                cp(out, new)
+                send(1, V("nin", 128 * t + c, 128 * t + c + 64), out, ("an%d", "am%d")[h] % (t + 1))
+        gather("hh", 0, tab, "nin", n0, H)
+        mm(wrap(V("pa", 128, 192), PT, "hh", 0, H))
+        ts(V("pv", 384, 448), V("pa", 128, 192), float(BX(t) + H), ALU.is_lt)
+        ts(V("pv", 448, 512), V("pu", 64, 128), float(BX(t)), ALU.is_lt)
+        tt(V("d0", 2, 384, 3), V("pv", 384, 512), V("s1"), ALU.mult)
+        scan(V("sr"), V("d0"), V("dr" if last else "dq"))
+        if last:
+            cp(V("ur", 0, 128), V("sr", 2, 384, 3))
+            gather("rout", K, old, "ur", 0, K)
+        else:
+            mm([(V("pn", 256, 320), turn(0), V("sr", 2, 192, 3))])
+            mm([(V("pn", 320, 384), turn(128 - SH), V("sr", 194, 384, 3))])
+            cp(V("ur", n0, n0 + 128), V("pn", 256, 384))
+            send(1, V("ui", n0 + 128, n0 + 256), V("ur", n0, n0 + 128), "au%d" % (t + 1))
+        scan(V("sv"), V("d0"), V("dv"))
+        cp(V("uv"), V("sv", 2, 384, 3))
+        gather("pool", W0 + BX(t), old, "uv", 0, K)
+        mm([(V("pn", 128, 256), turn(0), V("jj")), (V("pn", 128, 256), mat(BIG), V("nh"))])
+        ts(V("ux"), V("pn", 128, 256), float(K), ALU.min)
+        for q in range(4):
+            act(V("xx", x0 + 512 * q, x0 + 512 * q + 512), IND(V("ab", a0, a0 + K + 16), V("ux", 32 * q, 32 * q + 32)), FN.Exp, scale=-1.0 / 64)
+        if not last:
+            for k in range(0, 16, 2):
+                mm([(V("pe", 0, 128), turn(0), V("xx", x0 + k + u, x0 + K, 16)) for u in range(2)], "e%d" % t)
+        else:
+            for h in range(2):
+                out = V("pe", 64 * h, 64 * h + 64)
+                for k in range(0, 16, 4):
+                    mm([(out, turn((SH * t * h) % 128), V("xx", x0 + H * h + k + u, x0 + H * h + H, 16)) for u in range(4)], "e%d" % t)
+                mm([(out, turn((SH * u * h) % 128), V("ein", 128 * u + 64 * h - 128, 128 * u + 64 * h - 64)) for u in range(1, NT)], "e%d" % t)
+        cp(V("eout", n0, n0 + 128), V("pe", 0, 128), True)
+        if not last:
+            send(-t, V("ein", n0, n0 + 128), V("eout", n0, n0 + 128), "ae%d" % t)
+
+    t = NT
+    dma("s", [(X("ye", 0, 128, 0, 128), V("eout", 384, 512))], 64)
+    mm(wrap(V("pb", 0, 160), PT, "tab", 0, W))
+    cp(V("pu"), V("pb", 0, 160))
+    for q in range(2):
+        for u in range(4):
+            gather("wout", 640 * u + 320 * q, V("pool", W0, NP), "pu", 40 * u + 20 * q, 320)
+        out = V("pd", 512 * q, 512 * q + 320)
+        mm([(out, mat(m), V("wout", 640 * u + 320 * q, 640 * u + 320 * q + 320)) for u, m in enumerate((IDB, NID, P2, N2))])
+        cp(V("ow", 320 * q, 320 * q + 320), out, True)
+        dma("s", [(X("yw", 0, 128, 320 * q, 320 * q + 320), V("ow", 320 * q, 320 * q + 320))], 160)
+    o = (SH * NT) % 128
+    mm([(V("pc"), mat(m), V("rout", K + 512 * u, K + 512 * u + 512)) for u, m in enumerate((IDB, NID, P2 + o, N2 + o))])
+    cp(V("orr"), V("pc"), True)
+    dma("s", [(X("yr", 0, 128, 0, 512), V("orr"))], 256)
+
+    if SEED[0] not in ORDER:
+        ORDER[SEED[0]] = arrange(ops, SEED[0])
+    clock = {e: {} for e in Q}
+    total, hist, bank, ndma = {}, {}, {}, 0
+
+    def wait(e, tok):
+        if clock[e].get(tok[0], 0) < tok[1]:
+            Q[e].wait_ge(T.sem[tok[0]], tok[1])
+            for s, c in list(tok[2].items()) + [(tok[0], tok[1])]:
+                if clock[e].get(s, 0) < c:
+                    clock[e][s] = c
+
+    def token(e, sem, c):
+        total[sem] = total.get(sem, 0) + c
+        return (sem, total[sem], dict(clock.get(e, {})))
+
+    def write(dst, out, a, sem, local, eng):
+        rid, pid = topo.addr(dst, core)
+        g.remote_dma(out, a, T.sem[sem], T.sem[local], pid, rid, sum(1 << k for k in eng))
+        return token("g", local, len(eng))
+
+    nxt = T.cores[(rank + 1) % n]
+    spare = [k for k in topo.engines(T.cores[rank], helper(rank, 0)) if k not in topo.engines(T.cores[rank], nxt)]
+    for i, e in ORDER[SEED[0]][0]:
+        o = ops[i]
+        if role is not None:
+            if o["kind"] == "send" and o["via"] == role:
+                a, q = H * o["slot"], "g"
+                tok = token("-", "h%d" % o["slot"], len(spare))
+                if role:
+                    wait("s", tok)
+                    g.sync.dma_start(T.hq[SH:128, a:a + H], T.hop[0:128 - SH, a:a + H]).then_inc(T.sem["d%d" % ndma], 16)
+                    g.sync.dma_start(T.hq[0:SH, a:a + H], T.hop[128 - SH:128, a:a + H]).then_inc(T.sem["d%d" % ndma], 16)
+                    tok = token("s", "d%d" % ndma, 32)
+                    ndma += 1
+                wait("g", tok)
+                write(nxt, o["out"][0], T["hq" if role else "hop"][:, a:a + H], o["sem"], "sent", topo.engines(core, nxt))
+            continue
+        if o["kind"] == "land":
+            src = T.cores[(rank - o["d"]) % n] if o["via"] is None else helper(rank - 1, o["via"])
+            tok = token(e, o["sem"], len(topo.engines(src, core)))
+            note(hist, tok, [], o["w"])
+            continue
+        wr = o["w"]
+        if e == "p":
+            wr = []
+            toks = [k for k in overlap(hist, [], o["w"]) if k[0] != "ep"]
+        else:
+            toks = []
+        toks += list(overlap(hist, o["r"], wr)) + [bank[b][0] for b in banks(o) if b in bank and bank[b][1] != e]
+        for tok in sorted(toks, key=lambda k: (-len(k[2]), -k[1])):
+            wait(e, tok)
+        if o["kind"] == "send":
+            if o["via"] is None:
+                dst = T.cores[(rank + o["d"]) % n]
+                write(dst, o["out"][0], o["a"][0], o["sem"], "sent", topo.engines(core, dst))
+            else:
+                a = H * o["slot"]
+                tok = write(helper(rank, o["via"]), T.hop[:, a:a + H], o["a"][0], "h%d" % o["slot"], "o%d%d" % (o["via"], o["slot"]), spare)
+                note(hist, tok, o["r"], [])
+            continue
+        if o["kind"] == "dma":
+            sem = "d%d" % ndma
+            ndma += 1
+            for a, b in o["pairs"]:
+                Q[e].dma_start(ap(a), ap(b)).then_inc(T.sem[sem], 16)
+            tok = token(e, sem, 16 * len(o["pairs"]))
+        else:
+            o["calls"][e][0]().then_inc(T.sem["e" + e], 1)
+            tok = token(e, "e" + e, 1)
+        note(hist, tok, o["r"], o["w"], o.get("group") is not None)
+        for b in banks(o):
+            bank[b] = (tok, e)
+    for sem in sorted(total):
+        wait("g", (sem, total[sem], {}))

@@ -3,17 +3,23 @@ from concourse.mybir import AluOpType, ActivationFunctionType
 ALU = AluOpType
 FN = ActivationFunctionType
 W, K, H, NT, GS = 2560, 2048, 1024, 4, 5
-ZZ = 3 * H
-SLOT = ZZ + 16
-W0 = NT * SLOT
+LW = 2 * H + 16
+W0 = 2 * LW
 NP = W0 + W + NT * K
 SH = (16 * GS) % 128
-LW = K + 16
-CH = 512
+OPT = dict(ch=512, big=1024, sc=1024, on=(2 * H, H), hold=(1,), sg=2, ur=2, rch=1024, ls=(1, 0))
 
 
-def SL(t):
-    return (NT - t) * SLOT
+def ZP(h):
+    return LW * (1 - h)
+
+
+def RP(h):
+    return ZP(h) + 16
+
+
+def YP(h):
+    return ZP(h) + 16 + H
 
 
 def BX(t):
@@ -23,31 +29,50 @@ def BX(t):
 F32, BF, I32, U16 = "float32", "bfloat16", "int32", "uint16"
 SCRATCH = {}
 for _n, _c, _d in [
-        ("pool", NP, BF), ("tab", W, BF), ("c0", K, BF), ("gg", K, BF), ("src", K, BF), ("hh", H, BF), ("oo", K, BF),
-        ("ab", 2 * K + 32, BF), ("xx", 2 * K, F32), ("rout", 2 * K, BF), ("wout", W, BF),
-        ("land", 6 * LW, BF), ("hop", 6 * H, BF), ("hq", 6 * H, BF), ("ui", 512, U16), ("dq", 384, F32),
-        ("nmi", 128, I32), ("nout", NT * 128, U16), ("nin", NT * 128, U16), ("pli", 128, I32), ("plf", 128, F32),
-        ("fout", 512, F32), ("fin", 384, F32), ("eout", 512, F32), ("ein", 384, F32),
-        ("t320", 320, I32), ("t640", 640, I32), ("zb", 640, BF), ("zc", 256, BF), ("pci", 8, I32), ("col", 32, F32),
-        ("xi", 160, F32), ("xw", 256, F32), ("xb", 128, F32), ("xf", 256, F32), ("wf", 256, F32), ("idf", 256, F32),
-        ("idb", 896, BF), ("sel", 5 * 144, BF), ("blk", 128, BF), ("bond", 128, BF), ("nh", 128, BF),
-        ("pu", 160, U16), ("du", 128, U16), ("ur", 384, U16), ("uv", 128, U16), ("ux", 128, U16),
-        ("ow", 640, F32), ("orr", 512, F32), ("jj", 128, F32), ("dl", 128, F32), ("lr", 128, F32),
-        ("la", 128, F32), ("ww", 128, F32), ("s1", 128, F32), ("n0", 256, F32), ("n1", 256, F32), ("ln", 256, F32),
-        ("d0", 384, F32), ("dr", 384, F32), ("dv", 384, F32), ("sr", 384, F32), ("sv", 384, F32)]:
+        ("pool", NP, BF), ("tab", W + H, BF), ("dnt", W, BF), ("c0", K, BF), ("gg", K, BF), ("src", H, BF), ("hh", H, BF), ("oo", K, BF),
+        ("lq", 64, F32), ("lb", 64, U16),
+        ("ab", 2 * K + 64, BF), ("xx", 2 * K, F32), ("xs", K, F32), ("mk", 512, BF), ("rout", 2 * K, BF), ("rb2", H, BF), ("wout", W, BF),
+        ("land", 6 * LW, BF), ("hop", 6 * H, BF), ("hq", 6 * H, BF),
+        ("nmi", 128, I32), ("nl", NT * 128, U16), ("uo", NT * 384 + 160, U16), ("ui", NT * 384 + 160, U16),
+        ("eo", NT * 512, F32), ("en", NT * 512, F32), ("ur", 128, U16),
+        ("pli", 128, I32), ("plf", 128, F32), ("fout", 512, F32), ("fin", 384, F32), ("eout", 512, F32), ("ein", 384, F32),
+        ("dni", 160, I32), ("zb", 320, BF), ("zi", 320, BF), ("mt", 256, BF), ("it", 160, BF), ("i4", 768, BF),
+        ("ph", 384, BF), ("one", 128, BF), ("pci", 8, I32), ("col", 32, F32), ("eq", 32, F32),
+        ("xi", 144, F32), ("xw", 256, F32), ("xb", 128, F32), ("xf", 256, F32), ("wf", 256, F32), ("idf", 256, F32),
+        ("idb", 1024, BF), ("sel", 14 * 144, BF), ("blk", 128, BF), ("bond", 128, BF), ("cc", 64, BF), ("c16", 64, BF), ("c64", 64, BF),
+        ("du", 128, U16), ("uv", 128, U16), ("ux", 128, U16), ("sw", 128, BF), ("sd", 128, BF),
+        ("ow", 640, F32), ("orr", 512, F32), ("dl", 128, F32), ("lr", 128, F32),
+        ("la", 128, F32), ("ww", 128, F32), ("n0", 256, BF), ("ln", 128, F32)]:
     SCRATCH[_n] = ("sbuf", [128, _c], _d)
-for _n in ("pd", "pa", "pb", "pc", "pv", "pe", "pn"):
-    SCRATCH[_n] = ("psum", [128, 1024 if _n == "pd" else 512], F32)
-NDMA = 24
-SEMAPHORES = (["ev", "ea", "ep", "eg", "sent"] + ["d%d" % i for i in range(NDMA)]
-              + [a + str(t) for a in ("an", "am", "au", "af", "ae") for t in range(1, NT + 1)] + ["ar1"]
+for _n in ("pd", "pc", "pa", "pb", "pe", "pn"):
+    SCRATCH[_n] = ("psum", [128, 1024 if _n in ("pd", "pc") else 512], F32)
+NDMA = 36
+SEMAPHORES = (["ev", "ea", "ep", "eg", "sent", "an", "ad", "ar0", "ar1", "aw"] + ["d%d" % i for i in range(NDMA)]
+              + [a + str(t) for a in ("pa", "pb", "na", "nb", "sg", "au", "av", "af", "ae") for t in range(1, NT + 1)]
               + ["l%d%d%d" % (t, h, m) for t in range(2, NT + 1) for h in range(2) for m in range(2)]
               + ["h%d" % m for m in range(6)] + ["o%d%d" % (h, m) for h in range(2) for m in range(6)])
 
-EST = dict(g=1.5, s=3.5, cyc=1.0e-3, fix=0.06, pcyc=0.5e-3, dfix=1.6, dbw=4e5, rbw=1e5, rfix=2.0, first=3.0, wake=0.1)
-SEED, ROUNDS, NOISE = [0], [1], [1.5, 10.0, 0.7, 0.5, 0.3]
+EST = dict(g=1.45, s=3.1, cyc=0.87e-3, fix=0.055, pcyc=0.59e-3, dfix=1.5, dbw=4.5e5, rbw=1.3e5, rfix=1.5, riss=0.7, first=3.0, wake=0.09)
+PERIOD = 17.0
 ORDER = {}
-PLAN = ["1M1T20261P1Q1W1Y24282A2C22363J1U332E312I3X2G3Z2K5H2O6T48636V3U6X2S654H3O4J2Q4L693Q386B2Y3L3B676D3D3F3H4N3S342U4P2M446N2W4A4F6P3M6G4C6R4652424Q40506I4Y5Q546K004U4S73744W5I777A827E7C7H787Z868O8M8157968B580290707J7K6Y5A949B7Q925C7S8I88048E8L8H8W0M8S8Z148Q8V9E989Z9C5S0G7U5E9K8C9H84A19S9I7M9M9OATA29Q9WBQA4AVA6A87O0EAA7W5KAFAWB0BS9UAYADB2BEBVBGAG0IB4AIB608AKCZB8D0AMBJBAD2D6BCDABND4AOD80KAQBPBL0CDH0ADFCMDJE6EM5UEE5WCQDLEOCSCPDMDUDODRCWE2EIDWDYCUF0EHDSELESE1F2FBE8EBEWEVEQEZF4DCGFF8E4FYF6FHG1FC0YFKFIFMGDG2FOFQFWHQGVG4GGG6G8GT6EGAH0ECFEGI0WFSBXGWGKFU5MGMGYBZH2GOH4GQC1HEH610H80QJ0IZCAHGHAC8HPJ6HCJ2J80SHJCEJA12HLC4HNC20UCCINC6KBCG5YJLJIIRJ4JUHSJQJMJFJGIPJOKEK6JSKOITKMKHL0JZL2K1IUKIJCCJK8LZM0CKL4KSK2KLJWN0KCM2KVMCKWLBMSKQKZL6IWMVM460L8K406LELHLCHXLKLIMWLM1GLSHVLOLQLUNQHZLWMYM6I1M8N2MANEMFI2NG1EN4NINLN6N8MGNANNICMINCMK18NSOWOVMMI6MONPOYP2MQ1KI4P0NVP4IG1CP9IAI8P71AIEON1IQ6Q4PTIJPRIKPBPCPWOPOQPEOTPGQ0PIPKPNQI0OPPQKPZQONZQAQ3QMQSQDQEREQ8QHQWRHQUQQRM5OPUR2RIRAQZNXRKR0R4R6TEO1R8RCROS2OAS4RQO2S9SERSS6O6RXO4SGTGSDSAOCRVO8S0OESLRYOGSJTKUAOITJTMOKSSTPU0U3TQTYSPTWSQTSU4SNTUSWUD16T8U7SYU8T6UET4T0T2SUTBTC"]
+ROUND = {w.split(":")[0]: (float(w.split(":")[1][:-1]), w[-1]) for w in """
+puA1:-1.99- puA0:-1.61- src0:-1.25v ggA0:-0.85v puA2:-0.22- ggA1:0.36a onA0:0.94- load0:1- src1:1.2- load1:2- markA1:2.33- markA0:2.54- load2:3- yA1:3.95v load3:4- back1:4.01- absA3:4.18- back0:4.35- RA0:4.54- onA1:4.71- yA0:4.8- load4:5- duA2:5.15- duA0:5.65- ggB1:5.66a sgA1:5.91a load5:6- puB1:6.08- laA1:6.13- duA1:6.28- holdA0:6.41a lb2:6.83- lb1:7.16- lb0:7.68- puB2:7.86- ooA1:7.93v ggB0:8.18v dnB0:8.21a laA0:8.32- puB0:8.38- sum8:8.62- absA0:8.75- markB1:8.78- back3:9.08- absA2:9.44- ooA0:10.32v absA1:10.38- eA1:10.78- bA0:10.83- lb3:10.95v duB0:10.99- bA1:11.11- markB0:11.16- dnA1:11.17v laA2:11.24a sum9:11.24- laB0:11.31- uxA1:11.48- yB0:11.67a holdA4:11.71- dnA0:11.71- onB0:11.86- back2:11.89- laA3:11.89- duB1:12.42- RB0:12.68a holdA1:13.05- ZA0:13.15v holdB4:13.44- uxA0:13.5- dnB1:13.53a yw0:13.58- absB3:13.61- holdA2:13.62- holdB1:13.71- sgA0:13.81- yB1:14.19a eA0:14.26- onB1:14.28- ooB0:14.29- absB0:14.33- uvA1:14.41- holdB0:14.71a laB1:14.81- yw4:14.81a sgA2:14.84- laB2:15.03- holdA3:15.17- fin2:15.3- swapA0:15.37- uxB1:15.4- absB2:15.52- bB0:15.7- holdB2:15.92- absB1:16.2- urA1:16.31- yw3:16.54- yr0:16.78- ooB1:16.88v expA0:16.92- urA2:16.94- fin1:16.97- set0:17- set7:17- set9:17.05- set1:17.1- set10:17.1- bB1:17.11- set13:17.12- set14:17.15- set2:17.2- set11:17.2a fin0:17.3- set12:17.3- set15:17.4- laB3:17.41- set18:17.5- ZA1:17.53v laB4:17.55- nameB1:17.59- duB2:17.65- XB0:17.68a eB0:17.74- expA1:18.02- eA2:18.06- swapA2:18.16- swapA3:18.17- holdB3:18.21- urB1:18.32- eB1:18.33- laA4:18.38- wall4:18.5v yw5:18.6- nameA0:18.66- XA0:18.68a uvA0:18.69- uxB0:18.86- set16:19- set17:19.1- swapB0:19.12- set8:19.2- XB1:19.51a nameA1:19.52- nameB2:19.57- swapA1:19.64- urB0:19.76- first3:19.82- swapB3:19.85- nameB0:19.94- swapB1:20.06- urA0:20.15- first1:20.25- first2:20.59- first0:20.62- first4:20.69- first5:20.89- wall5:20.91v first6:21.34- uvB0:21.41- swapB2:21.57- dnt1:21.58- urB2:21.83- yr1:21.87a yr2:22.04- eB2:22.12- XA1:22.16v nameB3:22.39a wall6:22.73v wall0:22.9v uvB1:23.6- yw2:23.75- wall1:23.83v dnt0:24.79- wall3:24.98- wall7:25.18a yw1:25.47v expB0:25.53- ZB0:27.09v ZB1:28.72v expB1:29.35- sum0:30.35- sum6:30.72- wall2:31.32- sum2:32.29- sum1:32.35- sum4:32.43- sum7:33.3- sum3:33.57- sum5:33.92- tot2:34.78- tot0:35.3v tot1:36.72-
+""".split()}
+ROUND = {w.split(":")[0]: (float(w.split(":")[1][:-1]), w[-1]) for w in """
+ggA1:-4.36a ggA0:-4.06a ggA0.4:0.2v src0:0.8v load0:1- load1:1.1- load2:1.2- load3:1.3- puA1:1.4- puA2:1.5- early0:2- early1:2.01- early11:2.1- early3:2.2- early4:2.21- early5:2.22- early9:2.3- early6:2.31a early10:2.32a early12:2.33a early8:2.34a early2:2.4- early14:2.45- first0:2.46- first1:2.46- first2:2.47- early7:2.5- early13:2.6- first3:2.7- first4:2.8- early15:2.9a early16:2.91a early17:2.92v early18:2.93- set54:2.99- load4:3- load5:3.1- dnt0:3.2- puA0:3.23- dnt1:3.3- first5:3.4- set5:3.5- markA0.1:3.6- ggB0.1:3.7v ggB1.1:3.7a lb0.1:3.8- lb1.1:3.81- lb2.1:3.82- markB0.1:3.83- dnA0.1:3.9a dnA1.1:3.91a duA0.1:3.92- duA1.1:3.93- yA0.1:4a yA1.1:4.1a ggB0:4.6v ggB1:4.6a markA0:4.61- duA0:4.84- back0:5- duA1:5.35- duA2:5.5- lb1:5.95- lb2:6.15- yA0.4:6.18v sgA0.4:6.23- puB1:6.45- puB2:6.6- markB0:6.6- lb3:6.7a laA0.4:6.7- RA0:6.8a laA1:6.9- lb0.4:7.14- puB0:7.9- laA0:8.1- sumA4:8.15- laA1.4:8.15- absA0:8.2- yA1:8.24a onA0:8.3- absA1:8.37- absA2.4:8.46- yA0:8.54a lb0:8.55- dnB0:8.6a absA2:8.7- yB0.1:8.85v sgA1:8.93v duB0:9.02- dnB1:9.4a ooA0:9.55v ooA1:9.55a eA1:9.56- laB0:9.6- RB0:9.61a back1:10- sum4:10- sum9:10- lb2.4:10.14- bA0:10.29- duB1:10.3- eA0:10.3- laA3:10.32- sgA2:10.4- yB0:10.45v bA1.4:10.53- laB3.4:10.54- sgA0:10.58- absA3:10.8- holdA0:10.95v eA2:11.05- onB0:11.2- duA2.1:11.21- duB2:11.3- yB1:11.3a absA1.1:11.34- ooB0.1:11.38- holdB0:11.39v ooB0:11.4v fin0.4:11.49- fin2:11.6- laB1.1:11.96- bA1.1:12.09- eA0.1:12.09- laA4:12.1- laB0.1:12.11- absB0:12.12- holdA1:12.15- yB0.4:12.15a laB1:12.16- yB1.4:12.17- onB1:12.2- holdA3:12.25- laB2:12.31v ooB1:12.32- ooB1.1:12.32a absB1:12.4- laB4:12.45- bB1:12.6- bB0:12.61- absB2:12.67- laB1.4:12.68- laA2:12.79- bA1:12.88- absB3:12.9- holdB2:12.97- sumA1:12.97- holdA4:13.05- bB0.1:13.08- eB0:13.1- laB3:13.1- holdA2:13.14- swapA0:13.15- back2:13.2- uxA0:13.2- swapB0.4:13.26- swapB0.1:13.26- uxA1:13.35- fin1.4:13.45- swapA2:13.5- expA0:13.5- laB0.4:13.54- eB1:13.7- swapA3:13.75- eB2:13.8- nameA0:13.95- holdB1:14.1- uvA0:14.1- nameA1:14.2- holdB2.4:14.29- holdB3:14.3- swapB1:14.35- holdB4:14.5- swapB2:14.7- uxB0:14.7- ZB0.4:14.87a absB0.4:14.88- swapB3:14.9- XA0:14.98a uxB1:15- expA1.4:15.02- expB0:15.1- urA0:15.23- urB1:15.4- holdB2.1:15.42- uvB1:15.5- swapA1:15.95- ZA0:16v sum0:16- uvA1.1:16.02- swapB0:16.09- sumA0:16.1- sum1:16.2- ZB1.4:16.25a sum2:16.4- ZA1:16.5v laA3.1:16.59- sum3:16.6- XA1:17a set29:17.43a nameB0:17.45- holdB3.1:17.59- urB0:17.6- sumA2:17.9- sum5:18- laB4.4:18.12- expB1:18.15- sum6:18.2- sum7:18.4- sumA5:18.5- yr0:18.5- uvB0:18.53- sum8:18.6- sumA6:18.7- wall0:19v wall1.4:19v XB0:19.18- yr1:19.2- wall3:19.5a yr2:19.5- nameB3:19.6a yw0:20- wall2.4:20.01a wall7.4:20.26v wall4.4:20.3a nameB2:20.5- wall6:20.5v yw1:20.5- sumB0:20.6- sumA3:20.85- XB1.4:20.94- yw2:21- yw3:21- nameB1:21.23- uvA1:21.43- yw4:21.5- sumA2.1:21.86- set37:21.89a yw5:22- set23:22.12a set36:22.52- sumB2:23- wall5.4:23.01a set38:23.34a sumB4:23.5- sumB5:23.7- sumB6:25.5- set49:25.57v sumB7:25.7- tot0:26a tot1:26.2- sumA7:28.96- sumB1:28.97- set58:29.95- set10:31.97v sumB3:36.71- set57:38.96- set63:75.92-
+""".split()}
+ROUND = {w.split(":")[0]: (float(w.split(":")[1][:-1]), w[-1]) for w in """
+ggA0:-0.23a ggA1:0a src0:0.8v puA0:0.8- load0:1- load1:1.1- load2:1.2- load3:1.3- puA1:1.4- load5:1.4- puA2:1.5- early0:2- early1:2.01- early11:2.1- early3:2.2- early4:2.21- early5:2.22- early9:2.3- early6:2.31a early10:2.32a early12:2.33a early8:2.34a early13:2.35a early2:2.4- early14:2.45- first0:2.46- first1:2.46- first2:2.47- early7:2.5- early15:2.6- load4:2.7- first3:2.7- first4:2.8- early16:2.91a early17:2.92v early18:2.93- dnt0:3.2- dnt1:3.3- first5:3.4- set5:3.5- markA0.1:3.6- ggB0.1:3.7v ggB1.1:3.7a lb0.1:3.8- lb1.1:3.81- yB0.1:3.81v lb2.1:3.82- markB0.1:3.83- dnA0.1:3.9a duA0.1:3.92- duA1.1:3.93- yA0.1:4a yA1.1:4.1a set41:4.16a yA0.4:4.59v ggB0:4.6v duA1:5.35- duA2:5.5- dnA1.1:5.5v markA0:5.67- lb1:5.95- lb2:6.15- puB1:6.45- laA0.4:6.57- puB2:6.6- markB0:6.6- lb3:6.7a ggB1:6.79a RA0:6.8a yA1:7.1a duA0:7.27- yA0:7.8a RB0:8.1a absA0:8.11- laA1:8.12- dnB0:8.6a absA2:8.7- lb0.4:8.7- puB0:8.9- lb0:9.07- dnB1:9.4a ooA0:9.55v ooA1:9.55a laB0:9.6- absA1.1:9.64- sgA1:9.83v back0:10- sum4:10- sum9:10- lb2.4:10.13- laA0:10.19- duB1:10.3- laA3:10.32- absA1:10.35- eA1:10.4- sgA2:10.4- yB0:10.45v duB0:10.48- eA0:10.48- bA0:10.59- bA1.4:10.67- eA2:10.71- sgA0:10.75- absA3:10.8- holdA0:10.95v bA1.1:11.05- holdA4:11.2- duB2:11.3- yB1:11.3a ooB0:11.4v duA2.1:11.49- fin1:11.5- laB3:11.53- absB2.4:11.59- fin2:11.6- absB0:11.82- bB1:11.82- laB4:11.97- laB1:12- holdA2:12.05- fin0.4:12.08- eA0.1:12.09- holdA1:12.15- holdA1.4:12.15- RB0.4:12.16a onB1:12.2- laB0.1:12.21- holdA3:12.25- laB2:12.31v ooB1:12.32a onA0:12.34- yB0.4:12.38- absB1:12.4- absB2:12.67- bA1:12.76- laB0.4:12.79- absB3:12.9- bB0:12.9- back1:13- eB0:13.1- swapA0:13.15- uxA0:13.2- swapA1:13.3- ooB0.1:13.32- holdB2.4:13.34- uxA1:13.35- swapB0.4:13.35- swapA2:13.5- expA0:13.5- laA2:13.64v eB1:13.7- laA4:13.71- swapA3:13.75- eB2:13.8- nameA0:13.95- holdB1:14.1- uvA0:14.1- swapB0:14.1- nameA1:14.2- swapB1.4:14.27- holdB3:14.3- holdB0.4:14.34v absB0.4:14.39- onB0:14.44- holdB4:14.5- urA0:14.58- laB4.4:14.65- uxB0:14.7- swapB3:14.9- expA1.4:14.99- uxB1:15- urB0:15.1- uxB1.1:15.27- uxB1.4:15.37- uvB1:15.5- holdB0:15.51v swapB2:15.67- laB1.1:15.81- holdB2:15.88- ZA0:16v sum0:16- sumA0:16.1- swapB1:16.16- sumA1:16.2- sum1:16.2- sum2:16.4- ZA1:16.5v sum3:16.6- XA0:16.8a XA1:17a ZB1.4:17.2a uvA1.1:17.22- urB1:17.44- nameB0:17.45- yw1.4:17.62v sumA2:17.9- sum5:18- lb3.1:18.02- sumA4:18.2- sum6:18.2- ZB0.4:18.2a holdB3.1:18.45- sumA5:18.5- yr0:18.5- sum8:18.6- sumA6:18.7- wall0:19v wall1.4:19v expB0:19.13- uvB0:19.16- yr1:19.2- wall3:19.5a yr2:19.5- nameB3:19.6a expB1:19.7- XB0:19.95- set21:20.22a set7:20.24a wall7.4:20.26v XB0.1:20.41a nameB2:20.5- wall6:20.5v wall2.4:20.5a sumB0:20.6- sumB1:20.8- XB1.4:20.93- yw2:21- yw3:21- set37:21.46- yw4:21.5- nameB1:21.7- sumA0.1:21.72- uvA1:21.92- yw5:22- set26:22.36v nameB3.1:22.38v set61:22.6- sumB2:23- set15:23.02- set60:23.03- set16:23.09a sumB3:23.2- sumB4:23.5- sumB5:23.7- yw0.4:24- set9:24.84v wall4.4:24.98- wall5.4:24.99a sum7.4:25- sumB6:25.5- sumB7:25.7- tot0:26a tot1:26.2- set68:26.9- set25:28.05a set36:28.39v set34:28.68- sumA3:32.19- set48:32.25- set11:36.89- sumA7:38.01- set62:40.73- set63:42.55- set65:59.1- set20:71.74v set30:74.47a set44:81.86v
+""".split()}
+ROUND = {w.split(":")[0]: (float(w.split(":")[1][:-1]), w[-1]) for w in """
+ggA0:0v ggA1:0a ggA1.4:0.04a puA0:0.8- load0:1- load1:1.1- load2:1.2- load3:1.3- load5:1.4- puA2:1.5- early0:2- early1:2.01- early11:2.1- early3:2.2- early4:2.21- early5:2.22- early9:2.3- early6:2.31a early10:2.32a early12:2.33a early8:2.34a early13:2.35a early2:2.4- early14:2.45- first0:2.46- first1:2.46- set39:2.46- first2:2.47- early7:2.5- early15:2.6- ggA0.4:2.6v load4:2.7- first3:2.7- first4:2.8- set54:2.8- early16:2.91a set38:2.91- early17:2.92v early18:2.93- src0:3.02v dnt0:3.2- dnt1:3.3- first5:3.4- set5:3.5- markA0.1:3.6- ggB0.1:3.7v ggB1.1:3.7a lb0.1:3.8- lb1.1:3.81- lb2.1:3.82- markB0.1:3.83- dnA0.1:3.9a duA0.1:3.92- duA1.1:3.93- yA0.1:4a yA1.1:4.1a yB0.1:4.26v puA1:4.29- ggB0:4.6v ggB1:4.6a duA1:5.35- markA0:5.67- puB0:5.9- lb1:5.95- yA1:6.05a dnA1.1:6.11v lb2:6.15- yA0:6.17a dnB1.1:6.34a dnB0.1:6.41a duB0.1:6.42- yA0.4:6.5v puB2:6.6- markB0:6.6- lb3:6.7a yA1.4:6.74a ggB1.4:6.74- duA0:6.76- RA0:6.8a laA0:8.1- duA2:8.2- absA0:8.2- onA0:8.3- puB1:8.5- absA2:8.7- lb0:8.86- bA0:9- laA1:9.04- RB0:9.21a ooA0:9.55v sgA0:9.55- laB0:9.6- laB1:9.61- puB0.4:9.71- sgA1.1:9.83- laA0.1:9.87- absA3.1:9.87- absA1.1:9.87- sgA1.4:9.92v back0:10- lb2.4:10.13- duB1:10.3- eA0:10.3- laA3:10.32- holdA0.1:10.33a bB1:10.35- bA1.1:10.35- absA0.1:10.38- eA1:10.4- sgA2:10.4- yB0:10.46a ooA1:10.79- absA2.1:10.87- holdA0:10.91v laB3:10.92- bA0.1:10.94- absB0:10.99- sgA1:11.02v absA2.4:11.02- eA2:11.05- yB1:11.05a absA1:11.12- duB0:11.14- onB0:11.2- absB3:11.3- bA1:11.4- absA3:11.45- fin1:11.5- fin2:11.6- absA0.4:11.61- yB1.4:11.61a ooA0.1:11.66- ooB0:11.95a absB2:12.04- holdA2:12.05- laA4:12.1- holdA1:12.15- onB1:12.2- holdA3:12.25- ooB1:12.3v absB1:12.4- laB0.1:12.74- absB0.1:12.75- holdA0.4:12.82- yB0.4:12.89- laB2:12.9- bB0:12.9- eB0:13.1- uxA0:13.2- swapA1:13.3- uxA1:13.35- bB1.1:13.36- duB2:13.4- holdA4:13.51- laA2:13.64v swapA3:13.75- eB2:13.8- absB2.1:13.86- laB4:13.9- nameA0:13.95- eB1:13.98- holdB0:14a urA0:14- holdB0.4:14.06v uvA0:14.1- absB2.4:14.18- nameA1:14.2- holdB1.4:14.24- holdB3:14.3- swapA0:14.35- holdB4:14.5- laA2.4:14.66a swapB2:14.7- uxB0:14.7- bB0.4:14.71- laA2.1:14.73v laB1.1:14.87- expA0.4:14.95- uxB1:15- absB0.4:15.05- urB0:15.1- expB0:15.1- uvB1:15.5- swapB1.4:15.85- swapA2:15.86- ZA0:16v back1:16.1- swapB3:16.13- holdB2:16.55- fin0.4:16.57- swapB0:16.66- XA0:16.8a XA1:17a ZB0:17v uxB0.4:17.31- nameB1:17.5- ZA1.4:17.77- sumA1.4:17.99- expA1.4:18.08- holdB1:18.36- XB1:18.5a yr0:18.5- lb3.1:18.95a urB0.4:19.11- XB0.1:19.14a swapB1:19.3- yr2:19.5- nameB3:19.6a expB1:19.7- wall3.4:19.91v wall2.4:19.94a expA0:19.95- ZB1.4:19.95- wall1.4:19.98v wall5:20a yw0:20- swapB0.1:20.28- set68:20.49- wall6:20.5v yw1:20.5- swapB1.1:20.73- set26:20.89a XB0:20.91- yw3:21- uvA1.1:21.02- urB1:21.11- uvB0:21.25- holdB2.1:21.27- yw4:21.5- nameB0:21.63- nameB2:21.68- uvA1:21.75- sumA0:21.89- yw5:22- wall0.4:22.95a wall7.4:23.25v onB1.1:23.91- set63:24.1- uvA1.4:24.54- yr1.4:24.83v wall4.4:24.98- yw2.4:25.14- set17:25.89- tot1:26.2- sumB0:26.37- sumA2.1:26.41v set21:26.78- sumA1:26.9- set27:27.21- sumA2:27.31a sumB1:27.32- sumB2:28- set59:28.72v set36:28.76- set58:28.99v sumB0.1:29.2- set44:29.49a set34:30.22- tot0:35.31- set55:56.01- set29:58.36a set67:76.12-
+""".split()}
+PLAN = ["""
+load0 load1 early0 early11 early1 load2 early3 early4 early5 load3 set1 set4 early9 set2 load5 early6a early2 early14 early8a early10a first1 set3 set6 set7a set36a early12a early7 set39 set38 first0 early13a set34a set51 set8 set15a set59v set14a set24a set57 set67 early16a set37 set13a early15 set45 load4 set74 set68 set10a set75 first2 set40a set52 early17v markA0.1 set48 first3 set50 set16a set70 set25a set5 set58a early18 dnt0 set49 set17a set26a set23a set11a set12a set46 set27a first4 set41a set42a set47 set53a yA0.1a yA1.1a bA1.1 ggB1.1a set9a ggB0.1v laA1.1 yB1.1v lb0.1 first5 yB0.1a set18a absA0.1 onB1.1 bA0.1 set21a laA0.1 onA0.1 set22a dnt1 lb1.1 set55 set35a set0 dnA1.1a dnA0.1a set19a set54 set61 lb2.1 set28a markB0.1 back0.1 duA0.1 absA2.1 absA1.1 absB0.1 sgA0.1 bB0.1 duA1.1 set69 ooA0.1v onB0.1 lb3.1v set32a laA2.1a laA3.1 set43a set62 sgA1.1v set31a dnB1.1a set71 ooA1.1a absA3.1 dnB0.1a absB1.1 set30v set63 eA0.1 sgA2.1 laA4.1 set73 set65 duA2.1 set60 eA1.1 bA2.1 set66 holdA2.1 duB0.1 holdA0.1a set44v eA2.1 set20a set72 holdA1.1 laB0.1 duB1.1 holdA3.1 set29v holdA4.1 absB2.1 uxA0.1 set56 bB1.1 ooB1.1a laB2.1a laB1.1 set33a duB2.1 ooB0.1v back1.1 set64 swapA0.1 uxA1.1 absB3.1 bB2.1 swapA1.1 nameA0.1 swapA2.1 laB3.1 eB0.1 swapA3.1 nameA1.1 swapB0.1 laB4.1 holdB0.1v eB1.1 holdB1.1 uvA0.1 holdB2.1 uvA1.1 holdB3.1 expA0.1 holdB4.1 swapB1.1 urA0.1 uxB0.1 swapB2.1 ggA0.2a swapB3.1 urB0.1 eB2.1 ggA1.2a urB1.1 sumA0.1 urB2.1 duA0.2 uvB0.1 XA0.1a uvB1.1 XB0.1a puA0.2 src0.2v puA1.2 nameB0.1 nameB1.1 RA0.2a bA0.2 markA0.2 nameB2.1 laA0.2 ggB0.2v nameB3.1v ggB1.2a puA2.2 yA0.2a yA1.2a lb0.2 uxB1.1 sumA1.1 onA0.2 RB0.2a puB0.2 laA2.2v duA2.2 lb1.2 expB0.1 lb2.2 duA1.2 puB1.2 absA0.2 duB0.2 bA1.2 laA1.2 absA2.2 absA1.2 markB0.2 duB1.2 laB0.2 expB1.1 absA3.2 sgA0.2 ooA0.2v puB2.2 ooA1.2a lb3.2v onB0.2 sgA1.2v sumB0.1 bB0.2 eA0.2 laB2.2a laA4.2 laA3.2 sgA2.2 eA1.2 yB0.2a yB1.2a bA2.2 holdA0.2a ooB1.2a sumB1.1 absB0.2 holdA1.2 laB1.2 ooB0.2v holdA2.2 eA2.2 onB1.2 absB1.2 sumA2.1v sumB2.1v tot0.1 holdA3.2 laB4.2 duB2.2 holdA4.2 swapA0.2 back1.2 absB2.2 uxA0.2 bB1.2 laB3.2 uxA1.2 absB3.2 bB2.2 swapA1.2 swapA2.2 swapB0.2 holdB2.2 expA0.2 eB0.2 swapA3.2 nameA0.2 holdB0.2a holdB1.2 nameA1.2 swapB1.2 uvA0.2 eB1.2 holdB3.2 holdB4.2 eB2.2 swapB2.2 urA0.2 back0.2 swapB3.2 urB0.2 urB1.2 uvA1.2 urB2.2 uvB0.2 ggA0.3a ggA1.3a src0.3v uvB1.2 puA0.3 XA0.2a XB0.2a uxB0.2 puA1.3 markA0.3 nameB0.2 uxB1.2 RA0.3a duA0.3 duA1.3 nameB1.2 nameB2.2 bA0.3 puA2.3 duA2.3 ggB0.3v laA0.3 ggB1.3a lb0.3 puB0.3 yA1.3a yA0.3a expB1.2 laA1.3 nameB3.2v sumA1.2 absA2.3 sumA0.2 lb1.3 RB0.3a expB0.2 duB0.3 absA0.3 bA1.3 bB0.3 lb2.3 onA0.3 puB1.3 puB2.3 markB0.3 laA2.3v ooA0.3v sgA0.3 absA3.3 lb3.3v sgA1.3v onB0.3 sgA2.3 sumB0.2 absA1.3 ooA1.3a laB0.3 eA0.3 laA4.3 back0.3 laA3.3 yB0.3a eA1.3 sumB1.2 bA2.3 absB0.3 yB1.3a laB2.3v eA2.3 holdA0.3a duB1.3 ooB1.3a ooB0.3v sumB2.2a laB1.3 holdA1.3 holdA2.3 absB2.3 absB1.3 onB1.3 duB2.3 laB4.3 swapA0.3 laB3.3 holdA3.3 sumA2.2v tot0.2 holdA4.3 swapA1.3 bB1.3 absB3.3 bB2.3 uxA0.3 swapB0.3 swapA2.3 uxA1.3 eB0.3 holdB0.3a holdB2.3 swapA3.3 swapB1.3 eB1.3 holdB1.3 expA0.3 back1.3 holdB3.3 uvA0.3 nameA0.3 eB2.3 urA0.3 holdB4.3 uvA1.3 swapB2.3 uxB0.3 swapB3.3 nameA1.3 ggA1.4a urB0.3 urB1.3 uvB0.3 ggA0.4v uvB1.3 puA0.4 sumA1.3 puA1.4 nameB0.3 urB2.3 XA0.3a XB0.3a RA0.4a nameB1.3 markA0.4 nameB2.3 ggB0.4v uxB1.3 puA2.4 sumA0.3 laA0.4 bA0.4 ggB1.4a lb0.4 puB0.4 nameB3.3v yA0.4a yA1.4a lb1.4 expB0.3 lb3.4v absA0.4 absA2.4 absA1.4 lb2.4 absA3.4 puB1.4 markB0.4 puB2.4 bA1.4 laA1.4 RB0.4a expB1.3 laA2.4v laA3.4 bA2.4 sgA0.4 sgA1.4a sgA2.4 holdA0.4v holdA1.4 laB0.4 swapA0.4 sumB0.3 fin0.4 bB0.4 sumB1.3 sumA2.3v holdA2.4 holdA3.4 sumB2.3a holdA4.4 uxA0.4 yB1.4a tot0.3 absB2.4 laA4.4 yB0.4v absB0.4 uxA1.4 fin1.4 swapA1.4 swapA2.4 expA0.4 laB2.4a bB1.4 absB3.4 laB1.4 absB1.4 bB2.4 swapA3.4 laB3.4 uvA0.4 expA1.4 holdB0.4a uvA1.4 sumA2.4 fin2.4 holdB1.4 swapB0.4 oldA0.4 urA0.4 holdB2.4 XA0.4a laB4.4 oldB0.4 holdB3.4 holdB4.4 uxB0.4 XA1.4a uxB1.4 expB1.4 expB0.4 sumA4.4 sumA1.4 sumA0.4 swapB1.4 swapB2.4 swapB3.4 urB0.4 sumA7.4 uvB0.4 sumA3.4 sumB1.4 sumA6.4 urB1.4 ZA0.4v sumB0.4 sumB4.4 ZA1.4v ZB0.4a ZB1.4a sumB3.4 yr0.4 uvB1.4 XB0.4v XB1.4a wall0.4v sumB2.4 wall2.4v wall1.4a wall3.4a sumB5.4 yw0.4 wall5.4a wall4.4a wall6.4v wall7.4v sumB6.4 yw1.4v yw3.4 sumB7.4 sumA5.4 yr1.4v yw2.4 yr2.4 yw4.4a yw5.4 tot0.4a tot1.4
+"""]
+PLAN = ["""
+set61 early0 load1 early3 early4 early1 load0 early5 load3 load2 load5 early9 set1 early11 early8a set7a set8 early13v early14 early16a early2 first1 early10a load4 early12a set2 early6a early15 early17a set37 set4 set38 set68 first2 early7 dnt0 first0 early18 set39 set41a set13a first3 set3 set15v set17a first4 set45 dnt1 set50 far1 set59a far0 set6 set34v set23a set0 set47 set5 set40v set52 set46 set74 set49 set67 first5 markA0.1 set48 set16a set57 set36a set25a ggB0.1v yA1.1a yA0.1a set26a set10a set51 ggB1.1a onA0.1 yB0.1v set71 yB1.1a bA1.1 laA1.1 set27a lb0.1 lb1.1 lb2.1 bB1.1 set14a laA0.1 absA2.1 bA0.1 absA0.1 set53a set54 set28a markB0.1 far2 set65 set9a set24a lb3.1a set22a set11a dnA1.1a dnA0.1a absA3.1 duA0.1 duA1.1 set55 ooA0.1v absA1.1 set69 ooA1.1a sgA0.1 bA2.1 set72 holdA0.1v sgA1.1a onB0.1 sgA2.1 set58v eA0.1 set63 duA2.1 set60 absB0.1 holdA1.1 eA1.1 eA2.1 set12a set18v set56 dnB1.1a set42a laA2.1a laB0.1 absB2.1 set70 set73 set66 dnB0.1v laA3.1 set19a duB0.1 holdA2.1 holdA3.1 holdA4.1 set75 set43a set44a swapA0.1 bB0.1 uxA0.1 duB1.1 absB1.1 laA4.1 absB3.1 ooB0.1v ooB1.1a back1.1 laB1.1 set29a swapA1.1 bB2.1 swapA2.1 uxA1.1 laB2.1a set62 swapA3.1 set32v laB3.1 urA0.1 holdB0.1v swapB0.1 duB2.1 holdB1.1 urA1.1 set35a set30a laB4.1 nameA0.1 holdB2.1 holdB3.1 holdB4.1 eB0.1 eB1.1 uvA0.1 uxB0.1 set21a swapB1.1 expA0.1 nameA1.1 swapB2.1 uvA1.1 swapB3.1 ggA1.2a ggA0.2v XA0.1a uvB0.1 back0.1 sumA0.1 urA2.1 urB0.1 puA0.2 eB2.1 uxB1.1 set20v src0.2a RA0.2a duA0.2 uvB1.1 puA1.2 urB1.1 XB0.1v nameB0.1 puA2.2 nameB1.1 urB2.1 markA0.2 nameB2.1 ggB0.2v set31v sumA1.1 set64 onA0.2 expB0.1 yA1.2a yA0.2a bA0.2 laA0.2 onA1.2 absA2.2 absA0.2 ggB1.2a lb0.2 nameB3.1v absA3.2 lb1.2 absA1.2 laA2.2a puB0.2 bA2.2 lb2.2 duA1.2 set33a puB1.2 duB0.2 RB0.2a expB1.1 markB0.2 puB2.2 bA1.2 lb3.2a holdA0.2a bB0.2 holdA1.2 onB0.2 laA1.2 ooA1.2a ooA0.2v sgA0.2 laB0.2 duA2.2 duB1.2 laA4.2 laA3.2 holdA2.2 sgA1.2a sgA2.2 eA0.2 yB1.2a yB0.2a eA1.2 eA2.2 holdA3.2 duB2.2 swapA0.2 absB2.2 absB0.2 laB2.2a laB1.2 ooB0.2v holdA4.2 uxA0.2 ooB1.2a absB1.2 absB3.2 sumB0.1 sumB1.1 swapA1.2 uxA1.2 laB3.2 eB0.2 eB1.2 swapA2.2 swapA3.2 expA0.2 onB1.2 bB1.2 nameA0.2 urA0.2 bB2.2 urA1.2 nameA1.2 holdB0.2a back1.2 holdB1.2 ggA0.3v laB4.2 uvA0.2 uvA1.2 holdB2.2 back0.2 sumA2.1v swapB0.2 holdB3.2 swapB1.2 eB2.2 holdB4.2 urA2.2 swapB2.2 ggA1.3a puA0.3 puA1.3 swapB3.2 uxB0.2 uxB1.2 uvB0.2 sumB2.1a src0.3v puA2.3 urB0.2 urB1.2 tot0.1 XA0.2a duA0.3 nameB0.2 uvB1.2 nameB1.2 markA0.3 nameB2.2 RA0.3a urB2.2 bA0.3 onA0.3 laA0.3 XB0.2a yA0.3a absA0.3 ggB1.3a duA1.3 ggB0.3v lb0.3 sumA1.2 nameB3.2a yA1.3a onA1.3 puB0.3 lb3.3v laA2.3v lb1.3 absA1.3 lb2.3 duA2.3 absA2.3 laA1.3 puB1.3 expB1.2 absA3.3 bA2.3 duB0.3 bA1.3 markB0.3 RB0.3a puB2.3 duB1.3 ooA0.3v expB0.2 onB0.3 laB0.3 sgA0.3 laA3.3 sumA0.2 back0.3 ooA1.3a sgA1.3a swapA0.3 holdA2.3 sgA2.3 holdA0.3v yB0.3a eA0.3 eA1.3 laA4.3 yB1.3a bB0.3 sumB0.2 eA2.3 absB0.3 absB2.3 holdA1.3 sumB1.2 ooB0.3v ooB1.3a back1.3 holdA3.3 holdA4.3 bB1.3 sumA2.2a onB1.3 laB2.3a duB2.3 swapA1.3 uxA0.3 laB1.3 swapA2.3 uxA1.3 swapA3.3 laB4.3 urA0.3 sumB2.2v laB3.3 absB1.3 absB3.3 bB2.3 nameA0.3 urA1.3 nameA1.3 swapB0.3 uvA0.3 expA0.3 holdB2.3 urA2.3 ggA1.4a uvA1.3 holdB0.3v ggA0.4v eB0.3 holdB1.3 swapB1.3 eB1.3 holdB3.3 holdB4.3 eB2.3 puA0.4 swapB2.3 swapB3.3 puA1.4 puA2.4 tot0.2 uvB0.3 XA0.3a uvB1.3 urB0.3 RA0.4a uxB0.3 bA0.4 markA0.4 XB0.3a laA0.4 nameB0.3 nameB1.3 yA1.4a urB1.3 laA2.4v uxB1.3 nameB2.3 urB2.3 ggB1.4a absA2.4 ggB0.4v nameB3.3a expB1.3 yA0.4v puB0.4 puB1.4 sumA0.3 lb0.4 expB0.3 absA3.4 absA0.4 absA1.4 bA1.4 laA1.4 bA2.4 lb1.4 RB0.4a laB0.4 lb2.4 markB0.4 holdA0.4a holdA1.4 bB0.4 laA3.4 holdA2.4 sgA0.4 holdA3.4 swapA0.4 sgA1.4v puB2.4 yB1.4a yB0.4a laB1.4 absB0.4 holdA4.4 lb3.4a sumB0.3 sumB1.3 sumB2.3v uxA0.4 laB2.4v uxA1.4 absB1.4 absB2.4 bB1.4 sgA2.4 sumA1.3 fin0.4 expA0.4 sumA2.3v expA1.4 laB4.4 laB3.4 absB3.4 bB2.4 tot0.3 sumA0.4 laA4.4 sumA1.4 fin1.4 swapA1.4 swapA2.4 swapA3.4 uvA0.4 holdB0.4a holdB2.4 uvA1.4 holdB1.4 urA0.4 holdB3.4 holdB4.4 XA0.4a swapB0.4 uxB0.4 uxB1.4 expB0.4 fin2.4 swapB1.4 expB1.4 XA1.4v sumA2.4 oldA0.4 swapB2.4 urA1.4 ZA0.4a swapB3.4 oldB0.4 uvB0.4 ZA1.4v urB0.4 urB1.4 uvB1.4 sumB4.4 sumB0.4 sumB3.4 ZB0.4v sumB7.4 ZB1.4a yr0.4 sumB2.4 XB1.4a XB0.4v wall4.4a wall7.4a wall6.4v wall5.4v yw3.4 wall0.4a wall3.4a sumB1.4 wall2.4v wall1.4v yr1.4v yw4.4v yr2.4 yw0.4 yw1.4a sumB5.4 sumB6.4 yw5.4 tot0.4a yw2.4 tot1.4
+"""]
 
 
 def overlap(hist, reads, writes):
@@ -69,119 +94,112 @@ def banks(o):
     return set((nm, b) for nm, lo, hi in o["r"] + o["w"] if SCRATCH[nm][0] == "psum" for b in range(lo // 512, (hi + 511) // 512))
 
 
-def arrange(ops, seed):
-    n = len(ops)
+def graph(ops):
     hist, pred, sent = {}, [], {}
     for i, o in enumerate(ops):
         grp = o.get("group")
-        pred.append(set(p for p in overlap(hist, o["r"], o["w"]) if grp is None or ops[p].get("group") != grp))
+        pred.append(set(p for p in overlap(hist, o["r"] + o.get("after", []), o["w"]) if grp is None or ops[p].get("group") != grp))
         note(hist, i, o["r"], o["w"], grp is not None)
-        if o["kind"] == "send":
-            sent[o["sem"]] = i
-    succ = [[] for _ in ops]
-    for i, o in enumerate(ops):
         if o["kind"] == "land":
-            pred[i].add(sent[o["sem"]])
-        if o["kind"] == "send" and o["sem"] != "an1":
-            pred[i].add(sent["an1"] - 1)
-        for p in pred[i]:
-            succ[p].append(i)
+            pred[i].add(i - 1)
+        if o["kind"] == "send" and o["sem"] != "an":
+            pred[i].add(ORDER["first"])
+        if o["name"] in ("load4", "dnt0"):
+            pred[i].add(ORDER["first"] + 2)
+    return pred
+
+
+def ways(ops, est):
+    out = []
+    for o in ops:
+        w = []
+        for e, cost in o["cost"].items():
+            busy, lat = cost(est)
+            use = [(e, 0.0, busy)] if e != "-" else []
+            use += [(b, 0.0, busy + est["wake"]) for b in banks(o)]
+            if o["kind"] == "dma":
+                use.append(("dma", busy + 0.6 * est["dfix"], busy + lat - 0.4 * est["dfix"]))
+            if o["kind"] == "send":
+                use.append((("link", o["via"] is None), busy + est["rfix"] / 2, busy + est["rfix"] / 2 + lat))
+                lat += est["rfix"] / 2
+            if o["kind"] == "land":
+                way = est["rfix"] / 2
+                if o["via"] is not None:
+                    way += (est["first"] if o["sem"] in ("l200", "l210") else 0) + est["riss"] + est["rfix"] + (est["dfix"] + 1.0) * o["via"] * (o["d"] == 1)
+                    use.append(("port", way, way + lat))
+                    way += lat
+                lat = way
+            w.append((e, busy + lat + (est["wake"] if o["kind"] != "send" else 0.0), use))
+        out.append(w)
+    return out
+
+
+def place(prio, pred, succ, way, pick):
+    n = len(prio)
+    line, end, got = {}, [0.0] * n, [None] * n
     left = [len(p) for p in pred]
-    topo_ = [i for i in range(n) if not left[i]]
-    for i in topo_:
+    ready = [i for i in range(n) if not left[i]]
+    while ready:
+        i = min(ready, key=lambda k: (prio[k], k))
+        ready.remove(i)
+        t0 = max([end[p] for p in pred[i]] + [0.0])
+        best = None
+        for e, d, use in way[i]:
+            if len(way[i]) > 1 and pick[i] in "va" and pick[i] != e:
+                continue
+            t, moved = t0, True
+            while moved:
+                moved = False
+                for r, a, b in use:
+                    ln = line.get(r, ())
+                    k = len(ln)
+                    while k and ln[k - 1][1] > t + a + 1e-9:
+                        k -= 1
+                    while k < len(ln) and ln[k][0] < t + b - 1e-9:
+                        t, moved = ln[k][1] - a, True
+                        k += 1
+            score = t + d + (0.5 if e == "v" else 0.0)
+            if best is None or score < best[4]:
+                best = (t + d, t, e, use, score)
+        end[i], got[i] = best[0], (best[1], best[2])
+        for r, a, b in best[3]:
+            line.setdefault(r, []).append((best[1] + a, best[1] + b))
+            line[r].sort()
         for s in succ[i]:
             left[s] -= 1
             if not left[s]:
-                topo_.append(s)
-    ways = []
-    for o in ops:
-        w = []
-        for e, (busy, lat) in o["cost"].items():
-            use = [(e, 0.0, busy)] if e != "-" else []
-            use += [(b, 0.0, busy + EST["wake"]) for b in banks(o)]
-            if o["kind"] == "dma":
-                use.append(("dma", busy + EST["dfix"], busy + lat))
-            if o["kind"] == "send":
-                way = EST["rfix"] + (0 if o["via"] is None else EST["rfix"] + 1.5 + 2.5 * o["via"])
-                use.append((("link", o["via"]), busy + way, busy + way + lat))
-                lat += way
-            w.append((e, busy + lat + (EST["wake"] if o["kind"] != "send" else 0.0), use))
-        ways.append(w)
-    back = [[(e, d, [(r, d - b, d - a) for r, a, b in use]) for e, d, use in w] for w in ways]
+                ready.append(s)
+    return end, got
 
-    pen = []
 
-    def place(prio, before, after, ways_):
-        line, end, got = {}, [0.0] * n, [None] * n
-        left = [len(p) for p in before]
-        ready = [i for i in range(n) if not left[i]]
-        while ready:
-            i = min(ready, key=lambda k: prio[k])
-            ready.remove(i)
-            t0 = max([end[p] for p in before[i]] + [0.0])
-            best = None
-            for e, d, use in ways_[i]:
-                t, moved = t0, True
-                while moved:
-                    moved = False
-                    for r, a, b in use:
-                        ln = line.get(r, ())
-                        k = len(ln)
-                        while k and ln[k - 1][1] > t + a + 1e-9:
-                            k -= 1
-                        while k < len(ln) and ln[k][0] < t + b - 1e-9:
-                            t, moved = ln[k][1] - a, True
-                            k += 1
-                if best is None or t + d + (pen[i] if e == "v" else 0) < best[4]:
-                    best = (t + d, t, e, use, t + d + (pen[i] if e == "v" else 0))
-            end[i], got[i] = best[0], (best[1], best[2])
-            for r, a, b in best[3]:
-                line.setdefault(r, []).append((best[1] + a, best[1] + b))
-                line[r].sort()
-            for s in after[i]:
-                left[s] -= 1
-                if not left[s]:
-                    ready.append(s)
-        return end, got
-
-    x = seed * 7919 + 1
-    prio = [0.0] * n
-    for i in reversed(topo_):
-        prio[i] = min([prio[s] for s in succ[i]] + [0]) - min(w[1] for w in ways[i])
-    keep, cur, rnd = None, None, [x]
-    marks = [i for i in range(n) if ops[i]["kind"] == "send"]
-    ORDER["path"] = -min(prio)
-
-    def draw():
-        rnd[0] = (rnd[0] * 1103515245 + 12345) % 2147483648
-        return rnd[0] / 2147483648
-
-    pen[:] = [NOISE[2]] * n
-    if len(PLAN[0]) == 2 * n:
-        for k in range(n):
-            v = int(PLAN[0][2 * k:2 * k + 2], 36)
-            prio[v // 2], pen[v // 2] = k, 99 if v % 2 else -99
-    for it in range(ROUNDS[0]):
-        end, got = place(prio, pred, succ, ways)
-        if it % 2:
-            endb, gotb = place([-v for v in end], succ, pred, back)
-            end, got = place([-v for v in endb], pred, succ, ways)
-        val = max(end) + NOISE[3] * sum(end[i] for i in marks) / len(marks)
-        if keep is None or val <= keep[3]:
-            keep = (max(end), got, list(pen), val)
-        if cur is None or val <= cur[3] + NOISE[4] * (1 - it / ROUNDS[0]) * draw():
-            cur = (max(end), got, list(pen), val)
-        pen[:] = cur[2]
-        lo = draw() * cur[0] - 5
-        hi = lo + NOISE[1] * draw()
-        prio = [cur[1][i][0] for i in range(n)]
-        for i in range(n):
-            if lo <= prio[i] <= hi:
-                prio[i] += NOISE[0] * draw() if it % 3 else (6 * NOISE[0] * (draw() - 0.5) if draw() < 0.1 else 0)
-                if draw() < 0.15:
-                    pen[i] = 2 * NOISE[2] * draw()
-    rank_ = {i: k for k, i in enumerate(topo_)}
-    return [(i, keep[1][i][1]) for i in sorted(range(n), key=lambda k: (round(keep[1][k][0], 6), rank_[k]))], keep[0]
+def arrange(ops):
+    n = len(ops)
+    if PLAN[0]:
+        ix = {o["name"] + (".%d" % o["t"] if o["t"] else ""): i for i, o in enumerate(ops) if o["name"]}
+        out = []
+        for w in PLAN[0].split():
+            i = ix[w] if w in ix else ix[w[:-1]]
+            out.append((i, list(ops[i]["cost"])[0] if w in ix else w[-1]))
+            if ops[i]["kind"] == "send":
+                out.append((i + 1, "-"))
+        assert len(out) == n
+        return out
+    pred, way = graph(ops), ways(ops, EST)
+    succ = [[] for _ in ops]
+    for i in range(n):
+        for p in pred[i]:
+            succ[p].append(i)
+    prio, pick = [0.0] * n, ["-"] * n
+    for i in reversed(range(n)):
+        o = ops[i]
+        at = ROUND.get("%s.%d" % (o["name"], o["t"])) or ROUND.get(o["name"])
+        if at:
+            prio[i], pick[i] = PERIOD * o["t"] + at[0], at[1]
+        else:
+            prio[i] = min([prio[s] for s in succ[i]] + [200.0]) - min(w[1] for w in way[i])
+    end, got = place(prio, pred, succ, way, pick)
+    ORDER["ops"], ORDER["end"] = ops, max(end)
+    return [(i, got[i][1]) for i in sorted(range(n), key=lambda k: (round(got[k][0], 6), k))]
 
 
 def rank_program(g, core, T, topo):
@@ -189,7 +207,7 @@ def rank_program(g, core, T, topo):
 
     def helper(r, h):
         c = T.cores[r % n]
-        return [x for x in topo.cores_of(c) if x != c and (topo.die(x) != topo.die(c)) == bool(h)][0]
+        return [x for x in topo.cores_of(c) if topo.die(x) != topo.die(c)][h]
 
     rank, role = T.rank_of(core), None
     for r in range(n):
@@ -199,7 +217,14 @@ def rank_program(g, core, T, topo):
     if rank is None:
         return
     Q = {"v": g.vector, "a": g.scalar, "p": g.tensor, "g": g, "s": g.sync}
-    ops = []
+    ops, label, count = [], ["", 0], {}
+
+    def at(name, t):
+        label[:] = [name, t]
+
+    def add(**o):
+        k = count[tuple(label)] = count.get(tuple(label), -1) + 1
+        ops.append(dict(o, name=label[0] + str(k), t=label[1]))
 
     def V(name, a=0, b=None, st=1, p=None):
         if b is None:
@@ -210,8 +235,8 @@ def rank_program(g, core, T, topo):
     def IND(win, off):
         return (win[0].indirect(off[0]), win[1] + off[1], 16 * off[2], win[3], "ind")
 
-    def X(*at):
-        return (at, [], 0, "", "dram")
+    def X(*at_):
+        return (at_, [], 0, "", "dram")
 
     def ap(x):
         return T[x[0][0]][x[0][1]:x[0][2], x[0][3]:x[0][4]] if x[4] == "dram" else x[0]
@@ -223,11 +248,8 @@ def rank_program(g, core, T, topo):
         return x[0] if isinstance(x, tuple) else x
 
     def cyc(out, ins, k):
-        if out[4] == "ind":
-            k = EST["s"]
-        elif ins and ins[0][4] == "ind":
-            k = EST["g"]
-        return (EST["fix"] + max(64, k * out[2]) * EST["cyc"], 0.0)
+        key = "s" if out[4] == "ind" else "g" if ins and ins[0][4] == "ind" else None
+        return lambda est: (est["fix"] + max(64, (est[key] if key else k) * out[2]) * est["cyc"], 0.0)
 
     def half(*xs):
         return 0.5 if all(x[3] in (BF, U16) for x in xs) else 1
@@ -237,7 +259,7 @@ def rank_program(g, core, T, topo):
         writes = out[1]
         if out[4] == "ind":
             reads, writes = reads + out[1][1:], out[1][:1]
-        ops.append(dict(kind="op", r=reads, w=writes, calls=calls, cost={e: cyc(out, ins, k) for e, (c, k) in calls.items()}))
+        add(kind="op", r=reads, w=writes, calls=calls, cost={e: cyc(out, ins, k) for e, (c, k) in calls.items()})
 
     def cp(out, a, both=False):
         calls = {"v": (lambda: g.vector.tensor_copy(out[0], a[0]), half(out, a))}
@@ -269,20 +291,21 @@ def rank_program(g, core, T, topo):
     def act(out, a, f, scale=1.0):
         op({"a": (lambda: g.scalar.activation(out[0], a[0], f, scale=scale), 1)}, out, [a])
 
-    def gather(buf, a, win, obuf, oa, cnt):
-        for c in range(0, cnt, CH):
-            m = min(CH, cnt - c)
+    def gather(buf, a, win, obuf, oa, cnt, ch=None):
+        ch = ch or OPT["ch"]
+        for c in range(0, cnt, ch):
+            m = min(ch, cnt - c)
             cp(V(buf, a + c, a + c + m), IND(win, V(obuf, oa + c // 16, oa + (c + m) // 16)), True)
 
-    def iota(out, pat, cm, fl=True):
-        if fl:
-            op({"g": (lambda: g.iota(out[0], pat, 0, cm, allow_small_or_imprecise_dtypes=True), 2)}, out, [])
+    def iota(out, pat, cm, base=0):
+        if out[3] == I32:
+            op({"g": (lambda: g.iota(out[0], pat, base, cm), 2)}, out, [])
         else:
-            op({"g": (lambda: g.iota(out[0], pat, 0, cm), 2)}, out, [])
+            op({"g": (lambda: g.iota(out[0], pat, base, cm, allow_small_or_imprecise_dtypes=True), 2)}, out, [])
 
     runs, seen = {}, {}
 
-    def mm(items, group=None, whole=None):
+    def mm(items, group=None, after=()):
         runs[group] = runs.get(group, 0) + 1
 
         def call():
@@ -291,34 +314,43 @@ def rank_program(g, core, T, topo):
             for i, (o, l, r) in enumerate(items):
                 ins = g.tensor.matmul(o[0], l[0], r[0], start and i == 0, stop and i == len(items) - 1)
             return ins
-        c = sum(max(64, r[2]) * (4 if r[3] == F32 else 1) for o, l, r in items) * EST["pcyc"]
-        ops.append(dict(kind="op", r=[r for it in items for x in it[1:] for r in x[1]], calls={"p": (call, 0)}, cost={"p": (c, 0.0)},
-                        w=whole[1] if whole else sorted(set(r for it in items for r in it[0][1])), group=group))
+        c = sum(max(64, r[2]) * (4 if r[3] == F32 else 1) for o, l, r in items)
+        add(kind="op", r=[r for it in items for x in it[1:] for r in x[1]], calls={"p": (call, 0)}, cost={"p": lambda est: (c * est["pcyc"], 0.0)},
+            w=sorted(set(r for it in items for r in it[0][1])), group=group, after=[r for x in after for r in x[1]])
 
     def wrap(out, s, buf, a, cnt):
         return [(out, V("sel", 144 * s + 15 - k, 144 * s + 143 - k), V(buf, a + k, a + cnt, 16)) for k in range(16)]
 
     def dma(e, pairs, kb):
-        ops.append(dict(kind="dma", r=[r for o, i in pairs for r in i[1]], w=[r for o, i in pairs for r in o[1]], pairs=pairs,
-                        cost={e: (0.1 * len(pairs), EST["dfix"] + kb * 1024 / EST["dbw"])}))
+        add(kind="dma", r=[r for o, i in pairs for r in i[1]], w=[r for o, i in pairs for r in o[1]], pairs=pairs,
+            cost={e: lambda est: (0.1 * len(pairs), est["dfix"] + kb * 1024 / est["dbw"])})
+
+    def rows(buf, a, b, pairs):
+        dma("s", [(V(buf, a, b, p=(r, 128, 16)), tile) for r, tile in pairs], (40 + (b - a) // 24) * len(pairs))
 
     def send(d, out, a, sem, via=None, slot=0):
         by = 128 * a[2] * (4 if a[3] == F32 else 2)
-        ops.append(dict(kind="send", r=a[1], w=[], d=d, out=out, a=a, sem=sem, via=via, slot=slot,
-                        cost={"g": (0.3 + (EST["first"] if sem == "an1" else 0), 0.3 + by / EST["rbw"])}))
+        add(kind="send", r=a[1], w=[], d=d, out=out, a=a, sem=sem, via=via, slot=slot,
+            cost={"g": lambda est: (est["riss"] + (est["first"] if sem == "an" else 0), 0.3 + by / est["rbw"] / (1 if via is None else 2))})
+        ops.append(dict(kind="land", r=[], w=out[1], d=d, sem=sem, via=via, cost={"-": lambda est: (0.0, by / est["rbw"])}, name="", t=0))
 
-    def lands(d, out, sem, via=None):
-        ops.append(dict(kind="land", r=[], w=out[1], d=d, sem=sem, via=via, cost={"-": (0.0, 0.0)}))
-
-    def LD(t, h, m):
-        a = (2 * (t - 2) + h) * LW + H * m
-        return V("land", a, a + H)
+    def LD(t, h):
+        return (2 * (t - 2) + h) * LW
 
     def col(i):
         return V("col", i, i + 1)
 
-    PT, DS, HP, HN, A15 = 0, 1, 2, 3, 4
-    IDB, NID, P2, N2, BIG = 0, 128, 256, 512, 768
+    def eq(i):
+        return V("eq", i, i + 1)
+
+    DH, DL, QJ, QL = 0, 4, 8, 12
+    PL, PH, PJ, PI = 1, 5, 9, 13
+
+    def TG(t):
+        return 4 * t - 2
+
+    PT, DS, HP, HN, A15, PQ, S0, NG, PB = 0, 1, 2, 3, 4, 5, 6, 6, 9
+    IDB, NID, P2, N2, BIG = 0, 128, 384, 640, 896
 
     def mat(m):
         return V("idb", m, m + 128)
@@ -326,73 +358,87 @@ def rank_program(g, core, T, topo):
     def turn(o):
         return V("idf", o, o + 128)
 
-    for t in range(1, NT + 1):
-        n0 = 128 * (t - 1)
-        if t == 1:
-            lands(1, V("nin", 0, 128), "an1")
-            lands(1, V("pool", SL(1), SL(1) + K), "ar1")
-        else:
-            lands(1, V("nin", n0, n0 + 64), "an%d" % t)
-            lands(1, V("nin", n0 + 64, n0 + 128), "am%d" % t)
-            lands(1, V("ui", n0, n0 + 128), "au%d" % t)
-            for h in range(2):
-                for m in range(2):
-                    lands(1, LD(t, h, m), "l%d%d%d" % (t, h, m), h)
-        if t < NT:
-            lands(t, V("fin", n0, n0 + 128), "af%d" % t)
-            lands(-t, V("ein", n0, n0 + 128), "ae%d" % t)
-
+    at("load", 0)
     dma("s", [(V("nmi", 0, 64), X("nm", 0, 128, 0, 64)), (V("nmi", 64, 128, p=(SH, 128)), X("nm", 0, 128 - SH, 64, 128)),
               (V("nmi", 64, 128, p=(0, SH)), X("nm", 128 - SH, 128, 64, 128))], 64)
-    dma("a", [(V("t320", 0, 160), X("dn", 0, 8, 0, W))], 80)
-    dma("s", [(V("rout", 0, H), X("rc", 0, 128, 0, H)), (V("rout", H, K, p=(SH, 128)), X("rc", 0, 128 - SH, H, K)),
-              (V("rout", H, K, p=(0, SH)), X("rc", 128 - SH, 128, H, K))], 512)
-    dma("a", [(V("pli", p=(0, 8)), X("pl", 0, 8, 0, 128))], 4)
+    dma("a", [(V("dni"), X("dn", 0, 8, 0, W))], 80)
+    dma("a", [(V("pli", p=(0, 8)), X("pl", 0, 8, 0, 128))], 20)
+    dma("a", [(V("rout", 0, H), X("rc", 0, 128, 0, H))], 256)
     dma("s", [(V("pool", W0, W0 + W), X("wl", 0, 128, 0, W))], 640)
+    dma("a", [(V("rout", H, K, p=(SH, 128)), X("rc", 0, 128 - SH, H, K)), (V("rout", H, K, p=(0, SH)), X("rc", 128 - SH, 128, H, K))], 256)
 
-    iota(V("pci", 0, 1), [[0, 1]], 1, False)
-    iota(V("xi"), [[1, 160]], -1)
+    at("early", 0)
+    iota(V("pci", 0, 1), [[0, 1]], 1)
+    iota(V("mt"), [[1, 256]], 0)
+    fill(V("tab", 0, W), 0.0)
+    ts(V("pci", 4, 5), V("pci", 0, 1), 15, ALU.bitwise_and)
+    ts(V("pci", 5, 6), V("pci", 0, 1), 2, ALU.arith_shift_right, 3, ALU.bitwise_and)
+    cp(V("col", 1, 3), V("pci", 4, 6))
+    lin(V("it"), V("mt", 0, 160), 0.0, col(1))
+    rows("tab", 0, W, [(PI, V("it")), (PL, V("mt", 0, 160))])
+    lin(V("i4", 0, 256), V("mt"), 0.0, col(2))
+    ts(V("eq", 0, 16), V("mt", 0, 16), col(1), ALU.is_equal)
+    i4, m4 = [V("i4", 256 * u, 256 * u + 256, p=(0, 128, 4)) for u in range(3)], V("mt", p=(0, 128, 4))
+    lin(col(20), eq(PH), float(BX(1) // 128), eq(TG(1)))
+    fill(V("tab", W, W + H), 0.0)
+    lin(V("c0", 0, H), V("tab", W, W + H), 0.0, col(20))
+    lin(V("i4", 256, 512), V("i4", 0, 256), 1.0, float(W // 256))
+    cp(V("nl", 0, 128), V("nmi"))
+    ORDER["first"] = len(ops) - 1
+    rows("c0", 0, H, [(PJ, i4[0]), (PL, m4), (QJ, i4[1]), (QL, m4)])
+    lin(V("i4", 512, 768), V("i4", 0, 256), 1.0, float(H // 256))
+    lin(V("c0", H, K), V("tab", W, W + H), 0.0, col(20))
+    rows("c0", H, K, [(PJ, i4[2]), (PL, m4)])
+    at("set", 0)
+    iota(V("ph"), [[K // 128, NT - 1], [0, 128]], 0, BX(2) // 128)
+    iota(V("xi"), [[1, 144]], -1)
     iota(V("xw"), [[0, 2], [1, 128]], -1)
     iota(V("xb"), [[16, 8], [0, 16]], -1)
     iota(V("xf", p=(0, 8)), [[0, 2], [1, 8], [0, 16]], -1)
-    fill(V("tab"), 0.0)
-    ts(V("pci", 4, 5), V("pci", 0, 1), 15, ALU.bitwise_and)
-    cp(col(0), V("pci", 0, 1))
-    cp(col(1), V("pci", 4, 5))
-    ts(col(2), col(1), 160.0, ALU.mult, col(0), ALU.add)
-    ts(V("t320", 160, 320), V("xi"), col(2), ALU.add)
-    cp(V("nout", 0, 128), V("nmi"))
-    send(1, V("nin", 0, 128), V("nout", 0, 128), "an1")
-    send(1, V("pool", SL(1), SL(1) + K), V("rout", 0, K), "ar1")
-    ts(V("t640", 0, 320), V("t320"), 7, ALU.arith_shift_right)
-    ts(V("t640", 320, 640), V("t320"), 127, ALU.bitwise_and)
-    cp(V("zb", 0, 320), V("t640", 0, 320))
-    cp(V("zb", 320, 640), V("t640", 320, 640))
-    dma("s", [(V("tab", p=(r, 128, 16)), V("zb", c, c + 160)) for r, c in ((0, 0), (8, 160), (4, 320), (12, 480))], 100)
-    fill(V("c0"), 0.0)
-    lin(V("zc", 0, 128), V("xi", 0, 128), 0.0, col(1))
-    lin(V("zc", 128, 256), V("xi", 0, 128), 1.0, col(0))
-    dma("s", [(V("c0", p=(r, 128, 16)), V("zc", c, c + 128)) for r, c in ((8, 0), (12, 128))], 64)
-    ts(col(3), col(1), 8.0, ALU.is_lt)
-    ts(col(4), col(1), 8.0, ALU.is_equal)
-    for t in range(1, NT + 1):
-        lin(col(19 + t), col(4), float(BX(t) // 128), 0.0)
+    act(V("one"), V("mt", 0, 128), FN.Exp, scale=0.0)
+    ops[-1]["cost"] = {"a": lambda est: (1.5, 0.0)}
+    at("first", 0)
+    send(1, V("ui", 0, 128), V("nl", 0, 128), "an")
+    cp(V("zb", 0, 160), V("dni"))
+    tt(V("zb", 160, 320), V("dni"), V("zb", 0, 160), ALU.subtract)
+    send(-1, V("zi"), V("zb"), "ad")
+    for h in range(2):
+        send(1, V("pool", RP(h), RP(h) + H), V("rout", H * h, H * h + H), "ar%d" % h)
+        if h in OPT["hold"]:
+            ops[-2]["r"] = ops[-2]["r"] + V("zi")[1]
+    at("far", 0)
+    s2 = 2 * SH % 128
+    dma("s", [(V("rb2", p=(s2, 128)), X("rc", 0, 128 - s2, H, K)), (V("rb2", p=(0, s2)), X("rc", 128 - s2, 128, H, K))], 256)
+    for h in range(2):
+        send(2, V("land", LD(2, h) + 16, LD(2, h) + 16 + H), V("rb2") if h else V("rout", 0, H), "l2%d0" % h, h, 0)
+    at("set", 0)
+    count["set", 0] = 5
+    cp(V("eo", 129, 384, 2), V("nmi"))
+    SG = 256 if OPT["sg"] == 1 else -128
+    UO = 256 if OPT["ur"] == 1 else 0
     lin(col(5), col(1), -1.0, 15.0)
-    lin(col(6), col(4), 128.0, 0.0)
-    ts(col(7), col(1), 12.0, ALU.is_equal, col(6), ALU.add)
-    ts(col(8), col(1), 0.0, ALU.is_equal, 128.0, ALU.mult)
-    ts(col(9), col(1), 4.0, ALU.is_equal, col(8), ALU.add)
-    ts(col(10), col(1), 15.0, ALU.is_lt, 0.5, ALU.mult)
-    ts(col(11), col(1), 15.0, ALU.is_equal, 16.0, ALU.mult)
-    lin(col(12), col(1), -1.0, 0.0)
-    lin(col(13), col(0), 16.0, col(1))
-    for s, c in ((PT, 7), (DS, 9), (HP, 10), (A15, 11)):
-        ts(V("sel", 144 * s, 144 * s + 144), V("xi", 0, 144), col(5), ALU.is_equal, col(c), ALU.mult)
+    ts(V("sel", 144 * S0, 144 * S0 + 144), V("xi"), col(5), ALU.is_equal)
+    lin(col(3), eq(DH), 1.0, eq(DL))
+    lin(col(4), eq(PH), 128.0, eq(PL))
+    lin(col(6), eq(PJ), 256.0, col(4))
+    lin(col(7), eq(PI), 160.0, col(6))
+    lin(col(10), eq(15), -0.5, 0.5)
+    lin(col(11), eq(15), 0.5, -0.5)
+    lin(col(12), eq(15), 16.0, 0.0)
+    lin(col(18), eq(QJ), 256.0, eq(QL))
+    lin(V("eq", 16, 32), V("eq", 0, 16), -1.0, 0.0)
+    for t in range(2, NT + 1):
+        lin(col(20 + t), eq(TG(t)), -float(H + BX(t)), col(7))
+    for s, c in ([(PT, col(7)), (DS, col(3)), (HP, col(10)), (HN, col(11)), (A15, col(12)), (PQ, col(18))]
+                 + [(NG + t, eq(16 + TG(t))) for t in range(1, NT + 1)] + [(PB + t, col(20 + t)) for t in range(2, NT + 1)]):
+        lin(V("sel", 144 * s, 144 * s + 144), V("sel", 144 * S0, 144 * S0 + 144), c, 0.0)
+    lin(col(15), col(1), -1.0, 0.0)
+    lin(col(16), col(1), 1.0, 16.0)
+    lin(col(17), col(1), 1.0, 16.0 - H)
     ts(V("idf"), V("xw"), 0.0, ALU.is_equal)
     ts(V("wf", p=(0, 8)), V("xf", p=(0, 8)), 0.0, ALU.is_equal)
-    cp(V("plf", p=(0, 8)), V("pli", p=(0, 8)))
-    lin(V("sel", 144 * HN, 144 * HN + 144), V("sel", 144 * HP, 144 * HP + 144), -1.0, 0.0)
-    for m, w, c in ((IDB, 128, 1.0), (NID, 128, -1.0), (BIG, 128, 4096.0), (P2, 256, 2.0), (N2, 256, -2.0)):
+    ts(V("plf", p=(0, 8)), V("pli", p=(0, 8)), 1.0 / 128, ALU.max)
+    for m, w, c in ((IDB, 128, 1.0), (NID, 256, -1.0), (BIG, 128, 4096.0), (P2, 256, 2.0), (N2, 256, -2.0)):
         lin(V("idb", m, m + w), V("idf", 0, w), c, 0.0)
     for t in range(1, NT + 1):
         o = (-SH * t) % 128
@@ -401,164 +447,222 @@ def rank_program(g, core, T, topo):
     cp(V("fout"), V("pn"), True)
     for t in range(1, NT):
         send(t, V("fin", 128 * (t - 1), 128 * t), V("fout", 128 * (t - 1), 128 * t), "af%d" % t)
-    ts(V("blk"), V("xb"), col(12), ALU.is_equal)
-    lin(V("jj"), V("xi", 0, 128), 16.0, col(13))
-    for t in range(1, NT + 1):
-        fill(V("pool", SL(t) + ZZ, SL(t) + SLOT), 0.0)
-    for u in range(6):
-        fill(V("land", LW * u + K, LW * u + LW), 0.0)
+    ts(V("blk"), V("xb"), col(15), ALU.is_equal)
+    lin(V("c16"), V("mt", 0, 64), 16.0, 0.0)
+    lin(V("cc"), V("mt", 0, 64), 1.0 / 64, 1.0)
     for h in range(2):
-        for u, (a, b) in enumerate(((1.0, -H), (-1.0, K), (1.0, 0))):
-            lin(V("dq", 192 * h + u, 192 * h + 192, 3), V("jj", 64 * h, 64 * h + 64), a, float(b - a * H * h))
-    fill(V("ab", K, K + 16), 16384.0)
-    fill(V("ab", 2 * K + 16, 2 * K + 32), 16384.0)
+        fill(V("pool", ZP(h), ZP(h) + 16), 0.0)
+    for u in range(6):
+        fill(V("land", LW * u, LW * u + 16), 0.0)
+    fill(V("c64"), 1.0 / 64)
+    for u in range(4):
+        fill(V("ab", (H + 16) * u + H, (H + 16) * (u + 1)), 16384.0)
     fill(V("n0"), 0.0)
-    fill(V("d0"), 0.0)
-    lin(V("dr", 1, 384, 3), V("jj"), -1.0, float(ZZ))
-    lin(V("dr", 2, 384, 3), V("jj"), 1.0, 0.0)
-    lin(V("dr", 192, 384, 3), V("jj", 64, 128), 1.0, float(H - ZZ))
-    lin(V("dv", 0, 384, 3), V("jj"), -1.0, float(ZZ))
-    lin(V("dv", 193, 384, 3), V("jj", 64, 128), 0.0, -float(H))
-    lin(V("dv", 194, 384, 3), V("jj", 64, 128), 1.0, float(H))
+    fill(V("mk"), 1.0)
+    fill(V("mk", 0, 512, 16), 0.0)
+    at("dnt", 0)
+    dma("s", [(V("dnt", a, min(a + H, W)), V("tab", W, min(W + H, 2 * W - a))) for a in range(0, W, H)], 640)
+    rows("dnt", 0, W, [(DH, V("zi", 0, 160)), (DL, V("zi", 160, 320))])
 
-    tab = V("tab")
+    tab = V("tab", 0, W)
 
-    def ypos(t, h):
-        return W0 + BX(t) if h == 0 else SL(t) + K
-
-    for t in range(1, NT + 1):
-        last = t == NT
-        n0 = 128 * (t - 1)
-        pull = V("fout", 384, 512) if last else V("fin", n0, n0 + 128)
-        old = V("pool", SL(t), W0 + BX(t))
-        if t > 1:
-            for h in range(2):
-                a = (2 * (t - 2) + h) * LW
-                gather("pool", SL(t) + H * h, V("land", a, a + LW), "ui", n0 + 64 * h, H)
-        if not last:
-            for h in range(2):
-                send(1, LD(t + 1, h, 0), V("pool", SL(t) + H * h, SL(t) + H * h + H), "l%d%d0" % (t + 1, h), h, 2 * t - 2)
+    def index(t):
+        last, n0, e0, u0 = t == NT, 128 * (t - 1), 512 * t - 384, 384 * (t - 1)
         for h in range(2):
-            c, a = 64 * h, H * h
-            gather("gg", a, tab, "nin", n0 + c, H)
-            if t > 1 or h:
-                mm(wrap(V("pa", c, c + 64), PT, "gg", a, H))
-                cp(V("pu", c, c + 64), V("pa", c, c + 64))
-            lin(V("src", a, a + H), V("gg", a, a + H), col(3), col(19 + t))
-            tt(IND(tab, V("nin", n0 + c, n0 + c + 64)), V("src", a, a + H), V("c0", a, a + H), ALU.add)
-            if not last:
-                mm(wrap(V("pb", c, c + 64), DS, "gg", a, H))
-                cp(V("du", c, c + 64), V("pb", c, c + 64))
-            if t == 1:
-                gather("pool", ypos(t, h), V("pool", W0, W0 + W), "nin", c, H)
-            else:
-                gather("pool", ypos(t, h), V("pool", W0, W0 + BX(t) + a), "pu", c, H)
-        lf = V("n1", 1, 256, 2)
-        if not last:
-            cp(lf, V("nin", n0, n0 + 128))
-            tt(V("dl"), V("pb", 0, 128), lf, ALU.subtract)
-        u1 = V("pa", 0, 64) if t > 1 else V("n1", 1, 128, 2)
-        if last:
-            lin(V("dr", 0, 192, 3), u1, 1.0, float(W0 - SL(t) - ZZ))
-        else:
-            for h in range(2):
-                send(1, LD(t + 1, h, 1), V("pool", ypos(t, h), ypos(t, h) + H), "l%d%d1" % (t + 1, h), h, 2 * t - 1)
-        lin(V("dv", 2, 192, 3), u1, 1.0, float(W0 - SL(t)))
-        tt(V("dv", 1, 192, 3), V("jj", 0, 64), V("dv", 2, 192, 3), ALU.subtract)
-        bb = V("pc", 0, 128)
-        a0, x0 = (K + 16) * (t % 2), K * (t % 2)
-        for h in range(2):
-            for q in range(2):
-                a = H * h + 512 * q
-                pd = V("pd", 512 * q, 512 * q + 512)
-                mm([(pd, mat(IDB), V("pool", SL(t) + a, SL(t) + a + 512)), (pd, mat(NID), V("pool", ypos(t, h) + 512 * q, ypos(t, h) + 512 * q + 512))])
-                act(V("ab", a0 + a, a0 + a + 512), pd, FN.Abs)
-            out = V("pc", 64 * h, 64 * h + 64)
+            c, a, s = 64 * h, H * h, "AB"[h]
+            if t > 1:
+                at("gg" + s, t)
+                gather("gg", a, tab, "nl", n0 + c, H)
+                at("pu" + s, t)
+                p = V("pa", c, c + 64)
+                mm(wrap(p, (PT, PB + t)[h], "gg", a, H))
+                ts(V("uo", u0 + 128 + c, u0 + 192 + c), p, float(H * h), ALU.add)
+                lo, hi = u0 + 128 + c, u0 + 192 + c
+                if OPT["ur"] == h:
+                    lo, hi = min(lo, u0 + UO), max(hi, u0 + UO + 128)
+                send(1, V("ui", lo, hi), V("uo", lo, hi), ("pa%d", "pb%d")[h] % t)
+            elif h:
+                at("ggB", t)
+                gather("hh", 0, tab, "nl", 64, H)
             if h:
-                mm(wrap(V("pb", 384, 512), A15, "pool", SL(t), K))
-                mm(wrap(V("pc", 0, 64), HP, "pool", SL(t), H) + wrap(out, HP, "pool", SL(t) + H, H), "b%d" % t, bb)
-            mm(wrap(out, HP, "pool", ypos(t, h), H), "b%d" % t, bb)
-            mm(wrap(V("pb", 256 + 64 * h, 320 + 64 * h), A15, "pool", ypos(t, h), H))
-            mm(wrap(out, HN, "ab", a0 + H * h, H), "b%d" % t, bb)
-        cp(V("lr"), V("pb", 384, 512), True)
-        ly = V("pb", 256, 384)
-        tt(V("la"), ly, V("lr"), ALU.min)
-        tt(V("d0", 1, 384, 3), ly, V("lr"), ALU.is_le)
-        ts(V("bond"), bb, 0.0, ALU.is_gt, alt=(FN.Sign, 1.0, 0.0))
-        mm([(V("pb", 128, 256), V("blk"), V("bond"))])
-        tt(V("ww"), bb, V("la"), ALU.min)
-        tt(V("pv", 0, 128), V("pb", 128, 256), V("ww"), ALU.mult)
-        tt(V("pv", 128, 256), V("pv", 0, 128), pull, ALU.is_lt)
-        tt(V("nh"), V("pv", 128, 256), V("bond"), ALU.is_ge)
-        tt(V("pv", 256, 384), bb, V("la"), ALU.is_gt)
-        tt(V("s1"), V("pv", 256, 384), V("nh"), ALU.mult)
-        if not last:
-            tt(V("n1", 0, 256, 2), V("nh"), V("dl"), ALU.mult)
-            for h in range(2):
-                c = 64 * h
-                gather("oo", H * h, tab, "du", c, H)
-                mm(wrap(V("pa", 192 + c, 256 + c), PT, "oo", H * h, H))
-                ts(V("n0", 2 * c + 1, 2 * c + 128, 2), V("pa", 192 + c, 256 + c), float(BX(t)), ALU.is_lt)
-                scan(V("ln", 2 * c, 2 * c + 128), V("n0", 2 * c, 2 * c + 128), V("n1", 2 * c, 2 * c + 128))
-                new = V("ln", 2 * c + 1, 2 * c + 128, 2)
-                if h:
-                    mm([(V("pn", 0, 64), turn(128 - SH), new)])
-                    new = V("pn", 0, 64)
-                out = V("nout", 128 * t + c, 128 * t + c + 64)
-                cp(out, new)
-                send(1, V("nin", 128 * t + c, 128 * t + c + 64), out, ("an%d", "am%d")[h] % (t + 1))
-        gather("hh", 0, tab, "nin", n0, H)
-        mm(wrap(V("pa", 128, 192), PT, "hh", 0, H))
-        ts(V("pv", 384, 448), V("pa", 128, 192), float(BX(t) + H), ALU.is_lt)
-        ts(V("pv", 448, 512), V("pu", 64, 128), float(BX(t)), ALU.is_lt)
-        tt(V("d0", 2, 384, 3), V("pv", 384, 512), V("s1"), ALU.mult)
-        scan(V("sr"), V("d0"), V("dr" if last else "dq"))
+                at("lb", t)
+                q = V("pb", 256, 320)
+                mm(wrap(q, PQ, "gg" if t > 1 else "hh", a if t > 1 else 0, H))
+                tt(V("lq"), q, V("eo", e0 + 129, e0 + 256, 2), ALU.max)
+                cp(V("lb"), V("lq"))
+                ts(V("eo", e0 + SG + 64, e0 + SG + 128), q, 1.0, ALU.is_lt, alt=(FN.Relu, -1.0, 1.0))
+            for q in range(0, H, OPT["sc"]):
+                e = q + OPT["sc"]
+                mark = IND(V("tab"), V("lb", q // 16, e // 16)) if h else IND(tab, V("nl", n0 + q // 16, n0 + e // 16))
+                if h or t == 1 or last:
+                    at("mark" + s, t)
+                    cp(mark, V("c0", a + q, a + e))
+                else:
+                    at("src", t)
+                    lin(V("src", q, e), V("gg", q, e), col(3), 0.0)
+                    at("markA", t)
+                    tt(mark, V("src", q, e), V("c0", q, e), ALU.add)
+        at("sgA", t)
+        mm(wrap(V("pa", 128, 192), NG + t, "tab", W, H))
+        lin(V("eo", e0 + SG, e0 + SG + 64), V("pa", 128, 192), 1.0, 1.0)
+        if last or OPT["sg"] == 2:
+            send(1, V("en", e0 + SG, e0 + SG + 128), V("eo", e0 + SG, e0 + SG + 128), "sg%d" % t)
         if last:
-            cp(V("ur", 0, 128), V("sr", 2, 384, 3))
-            gather("rout", K, old, "ur", 0, K)
+            at("fin", t)
+            mm(wrap(V("pa", 192, 352), PT, "tab", 0, W))
+            cp(V("uo", 1536, 1696), V("pa", 192, 352))
+            send(1, V("ui", 1536, 1696), V("uo", 1536, 1696), "aw")
+            return
+        for h in range(2):
+            c, a, s = 64 * h, H * h, "AB"[h]
+            if t == 1:
+                at("dn" + s, t)
+                gather("gg", a, V("dnt", 0, W), "nl", c, H)
+            at("du" + s, t)
+            mm(wrap(V("pb", c, c + 64), DS, "gg", a, H))
+            cp(V("du", c, c + 64), V("pb", c, c + 64))
+            tt(V("dl", c, c + 64), V("pb", c, c + 64), V("eo", e0 + 2 * c + 1, e0 + 2 * c + 128, 2), ALU.subtract)
+            at("oo" + s, t)
+            gather("oo", a, tab, "du", c, H)
+            at("e" + s, t)
+            free = V("pb", 128 + c, 192 + c)
+            mm([(free, mat(IDB), V("one", 0, 64))] + wrap(free, NG + t, "oo", a, H))
+            tt(V("eo", e0 + 2 * c, e0 + 2 * c + 128, 2), free, V("dl", c, c + 64), ALU.mult)
+            lo, hi = e0 + 2 * c, e0 + 2 * c + 128
+            if OPT["sg"] == h:
+                lo, hi = min(lo, e0 + SG), max(hi, e0 + SG + 128)
+            send(1, V("en", lo, hi), V("eo", lo, hi), ("na%d", "nb%d")[h] % t)
+        at("back", t)
+        rows("c0", 0, K, [(PH, V("ph", 128 * t - 128, 128 * t)), (TG(t + 1), V("one"))])
+        dma("s", [(V("tab", 0, W, p=(0, 128, 4)), V("dnt", p=(0, 128, 4)))], 330)
+
+    def record(t):
+        last, n0, e0, u0 = t == NT, 128 * (t - 1), 512 * t - 384, 384 * (t - 1)
+        x0 = K * (t % 2)
+        for h in range(2):
+            c, R, Y, s = 64 * h, RP(h), YP(h), "AB"[h]
+            a0 = (H + 16) * (2 * (t % 2) + h)
+            pull = V("fout", 384 + c, 448 + c) if last else V("fin", n0 + c, n0 + c + 64)
+            if t > 1:
+                at("R" + s, t)
+                gather("pool", R, V("land", LD(t, h), LD(t, h) + LW), "ui", u0 + UO + c, H, OPT["rch"])
+            at("y" + s, t)
+            gather("pool", Y, V("pool", W0 - (H * h if t > 1 else 0), W0 + BX(t)), "ui", u0 + c + (128 if t > 1 else 0), H)
+            if not last:
+                at("on" + s, t)
+                for m in range(1 if t == 1 else 0, 2):
+                    a = LD(t + 1, h) + 16 + H * m
+                    send(1, V("land", a, a + H), V("pool", R + H * m, R + H * m + H), "l%d%d%d" % (t + 1, h, m), h if h or m else None, 2 * t - 2 + m)
+            at("abs" + s, t)
+            for q in range(2):
+                pd = V("pd", 512 * q, 512 * q + 512)
+                mm([(pd, mat(IDB), V("pool", R + 512 * q, R + 512 * q + 512)), (pd, mat(NID), V("pool", Y + 512 * q, Y + 512 * q + 512))])
+                act(V("ab", a0 + 512 * q, a0 + 512 * q + 512), pd, FN.Abs)
+            bb, nn, pv, gt, dd, nw = [V("pc", 512 * h + 64 * u, 512 * h + 64 * u + 64) for u in range(6)]
+            ly, lr = V("pe", 128 + c, 192 + c), V("pe", 256 + c, 320 + c)
+            lr_, la, ww, bond = [V(u, c, c + 64) for u in ("lr", "la", "ww", "bond")]
+            nh = V("n0", 2 * c + 1, 2 * c + 128, 2)
+            at("la" + s, t)
+            mm(wrap(lr, A15, "pool", R, H))
+            mm([(ly, mat(IDB), V("c64"))] + wrap(ly, A15, "pool", Y, H))
+            lin(lr_, lr, 1.0, 1.0 / 64)
+            tt(la, ly, lr_, ALU.min)
+            tt(dd, ly, lr_, ALU.is_le)
+            at("b" + s, t)
+            for w, buf, a in ((HP, "pool", R), (HP, "pool", Y), (HN, "ab", a0)):
+                mm(wrap(bb, w, buf, a, H), "b%d%d" % (t, h), (nn, nw))
+            at("hold" + s, t)
+            ts(bond, bb, 0.0, ALU.is_gt, alt=(FN.Sign, 1.0, 0.0))
+            mm([(nn, V("blk"), bond)])
+            tt(ww, bb, la, ALU.min)
+            tt(pv, nn, ww, ALU.mult)
+            tt(nh, pv, pull, ALU.is_lt)
+            if not last:
+                at("name" + s, t)
+                e1 = e0 + 512 + 2 * c
+                new = V("ln") if h else V("eo", e1, e1 + 128)
+                scan(new, V("n0", 2 * c, 2 * c + 128), V("en", e0 + 2 * c, e0 + 2 * c + 128))
+                if h:
+                    mm([(nw, turn(128 - SH), V("ln", 1, 128, 2))])
+                    cp(V("nl", n0 + 192, n0 + 256), nw)
+                    cp(V("eo", e1 + 1, e1 + 128, 2), nw, True)
+                else:
+                    cp(V("nl", n0 + 128, n0 + 192), V("eo", e1 + 1, e1 + 128, 2))
+            at("swap" + s, t)
+            sw, sd = V("sw", c, c + 64), V("sd", c, c + 64)
+            tt(gt, bb, la, ALU.is_gt)
+            tt(gt, gt, V("en", e0 + SG + c, e0 + SG + 64 + c), ALU.mult)
+            tt(sw, gt, nh, ALU.mult)
+            tt(sd, dd, sw, ALU.mult)
+            o = 0 if last else (128 - SH) * h
+            u, v, x = [V("pn", 128 * k + c, 128 * k + c + 64) for k in range(3)]
+            at("ur" + s, t)
+            mm([(u, mat(IDB), V("cc")), (u, mat(NID + o), sw), (u, mat(P2 + o), sd)])
+            lo = u0 + 384 + c
+            ts(V("ur", c, c + 64) if last else V("uo", lo, lo + 64), u, float(H), ALU.mult, col(17), ALU.add)
+            if not last:
+                send(1, V("ui", lo, lo + 64), V("uo", lo, lo + 64), ("au%d", "av%d")[h] % t)
+            at("uv" + s, t)
+            mm([(v, mat(IDB), V("cc")), (v, mat(NID), sw), (v, mat(NID), sd)])
+            ts(V("uv", c, c + 64), v, float(H), ALU.mult, col(16), ALU.add)
+            old = V("pool", ZP(h), ZP(h) + LW)
+            ch = OPT["ch"] if last else OPT["big"]
+            at("X" + s, t)
+            gather("pool", W0 + BX(t) + H * h, old, "uv", c, H, ch)
+            if last:
+                at("Z" + s, t)
+                gather("rout", K + H * h, old, "ur", c, H, ch)
+            at("ux" + s, t)
+            mm([(x, mat(IDB), V("c16")), (x, mat(BIG), nh)])
+            ts(V("ux", c, c + 64), x, col(1), ALU.add, float(H), ALU.min)
+            at("exp" + s, t)
+            ch = OPT["ch"] if last or h else OPT["big"]
+            for q in range(0, H, ch):
+                act(V("xx", x0 + H * h + q, x0 + H * h + q + ch), IND(V("ab", a0, a0 + H + 16), V("ux", c + q // 16, c + (q + ch) // 16)), FN.Exp, scale=-1.0 / 64)
+        for h in range(2):
+            at("sum" + "AB"[h], t)
+            out, o, a = V("pe", 64 * h, 64 * h + 64), turn((SH * t * h) % 128), x0 + H * h
+            if not last:
+                for q in range(0, H, 512):
+                    scan(V("xs", H * h + q, H * h + q + 512), V("mk"), V("xx", a + q, a + q + 512))
+                cp(V("eout", n0 + 64 * h, n0 + 64 * h + 64), V("xs", H * h + 15, H * h + H, 16), True)
+            else:
+                if OPT["ls"][h]:
+                    for q in range(0, H, 512):
+                        scan(V("xs", H * h + q, H * h + q + 512), V("mk"), V("xx", a + q, a + q + 512))
+                    mm([(out, o, V("xs", H * h + 15, H * h + H, 16))], "e", [V("pe", 128, 384)])
+                for k in range(0, 16 * (1 - OPT["ls"][h]), 2):
+                    mm([(out, o, V("xx", a + k + u, a + H, 16)) for u in range(2)], "e", [V("pe", 128, 384)])
+                at("old" + "AB"[h], t)
+                mm([(out, turn((SH * u * h) % 128), V("ein", 128 * u + 64 * h - 128, 128 * u + 64 * h - 64)) for u in range(1, NT)], "e", [V("pe", 128, 384)])
+        at("tot", t)
+        if last:
+            cp(V("eout", n0, n0 + 128), V("pe", 0, 128), True)
         else:
-            mm([(V("pn", 256, 320), turn(0), V("sr", 2, 192, 3))])
-            mm([(V("pn", 320, 384), turn(128 - SH), V("sr", 194, 384, 3))])
-            cp(V("ur", n0, n0 + 128), V("pn", 256, 384))
-            send(1, V("ui", n0 + 128, n0 + 256), V("ur", n0, n0 + 128), "au%d" % (t + 1))
-        scan(V("sv"), V("d0"), V("dv"))
-        cp(V("uv"), V("sv", 2, 384, 3))
-        gather("pool", W0 + BX(t), old, "uv", 0, K)
-        mm([(V("pn", 128, 256), turn(0), V("jj")), (V("pn", 128, 256), mat(BIG), V("nh"))])
-        ts(V("ux"), V("pn", 128, 256), float(K), ALU.min)
-        for q in range(4):
-            act(V("xx", x0 + 512 * q, x0 + 512 * q + 512), IND(V("ab", a0, a0 + K + 16), V("ux", 32 * q, 32 * q + 32)), FN.Exp, scale=-1.0 / 64)
-        if not last:
-            for k in range(0, 16, 2):
-                mm([(V("pe", 0, 128), turn(0), V("xx", x0 + k + u, x0 + K, 16)) for u in range(2)], "e%d" % t)
-        else:
-            for h in range(2):
-                out = V("pe", 64 * h, 64 * h + 64)
-                for k in range(0, 16, 4):
-                    mm([(out, turn((SH * t * h) % 128), V("xx", x0 + H * h + k + u, x0 + H * h + H, 16)) for u in range(4)], "e%d" % t)
-                mm([(out, turn((SH * u * h) % 128), V("ein", 128 * u + 64 * h - 128, 128 * u + 64 * h - 64)) for u in range(1, NT)], "e%d" % t)
-        cp(V("eout", n0, n0 + 128), V("pe", 0, 128), True)
-        if not last:
             send(-t, V("ein", n0, n0 + 128), V("eout", n0, n0 + 128), "ae%d" % t)
 
-    t = NT
+    for t in range(1, NT + 1):
+        index(t)
+        record(t)
+
     dma("s", [(X("ye", 0, 128, 0, 128), V("eout", 384, 512))], 64)
-    mm(wrap(V("pb", 0, 160), PT, "tab", 0, W))
-    cp(V("pu"), V("pb", 0, 160))
     for q in range(2):
+        at("wall", NT)
         for u in range(4):
-            gather("wout", 640 * u + 320 * q, V("pool", W0, NP), "pu", 40 * u + 20 * q, 320)
+            gather("wout", 640 * u + 320 * q, V("pool", W0, NP), "ui", 1536 + 40 * u + 20 * q, 320)
+        at("yw", NT)
         out = V("pd", 512 * q, 512 * q + 320)
         mm([(out, mat(m), V("wout", 640 * u + 320 * q, 640 * u + 320 * q + 320)) for u, m in enumerate((IDB, NID, P2, N2))])
         cp(V("ow", 320 * q, 320 * q + 320), out, True)
         dma("s", [(X("yw", 0, 128, 320 * q, 320 * q + 320), V("ow", 320 * q, 320 * q + 320))], 160)
+    at("yr", NT)
     o = (SH * NT) % 128
-    mm([(V("pc"), mat(m), V("rout", K + 512 * u, K + 512 * u + 512)) for u, m in enumerate((IDB, NID, P2 + o, N2 + o))])
-    cp(V("orr"), V("pc"), True)
+    mm([(V("pb"), mat(m), V("rout", K + 512 * u, K + 512 * u + 512)) for u, m in enumerate((IDB, NID, P2 + o, N2 + o))])
+    cp(V("orr"), V("pb"), True)
     dma("s", [(X("yr", 0, 128, 0, 512), V("orr"))], 256)
 
-    if SEED[0] not in ORDER:
-        ORDER[SEED[0]] = arrange(ops, SEED[0])
+    if "order" not in ORDER:
+        ORDER["order"] = arrange(ops)
     clock = {e: {} for e in Q}
     total, hist, bank, ndma = {}, {}, {}, 0
 
@@ -580,23 +684,24 @@ def rank_program(g, core, T, topo):
 
     nxt = T.cores[(rank + 1) % n]
     spare = [k for k in topo.engines(T.cores[rank], helper(rank, 0)) if k not in topo.engines(T.cores[rank], nxt)]
-    for i, e in ORDER[SEED[0]][0]:
+    for i, e in ORDER["order"]:
         o = ops[i]
         if role is not None:
             if o["kind"] == "send" and o["via"] == role:
-                a, q = H * o["slot"], "g"
+                a, b = H * o["slot"], H * o["slot"] + o["a"][2]
                 tok = token("-", "h%d" % o["slot"], len(spare))
-                if role:
+                lay, nxt = role and o["d"] == 1, T.cores[(rank + o["d"]) % n]
+                if lay:
                     wait("s", tok)
-                    g.sync.dma_start(T.hq[SH:128, a:a + H], T.hop[0:128 - SH, a:a + H]).then_inc(T.sem["d%d" % ndma], 16)
-                    g.sync.dma_start(T.hq[0:SH, a:a + H], T.hop[128 - SH:128, a:a + H]).then_inc(T.sem["d%d" % ndma], 16)
+                    g.sync.dma_start(T.hq[SH:128, a:b], T.hop[0:128 - SH, a:b]).then_inc(T.sem["d%d" % ndma], 16)
+                    g.sync.dma_start(T.hq[0:SH, a:b], T.hop[128 - SH:128, a:b]).then_inc(T.sem["d%d" % ndma], 16)
                     tok = token("s", "d%d" % ndma, 32)
                     ndma += 1
                 wait("g", tok)
-                write(nxt, o["out"][0], T["hq" if role else "hop"][:, a:a + H], o["sem"], "sent", topo.engines(core, nxt))
+                write(nxt, o["out"][0], T["hq" if lay else "hop"][:, a:b], o["sem"], "sent", topo.engines(core, nxt))
             continue
         if o["kind"] == "land":
-            src = T.cores[(rank - o["d"]) % n] if o["via"] is None else helper(rank - 1, o["via"])
+            src = T.cores[(rank - o["d"]) % n] if o["via"] is None else helper(rank - o["d"], o["via"])
             tok = token(e, o["sem"], len(topo.engines(src, core)))
             note(hist, tok, [], o["w"])
             continue
@@ -612,10 +717,13 @@ def rank_program(g, core, T, topo):
         if o["kind"] == "send":
             if o["via"] is None:
                 dst = T.cores[(rank + o["d"]) % n]
-                write(dst, o["out"][0], o["a"][0], o["sem"], "sent", topo.engines(core, dst))
+                again = o["a"][1][0][0] == "pool"
+                tok = write(dst, o["out"][0], o["a"][0], o["sem"], "o0%d" % o["slot"] if again else "sent", topo.engines(core, dst))
+                if again:
+                    note(hist, tok, o["r"], [])
             else:
                 a = H * o["slot"]
-                tok = write(helper(rank, o["via"]), T.hop[:, a:a + H], o["a"][0], "h%d" % o["slot"], "o%d%d" % (o["via"], o["slot"]), spare)
+                tok = write(helper(rank, o["via"]), T.hop[:, a:a + o["a"][2]], o["a"][0], "h%d" % o["slot"], "o%d%d" % (o["via"], o["slot"]), spare)
                 note(hist, tok, o["r"], [])
             continue
         if o["kind"] == "dma":

from concourse.mybir import AluOpType, ActivationFunctionType

ALU = AluOpType
FN = ActivationFunctionType
W, K, H, NT, GS = 2560, 2048, 1024, 4, 5
LW = 2 * H + 16
W0 = 2 * LW
NP = W0 + W + NT * K
SH = (16 * GS) % 128
OPT = dict(ch=512, big=1024, sc=1024, on=(2 * H, H), hold=(1,), sg=2, ur=2, rch=1024, ls=(1, 0))


def ZP(h):
    return LW * (1 - h)


def RP(h):
    return ZP(h) + 16


def YP(h):
    return ZP(h) + 16 + H


def BX(t):
    return W + (t - 1) * K


F32, BF, I32, U16 = "float32", "bfloat16", "int32", "uint16"
SCRATCH = {}
for _n, _c, _d in [
        ("pool", NP, BF), ("tab", W + H, BF), ("dnt", W, BF), ("c0", K, BF), ("gg", K, BF), ("src", H, BF), ("hh", H, BF), ("oo", K, BF),
        ("lq", 64, F32), ("lb", 64, U16),
        ("ab", 2 * K + 64, BF), ("xx", 2 * K, F32), ("xs", K, F32), ("mk", 512, BF), ("rout", 2 * K, BF), ("rb2", H, BF), ("wout", W, BF),
        ("land", 6 * LW, BF), ("hop", 6 * H, BF), ("hq", 6 * H, BF),
        ("nmi", 128, I32), ("nl", NT * 128, U16), ("uo", NT * 384 + 160, U16), ("ui", NT * 384 + 160, U16),
        ("eo", NT * 512, F32), ("en", NT * 512, F32), ("ur", 128, U16),
        ("pli", 128, I32), ("plf", 128, F32), ("fout", 512, F32), ("fin", 384, F32), ("eout", 512, F32), ("ein", 384, F32),
        ("dni", 160, I32), ("zb", 320, BF), ("zi", 320, BF), ("mt", 256, BF), ("it", 160, BF), ("i4", 768, BF),
        ("ph", 384, BF), ("one", 128, BF), ("pci", 8, I32), ("col", 32, F32), ("eq", 32, F32),
        ("xi", 144, F32), ("xw", 256, F32), ("xb", 128, F32), ("xf", 256, F32), ("wf", 256, F32), ("idf", 256, F32),
        ("idb", 1024, BF), ("sel", 14 * 144, BF), ("blk", 128, BF), ("bond", 128, BF), ("cc", 64, BF), ("c16", 64, BF), ("c64", 64, BF),
        ("du", 128, U16), ("uv", 128, U16), ("ux", 128, U16), ("sw", 128, BF), ("sd", 128, BF),
        ("ow", 640, F32), ("orr", 512, F32), ("dl", 128, F32), ("lr", 128, F32),
        ("la", 128, F32), ("ww", 128, F32), ("n0", 256, BF), ("ln", 128, F32)]:
    SCRATCH[_n] = ("sbuf", [128, _c], _d)
for _n in ("pd", "pc", "pa", "pb", "pe", "pn"):
    SCRATCH[_n] = ("psum", [128, 1024 if _n in ("pd", "pc") else 512], F32)
NDMA = 36
SEMAPHORES = (["ev", "ea", "ep", "eg", "sent", "an", "ad", "ar0", "ar1", "aw"] + ["d%d" % i for i in range(NDMA)]
              + [a + str(t) for a in ("pa", "pb", "na", "nb", "sg", "au", "av", "af", "ae") for t in range(1, NT + 1)]
              + ["l%d%d%d" % (t, h, m) for t in range(2, NT + 1) for h in range(2) for m in range(2)]
              + ["h%d" % m for m in range(6)] + ["o%d%d" % (h, m) for h in range(2) for m in range(6)])

EST = dict(g=1.45, s=3.1, cyc=0.87e-3, fix=0.055, pcyc=0.59e-3, dfix=1.5, dbw=4.5e5, rbw=1.3e5, rfix=1.5, riss=0.7, first=3.0, wake=0.09)
PERIOD = 17.0
ORDER = {}
ROUND = {w.split(":")[0]: (float(w.split(":")[1][:-1]), w[-1]) for w in """
puA1:-1.99- puA0:-1.61- src0:-1.25v ggA0:-0.85v puA2:-0.22- ggA1:0.36a onA0:0.94- load0:1- src1:1.2- load1:2- markA1:2.33- markA0:2.54- load2:3- yA1:3.95v load3:4- back1:4.01- absA3:4.18- back0:4.35- RA0:4.54- onA1:4.71- yA0:4.8- load4:5- duA2:5.15- duA0:5.65- ggB1:5.66a sgA1:5.91a load5:6- puB1:6.08- laA1:6.13- duA1:6.28- holdA0:6.41a lb2:6.83- lb1:7.16- lb0:7.68- puB2:7.86- ooA1:7.93v ggB0:8.18v dnB0:8.21a laA0:8.32- puB0:8.38- sum8:8.62- absA0:8.75- markB1:8.78- back3:9.08- absA2:9.44- ooA0:10.32v absA1:10.38- eA1:10.78- bA0:10.83- lb3:10.95v duB0:10.99- bA1:11.11- markB0:11.16- dnA1:11.17v laA2:11.24a sum9:11.24- laB0:11.31- uxA1:11.48- yB0:11.67a holdA4:11.71- dnA0:11.71- onB0:11.86- back2:11.89- laA3:11.89- duB1:12.42- RB0:12.68a holdA1:13.05- ZA0:13.15v holdB4:13.44- uxA0:13.5- dnB1:13.53a yw0:13.58- absB3:13.61- holdA2:13.62- holdB1:13.71- sgA0:13.81- yB1:14.19a eA0:14.26- onB1:14.28- ooB0:14.29- absB0:14.33- uvA1:14.41- holdB0:14.71a laB1:14.81- yw4:14.81a sgA2:14.84- laB2:15.03- holdA3:15.17- fin2:15.3- swapA0:15.37- uxB1:15.4- absB2:15.52- bB0:15.7- holdB2:15.92- absB1:16.2- urA1:16.31- yw3:16.54- yr0:16.78- ooB1:16.88v expA0:16.92- urA2:16.94- fin1:16.97- set0:17- set7:17- set9:17.05- set1:17.1- set10:17.1- bB1:17.11- set13:17.12- set14:17.15- set2:17.2- set11:17.2a fin0:17.3- set12:17.3- set15:17.4- laB3:17.41- set18:17.5- ZA1:17.53v laB4:17.55- nameB1:17.59- duB2:17.65- XB0:17.68a eB0:17.74- expA1:18.02- eA2:18.06- swapA2:18.16- swapA3:18.17- holdB3:18.21- urB1:18.32- eB1:18.33- laA4:18.38- wall4:18.5v yw5:18.6- nameA0:18.66- XA0:18.68a uvA0:18.69- uxB0:18.86- set16:19- set17:19.1- swapB0:19.12- set8:19.2- XB1:19.51a nameA1:19.52- nameB2:19.57- swapA1:19.64- urB0:19.76- first3:19.82- swapB3:19.85- nameB0:19.94- swapB1:20.06- urA0:20.15- first1:20.25- first2:20.59- first0:20.62- first4:20.69- first5:20.89- wall5:20.91v first6:21.34- uvB0:21.41- swapB2:21.57- dnt1:21.58- urB2:21.83- yr1:21.87a yr2:22.04- eB2:22.12- XA1:22.16v nameB3:22.39a wall6:22.73v wall0:22.9v uvB1:23.6- yw2:23.75- wall1:23.83v dnt0:24.79- wall3:24.98- wall7:25.18a yw1:25.47v expB0:25.53- ZB0:27.09v ZB1:28.72v expB1:29.35- sum0:30.35- sum6:30.72- wall2:31.32- sum2:32.29- sum1:32.35- sum4:32.43- sum7:33.3- sum3:33.57- sum5:33.92- tot2:34.78- tot0:35.3v tot1:36.72-
""".split()}
ROUND = {w.split(":")[0]: (float(w.split(":")[1][:-1]), w[-1]) for w in """
ggA1:-4.36a ggA0:-4.06a ggA0.4:0.2v src0:0.8v load0:1- load1:1.1- load2:1.2- load3:1.3- puA1:1.4- puA2:1.5- early0:2- early1:2.01- early11:2.1- early3:2.2- early4:2.21- early5:2.22- early9:2.3- early6:2.31a early10:2.32a early12:2.33a early8:2.34a early2:2.4- early14:2.45- first0:2.46- first1:2.46- first2:2.47- early7:2.5- early13:2.6- first3:2.7- first4:2.8- early15:2.9a early16:2.91a early17:2.92v early18:2.93- set54:2.99- load4:3- load5:3.1- dnt0:3.2- puA0:3.23- dnt1:3.3- first5:3.4- set5:3.5- markA0.1:3.6- ggB0.1:3.7v ggB1.1:3.7a lb0.1:3.8- lb1.1:3.81- lb2.1:3.82- markB0.1:3.83- dnA0.1:3.9a dnA1.1:3.91a duA0.1:3.92- duA1.1:3.93- yA0.1:4a yA1.1:4.1a ggB0:4.6v ggB1:4.6a markA0:4.61- duA0:4.84- back0:5- duA1:5.35- duA2:5.5- lb1:5.95- lb2:6.15- yA0.4:6.18v sgA0.4:6.23- puB1:6.45- puB2:6.6- markB0:6.6- lb3:6.7a laA0.4:6.7- RA0:6.8a laA1:6.9- lb0.4:7.14- puB0:7.9- laA0:8.1- sumA4:8.15- laA1.4:8.15- absA0:8.2- yA1:8.24a onA0:8.3- absA1:8.37- absA2.4:8.46- yA0:8.54a lb0:8.55- dnB0:8.6a absA2:8.7- yB0.1:8.85v sgA1:8.93v duB0:9.02- dnB1:9.4a ooA0:9.55v ooA1:9.55a eA1:9.56- laB0:9.6- RB0:9.61a back1:10- sum4:10- sum9:10- lb2.4:10.14- bA0:10.29- duB1:10.3- eA0:10.3- laA3:10.32- sgA2:10.4- yB0:10.45v bA1.4:10.53- laB3.4:10.54- sgA0:10.58- absA3:10.8- holdA0:10.95v eA2:11.05- onB0:11.2- duA2.1:11.21- duB2:11.3- yB1:11.3a absA1.1:11.34- ooB0.1:11.38- holdB0:11.39v ooB0:11.4v fin0.4:11.49- fin2:11.6- laB1.1:11.96- bA1.1:12.09- eA0.1:12.09- laA4:12.1- laB0.1:12.11- absB0:12.12- holdA1:12.15- yB0.4:12.15a laB1:12.16- yB1.4:12.17- onB1:12.2- holdA3:12.25- laB2:12.31v ooB1:12.32- ooB1.1:12.32a absB1:12.4- laB4:12.45- bB1:12.6- bB0:12.61- absB2:12.67- laB1.4:12.68- laA2:12.79- bA1:12.88- absB3:12.9- holdB2:12.97- sumA1:12.97- holdA4:13.05- bB0.1:13.08- eB0:13.1- laB3:13.1- holdA2:13.14- swapA0:13.15- back2:13.2- uxA0:13.2- swapB0.4:13.26- swapB0.1:13.26- uxA1:13.35- fin1.4:13.45- swapA2:13.5- expA0:13.5- laB0.4:13.54- eB1:13.7- swapA3:13.75- eB2:13.8- nameA0:13.95- holdB1:14.1- uvA0:14.1- nameA1:14.2- holdB2.4:14.29- holdB3:14.3- swapB1:14.35- holdB4:14.5- swapB2:14.7- uxB0:14.7- ZB0.4:14.87a absB0.4:14.88- swapB3:14.9- XA0:14.98a uxB1:15- expA1.4:15.02- expB0:15.1- urA0:15.23- urB1:15.4- holdB2.1:15.42- uvB1:15.5- swapA1:15.95- ZA0:16v sum0:16- uvA1.1:16.02- swapB0:16.09- sumA0:16.1- sum1:16.2- ZB1.4:16.25a sum2:16.4- ZA1:16.5v laA3.1:16.59- sum3:16.6- XA1:17a set29:17.43a nameB0:17.45- holdB3.1:17.59- urB0:17.6- sumA2:17.9- sum5:18- laB4.4:18.12- expB1:18.15- sum6:18.2- sum7:18.4- sumA5:18.5- yr0:18.5- uvB0:18.53- sum8:18.6- sumA6:18.7- wall0:19v wall1.4:19v XB0:19.18- yr1:19.2- wall3:19.5a yr2:19.5- nameB3:19.6a yw0:20- wall2.4:20.01a wall7.4:20.26v wall4.4:20.3a nameB2:20.5- wall6:20.5v yw1:20.5- sumB0:20.6- sumA3:20.85- XB1.4:20.94- yw2:21- yw3:21- nameB1:21.23- uvA1:21.43- yw4:21.5- sumA2.1:21.86- set37:21.89a yw5:22- set23:22.12a set36:22.52- sumB2:23- wall5.4:23.01a set38:23.34a sumB4:23.5- sumB5:23.7- sumB6:25.5- set49:25.57v sumB7:25.7- tot0:26a tot1:26.2- sumA7:28.96- sumB1:28.97- set58:29.95- set10:31.97v sumB3:36.71- set57:38.96- set63:75.92-
""".split()}
ROUND = {w.split(":")[0]: (float(w.split(":")[1][:-1]), w[-1]) for w in """
ggA0:-0.23a ggA1:0a src0:0.8v puA0:0.8- load0:1- load1:1.1- load2:1.2- load3:1.3- puA1:1.4- load5:1.4- puA2:1.5- early0:2- early1:2.01- early11:2.1- early3:2.2- early4:2.21- early5:2.22- early9:2.3- early6:2.31a early10:2.32a early12:2.33a early8:2.34a early13:2.35a early2:2.4- early14:2.45- first0:2.46- first1:2.46- first2:2.47- early7:2.5- early15:2.6- load4:2.7- first3:2.7- first4:2.8- early16:2.91a early17:2.92v early18:2.93- dnt0:3.2- dnt1:3.3- first5:3.4- set5:3.5- markA0.1:3.6- ggB0.1:3.7v ggB1.1:3.7a lb0.1:3.8- lb1.1:3.81- yB0.1:3.81v lb2.1:3.82- markB0.1:3.83- dnA0.1:3.9a duA0.1:3.92- duA1.1:3.93- yA0.1:4a yA1.1:4.1a set41:4.16a yA0.4:4.59v ggB0:4.6v duA1:5.35- duA2:5.5- dnA1.1:5.5v markA0:5.67- lb1:5.95- lb2:6.15- puB1:6.45- laA0.4:6.57- puB2:6.6- markB0:6.6- lb3:6.7a ggB1:6.79a RA0:6.8a yA1:7.1a duA0:7.27- yA0:7.8a RB0:8.1a absA0:8.11- laA1:8.12- dnB0:8.6a absA2:8.7- lb0.4:8.7- puB0:8.9- lb0:9.07- dnB1:9.4a ooA0:9.55v ooA1:9.55a laB0:9.6- absA1.1:9.64- sgA1:9.83v back0:10- sum4:10- sum9:10- lb2.4:10.13- laA0:10.19- duB1:10.3- laA3:10.32- absA1:10.35- eA1:10.4- sgA2:10.4- yB0:10.45v duB0:10.48- eA0:10.48- bA0:10.59- bA1.4:10.67- eA2:10.71- sgA0:10.75- absA3:10.8- holdA0:10.95v bA1.1:11.05- holdA4:11.2- duB2:11.3- yB1:11.3a ooB0:11.4v duA2.1:11.49- fin1:11.5- laB3:11.53- absB2.4:11.59- fin2:11.6- absB0:11.82- bB1:11.82- laB4:11.97- laB1:12- holdA2:12.05- fin0.4:12.08- eA0.1:12.09- holdA1:12.15- holdA1.4:12.15- RB0.4:12.16a onB1:12.2- laB0.1:12.21- holdA3:12.25- laB2:12.31v ooB1:12.32a onA0:12.34- yB0.4:12.38- absB1:12.4- absB2:12.67- bA1:12.76- laB0.4:12.79- absB3:12.9- bB0:12.9- back1:13- eB0:13.1- swapA0:13.15- uxA0:13.2- swapA1:13.3- ooB0.1:13.32- holdB2.4:13.34- uxA1:13.35- swapB0.4:13.35- swapA2:13.5- expA0:13.5- laA2:13.64v eB1:13.7- laA4:13.71- swapA3:13.75- eB2:13.8- nameA0:13.95- holdB1:14.1- uvA0:14.1- swapB0:14.1- nameA1:14.2- swapB1.4:14.27- holdB3:14.3- holdB0.4:14.34v absB0.4:14.39- onB0:14.44- holdB4:14.5- urA0:14.58- laB4.4:14.65- uxB0:14.7- swapB3:14.9- expA1.4:14.99- uxB1:15- urB0:15.1- uxB1.1:15.27- uxB1.4:15.37- uvB1:15.5- holdB0:15.51v swapB2:15.67- laB1.1:15.81- holdB2:15.88- ZA0:16v sum0:16- sumA0:16.1- swapB1:16.16- sumA1:16.2- sum1:16.2- sum2:16.4- ZA1:16.5v sum3:16.6- XA0:16.8a XA1:17a ZB1.4:17.2a uvA1.1:17.22- urB1:17.44- nameB0:17.45- yw1.4:17.62v sumA2:17.9- sum5:18- lb3.1:18.02- sumA4:18.2- sum6:18.2- ZB0.4:18.2a holdB3.1:18.45- sumA5:18.5- yr0:18.5- sum8:18.6- sumA6:18.7- wall0:19v wall1.4:19v expB0:19.13- uvB0:19.16- yr1:19.2- wall3:19.5a yr2:19.5- nameB3:19.6a expB1:19.7- XB0:19.95- set21:20.22a set7:20.24a wall7.4:20.26v XB0.1:20.41a nameB2:20.5- wall6:20.5v wall2.4:20.5a sumB0:20.6- sumB1:20.8- XB1.4:20.93- yw2:21- yw3:21- set37:21.46- yw4:21.5- nameB1:21.7- sumA0.1:21.72- uvA1:21.92- yw5:22- set26:22.36v nameB3.1:22.38v set61:22.6- sumB2:23- set15:23.02- set60:23.03- set16:23.09a sumB3:23.2- sumB4:23.5- sumB5:23.7- yw0.4:24- set9:24.84v wall4.4:24.98- wall5.4:24.99a sum7.4:25- sumB6:25.5- sumB7:25.7- tot0:26a tot1:26.2- set68:26.9- set25:28.05a set36:28.39v set34:28.68- sumA3:32.19- set48:32.25- set11:36.89- sumA7:38.01- set62:40.73- set63:42.55- set65:59.1- set20:71.74v set30:74.47a set44:81.86v
""".split()}
ROUND = {w.split(":")[0]: (float(w.split(":")[1][:-1]), w[-1]) for w in """
ggA0:0v ggA1:0a ggA1.4:0.04a puA0:0.8- load0:1- load1:1.1- load2:1.2- load3:1.3- load5:1.4- puA2:1.5- early0:2- early1:2.01- early11:2.1- early3:2.2- early4:2.21- early5:2.22- early9:2.3- early6:2.31a early10:2.32a early12:2.33a early8:2.34a early13:2.35a early2:2.4- early14:2.45- first0:2.46- first1:2.46- set39:2.46- first2:2.47- early7:2.5- early15:2.6- ggA0.4:2.6v load4:2.7- first3:2.7- first4:2.8- set54:2.8- early16:2.91a set38:2.91- early17:2.92v early18:2.93- src0:3.02v dnt0:3.2- dnt1:3.3- first5:3.4- set5:3.5- markA0.1:3.6- ggB0.1:3.7v ggB1.1:3.7a lb0.1:3.8- lb1.1:3.81- lb2.1:3.82- markB0.1:3.83- dnA0.1:3.9a duA0.1:3.92- duA1.1:3.93- yA0.1:4a yA1.1:4.1a yB0.1:4.26v puA1:4.29- ggB0:4.6v ggB1:4.6a duA1:5.35- markA0:5.67- puB0:5.9- lb1:5.95- yA1:6.05a dnA1.1:6.11v lb2:6.15- yA0:6.17a dnB1.1:6.34a dnB0.1:6.41a duB0.1:6.42- yA0.4:6.5v puB2:6.6- markB0:6.6- lb3:6.7a yA1.4:6.74a ggB1.4:6.74- duA0:6.76- RA0:6.8a laA0:8.1- duA2:8.2- absA0:8.2- onA0:8.3- puB1:8.5- absA2:8.7- lb0:8.86- bA0:9- laA1:9.04- RB0:9.21a ooA0:9.55v sgA0:9.55- laB0:9.6- laB1:9.61- puB0.4:9.71- sgA1.1:9.83- laA0.1:9.87- absA3.1:9.87- absA1.1:9.87- sgA1.4:9.92v back0:10- lb2.4:10.13- duB1:10.3- eA0:10.3- laA3:10.32- holdA0.1:10.33a bB1:10.35- bA1.1:10.35- absA0.1:10.38- eA1:10.4- sgA2:10.4- yB0:10.46a ooA1:10.79- absA2.1:10.87- holdA0:10.91v laB3:10.92- bA0.1:10.94- absB0:10.99- sgA1:11.02v absA2.4:11.02- eA2:11.05- yB1:11.05a absA1:11.12- duB0:11.14- onB0:11.2- absB3:11.3- bA1:11.4- absA3:11.45- fin1:11.5- fin2:11.6- absA0.4:11.61- yB1.4:11.61a ooA0.1:11.66- ooB0:11.95a absB2:12.04- holdA2:12.05- laA4:12.1- holdA1:12.15- onB1:12.2- holdA3:12.25- ooB1:12.3v absB1:12.4- laB0.1:12.74- absB0.1:12.75- holdA0.4:12.82- yB0.4:12.89- laB2:12.9- bB0:12.9- eB0:13.1- uxA0:13.2- swapA1:13.3- uxA1:13.35- bB1.1:13.36- duB2:13.4- holdA4:13.51- laA2:13.64v swapA3:13.75- eB2:13.8- absB2.1:13.86- laB4:13.9- nameA0:13.95- eB1:13.98- holdB0:14a urA0:14- holdB0.4:14.06v uvA0:14.1- absB2.4:14.18- nameA1:14.2- holdB1.4:14.24- holdB3:14.3- swapA0:14.35- holdB4:14.5- laA2.4:14.66a swapB2:14.7- uxB0:14.7- bB0.4:14.71- laA2.1:14.73v laB1.1:14.87- expA0.4:14.95- uxB1:15- absB0.4:15.05- urB0:15.1- expB0:15.1- uvB1:15.5- swapB1.4:15.85- swapA2:15.86- ZA0:16v back1:16.1- swapB3:16.13- holdB2:16.55- fin0.4:16.57- swapB0:16.66- XA0:16.8a XA1:17a ZB0:17v uxB0.4:17.31- nameB1:17.5- ZA1.4:17.77- sumA1.4:17.99- expA1.4:18.08- holdB1:18.36- XB1:18.5a yr0:18.5- lb3.1:18.95a urB0.4:19.11- XB0.1:19.14a swapB1:19.3- yr2:19.5- nameB3:19.6a expB1:19.7- wall3.4:19.91v wall2.4:19.94a expA0:19.95- ZB1.4:19.95- wall1.4:19.98v wall5:20a yw0:20- swapB0.1:20.28- set68:20.49- wall6:20.5v yw1:20.5- swapB1.1:20.73- set26:20.89a XB0:20.91- yw3:21- uvA1.1:21.02- urB1:21.11- uvB0:21.25- holdB2.1:21.27- yw4:21.5- nameB0:21.63- nameB2:21.68- uvA1:21.75- sumA0:21.89- yw5:22- wall0.4:22.95a wall7.4:23.25v onB1.1:23.91- set63:24.1- uvA1.4:24.54- yr1.4:24.83v wall4.4:24.98- yw2.4:25.14- set17:25.89- tot1:26.2- sumB0:26.37- sumA2.1:26.41v set21:26.78- sumA1:26.9- set27:27.21- sumA2:27.31a sumB1:27.32- sumB2:28- set59:28.72v set36:28.76- set58:28.99v sumB0.1:29.2- set44:29.49a set34:30.22- tot0:35.31- set55:56.01- set29:58.36a set67:76.12-
""".split()}
PLAN = ["""
load0 load1 early0 early11 early1 load2 early3 early4 early5 load3 set1 set4 early9 set2 load5 early6a early2 early14 early8a early10a first1 set3 set6 set7a set36a early12a early7 set39 set38 first0 early13a set34a set51 set8 set15a set59v set14a set24a set57 set67 early16a set37 set13a early15 set45 load4 set74 set68 set10a set75 first2 set40a set52 early17v markA0.1 set48 first3 set50 set16a set70 set25a set5 set58a early18 dnt0 set49 set17a set26a set23a set11a set12a set46 set27a first4 set41a set42a set47 set53a yA0.1a yA1.1a bA1.1 ggB1.1a set9a ggB0.1v laA1.1 yB1.1v lb0.1 first5 yB0.1a set18a absA0.1 onB1.1 bA0.1 set21a laA0.1 onA0.1 set22a dnt1 lb1.1 set55 set35a set0 dnA1.1a dnA0.1a set19a set54 set61 lb2.1 set28a markB0.1 back0.1 duA0.1 absA2.1 absA1.1 absB0.1 sgA0.1 bB0.1 duA1.1 set69 ooA0.1v onB0.1 lb3.1v set32a laA2.1a laA3.1 set43a set62 sgA1.1v set31a dnB1.1a set71 ooA1.1a absA3.1 dnB0.1a absB1.1 set30v set63 eA0.1 sgA2.1 laA4.1 set73 set65 duA2.1 set60 eA1.1 bA2.1 set66 holdA2.1 duB0.1 holdA0.1a set44v eA2.1 set20a set72 holdA1.1 laB0.1 duB1.1 holdA3.1 set29v holdA4.1 absB2.1 uxA0.1 set56 bB1.1 ooB1.1a laB2.1a laB1.1 set33a duB2.1 ooB0.1v back1.1 set64 swapA0.1 uxA1.1 absB3.1 bB2.1 swapA1.1 nameA0.1 swapA2.1 laB3.1 eB0.1 swapA3.1 nameA1.1 swapB0.1 laB4.1 holdB0.1v eB1.1 holdB1.1 uvA0.1 holdB2.1 uvA1.1 holdB3.1 expA0.1 holdB4.1 swapB1.1 urA0.1 uxB0.1 swapB2.1 ggA0.2a swapB3.1 urB0.1 eB2.1 ggA1.2a urB1.1 sumA0.1 urB2.1 duA0.2 uvB0.1 XA0.1a uvB1.1 XB0.1a puA0.2 src0.2v puA1.2 nameB0.1 nameB1.1 RA0.2a bA0.2 markA0.2 nameB2.1 laA0.2 ggB0.2v nameB3.1v ggB1.2a puA2.2 yA0.2a yA1.2a lb0.2 uxB1.1 sumA1.1 onA0.2 RB0.2a puB0.2 laA2.2v duA2.2 lb1.2 expB0.1 lb2.2 duA1.2 puB1.2 absA0.2 duB0.2 bA1.2 laA1.2 absA2.2 absA1.2 markB0.2 duB1.2 laB0.2 expB1.1 absA3.2 sgA0.2 ooA0.2v puB2.2 ooA1.2a lb3.2v onB0.2 sgA1.2v sumB0.1 bB0.2 eA0.2 laB2.2a laA4.2 laA3.2 sgA2.2 eA1.2 yB0.2a yB1.2a bA2.2 holdA0.2a ooB1.2a sumB1.1 absB0.2 holdA1.2 laB1.2 ooB0.2v holdA2.2 eA2.2 onB1.2 absB1.2 sumA2.1v sumB2.1v tot0.1 holdA3.2 laB4.2 duB2.2 holdA4.2 swapA0.2 back1.2 absB2.2 uxA0.2 bB1.2 laB3.2 uxA1.2 absB3.2 bB2.2 swapA1.2 swapA2.2 swapB0.2 holdB2.2 expA0.2 eB0.2 swapA3.2 nameA0.2 holdB0.2a holdB1.2 nameA1.2 swapB1.2 uvA0.2 eB1.2 holdB3.2 holdB4.2 eB2.2 swapB2.2 urA0.2 back0.2 swapB3.2 urB0.2 urB1.2 uvA1.2 urB2.2 uvB0.2 ggA0.3a ggA1.3a src0.3v uvB1.2 puA0.3 XA0.2a XB0.2a uxB0.2 puA1.3 markA0.3 nameB0.2 uxB1.2 RA0.3a duA0.3 duA1.3 nameB1.2 nameB2.2 bA0.3 puA2.3 duA2.3 ggB0.3v laA0.3 ggB1.3a lb0.3 puB0.3 yA1.3a yA0.3a expB1.2 laA1.3 nameB3.2v sumA1.2 absA2.3 sumA0.2 lb1.3 RB0.3a expB0.2 duB0.3 absA0.3 bA1.3 bB0.3 lb2.3 onA0.3 puB1.3 puB2.3 markB0.3 laA2.3v ooA0.3v sgA0.3 absA3.3 lb3.3v sgA1.3v onB0.3 sgA2.3 sumB0.2 absA1.3 ooA1.3a laB0.3 eA0.3 laA4.3 back0.3 laA3.3 yB0.3a eA1.3 sumB1.2 bA2.3 absB0.3 yB1.3a laB2.3v eA2.3 holdA0.3a duB1.3 ooB1.3a ooB0.3v sumB2.2a laB1.3 holdA1.3 holdA2.3 absB2.3 absB1.3 onB1.3 duB2.3 laB4.3 swapA0.3 laB3.3 holdA3.3 sumA2.2v tot0.2 holdA4.3 swapA1.3 bB1.3 absB3.3 bB2.3 uxA0.3 swapB0.3 swapA2.3 uxA1.3 eB0.3 holdB0.3a holdB2.3 swapA3.3 swapB1.3 eB1.3 holdB1.3 expA0.3 back1.3 holdB3.3 uvA0.3 nameA0.3 eB2.3 urA0.3 holdB4.3 uvA1.3 swapB2.3 uxB0.3 swapB3.3 nameA1.3 ggA1.4a urB0.3 urB1.3 uvB0.3 ggA0.4v uvB1.3 puA0.4 sumA1.3 puA1.4 nameB0.3 urB2.3 XA0.3a XB0.3a RA0.4a nameB1.3 markA0.4 nameB2.3 ggB0.4v uxB1.3 puA2.4 sumA0.3 laA0.4 bA0.4 ggB1.4a lb0.4 puB0.4 nameB3.3v yA0.4a yA1.4a lb1.4 expB0.3 lb3.4v absA0.4 absA2.4 absA1.4 lb2.4 absA3.4 puB1.4 markB0.4 puB2.4 bA1.4 laA1.4 RB0.4a expB1.3 laA2.4v laA3.4 bA2.4 sgA0.4 sgA1.4a sgA2.4 holdA0.4v holdA1.4 laB0.4 swapA0.4 sumB0.3 fin0.4 bB0.4 sumB1.3 sumA2.3v holdA2.4 holdA3.4 sumB2.3a holdA4.4 uxA0.4 yB1.4a tot0.3 absB2.4 laA4.4 yB0.4v absB0.4 uxA1.4 fin1.4 swapA1.4 swapA2.4 expA0.4 laB2.4a bB1.4 absB3.4 laB1.4 absB1.4 bB2.4 swapA3.4 laB3.4 uvA0.4 expA1.4 holdB0.4a uvA1.4 sumA2.4 fin2.4 holdB1.4 swapB0.4 oldA0.4 urA0.4 holdB2.4 XA0.4a laB4.4 oldB0.4 holdB3.4 holdB4.4 uxB0.4 XA1.4a uxB1.4 expB1.4 expB0.4 sumA4.4 sumA1.4 sumA0.4 swapB1.4 swapB2.4 swapB3.4 urB0.4 sumA7.4 uvB0.4 sumA3.4 sumB1.4 sumA6.4 urB1.4 ZA0.4v sumB0.4 sumB4.4 ZA1.4v ZB0.4a ZB1.4a sumB3.4 yr0.4 uvB1.4 XB0.4v XB1.4a wall0.4v sumB2.4 wall2.4v wall1.4a wall3.4a sumB5.4 yw0.4 wall5.4a wall4.4a wall6.4v wall7.4v sumB6.4 yw1.4v yw3.4 sumB7.4 sumA5.4 yr1.4v yw2.4 yr2.4 yw4.4a yw5.4 tot0.4a tot1.4
"""]
PLAN = ["""
set61 early0 load1 early3 early4 early1 load0 early5 load3 load2 load5 early9 set1 early11 early8a set7a set8 early13v early14 early16a early2 first1 early10a load4 early12a set2 early6a early15 early17a set37 set4 set38 set68 first2 early7 dnt0 first0 early18 set39 set41a set13a first3 set3 set15v set17a first4 set45 dnt1 set50 far1 set59a far0 set6 set34v set23a set0 set47 set5 set40v set52 set46 set74 set49 set67 first5 markA0.1 set48 set16a set57 set36a set25a ggB0.1v yA1.1a yA0.1a set26a set10a set51 ggB1.1a onA0.1 yB0.1v set71 yB1.1a bA1.1 laA1.1 set27a lb0.1 lb1.1 lb2.1 bB1.1 set14a laA0.1 absA2.1 bA0.1 absA0.1 set53a set54 set28a markB0.1 far2 set65 set9a set24a lb3.1a set22a set11a dnA1.1a dnA0.1a absA3.1 duA0.1 duA1.1 set55 ooA0.1v absA1.1 set69 ooA1.1a sgA0.1 bA2.1 set72 holdA0.1v sgA1.1a onB0.1 sgA2.1 set58v eA0.1 set63 duA2.1 set60 absB0.1 holdA1.1 eA1.1 eA2.1 set12a set18v set56 dnB1.1a set42a laA2.1a laB0.1 absB2.1 set70 set73 set66 dnB0.1v laA3.1 set19a duB0.1 holdA2.1 holdA3.1 holdA4.1 set75 set43a set44a swapA0.1 bB0.1 uxA0.1 duB1.1 absB1.1 laA4.1 absB3.1 ooB0.1v ooB1.1a back1.1 laB1.1 set29a swapA1.1 bB2.1 swapA2.1 uxA1.1 laB2.1a set62 swapA3.1 set32v laB3.1 urA0.1 holdB0.1v swapB0.1 duB2.1 holdB1.1 urA1.1 set35a set30a laB4.1 nameA0.1 holdB2.1 holdB3.1 holdB4.1 eB0.1 eB1.1 uvA0.1 uxB0.1 set21a swapB1.1 expA0.1 nameA1.1 swapB2.1 uvA1.1 swapB3.1 ggA1.2a ggA0.2v XA0.1a uvB0.1 back0.1 sumA0.1 urA2.1 urB0.1 puA0.2 eB2.1 uxB1.1 set20v src0.2a RA0.2a duA0.2 uvB1.1 puA1.2 urB1.1 XB0.1v nameB0.1 puA2.2 nameB1.1 urB2.1 markA0.2 nameB2.1 ggB0.2v set31v sumA1.1 set64 onA0.2 expB0.1 yA1.2a yA0.2a bA0.2 laA0.2 onA1.2 absA2.2 absA0.2 ggB1.2a lb0.2 nameB3.1v absA3.2 lb1.2 absA1.2 laA2.2a puB0.2 bA2.2 lb2.2 duA1.2 set33a puB1.2 duB0.2 RB0.2a expB1.1 markB0.2 puB2.2 bA1.2 lb3.2a holdA0.2a bB0.2 holdA1.2 onB0.2 laA1.2 ooA1.2a ooA0.2v sgA0.2 laB0.2 duA2.2 duB1.2 laA4.2 laA3.2 holdA2.2 sgA1.2a sgA2.2 eA0.2 yB1.2a yB0.2a eA1.2 eA2.2 holdA3.2 duB2.2 swapA0.2 absB2.2 absB0.2 laB2.2a laB1.2 ooB0.2v holdA4.2 uxA0.2 ooB1.2a absB1.2 absB3.2 sumB0.1 sumB1.1 swapA1.2 uxA1.2 laB3.2 eB0.2 eB1.2 swapA2.2 swapA3.2 expA0.2 onB1.2 bB1.2 nameA0.2 urA0.2 bB2.2 urA1.2 nameA1.2 holdB0.2a back1.2 holdB1.2 ggA0.3v laB4.2 uvA0.2 uvA1.2 holdB2.2 back0.2 sumA2.1v swapB0.2 holdB3.2 swapB1.2 eB2.2 holdB4.2 urA2.2 swapB2.2 ggA1.3a puA0.3 puA1.3 swapB3.2 uxB0.2 uxB1.2 uvB0.2 sumB2.1a src0.3v puA2.3 urB0.2 urB1.2 tot0.1 XA0.2a duA0.3 nameB0.2 uvB1.2 nameB1.2 markA0.3 nameB2.2 RA0.3a urB2.2 bA0.3 onA0.3 laA0.3 XB0.2a yA0.3a absA0.3 ggB1.3a duA1.3 ggB0.3v lb0.3 sumA1.2 nameB3.2a yA1.3a onA1.3 puB0.3 lb3.3v laA2.3v lb1.3 absA1.3 lb2.3 duA2.3 absA2.3 laA1.3 puB1.3 expB1.2 absA3.3 bA2.3 duB0.3 bA1.3 markB0.3 RB0.3a puB2.3 duB1.3 ooA0.3v expB0.2 onB0.3 laB0.3 sgA0.3 laA3.3 sumA0.2 back0.3 ooA1.3a sgA1.3a swapA0.3 holdA2.3 sgA2.3 holdA0.3v yB0.3a eA0.3 eA1.3 laA4.3 yB1.3a bB0.3 sumB0.2 eA2.3 absB0.3 absB2.3 holdA1.3 sumB1.2 ooB0.3v ooB1.3a back1.3 holdA3.3 holdA4.3 bB1.3 sumA2.2a onB1.3 laB2.3a duB2.3 swapA1.3 uxA0.3 laB1.3 swapA2.3 uxA1.3 swapA3.3 laB4.3 urA0.3 sumB2.2v laB3.3 absB1.3 absB3.3 bB2.3 nameA0.3 urA1.3 nameA1.3 swapB0.3 uvA0.3 expA0.3 holdB2.3 urA2.3 ggA1.4a uvA1.3 holdB0.3v ggA0.4v eB0.3 holdB1.3 swapB1.3 eB1.3 holdB3.3 holdB4.3 eB2.3 puA0.4 swapB2.3 swapB3.3 puA1.4 puA2.4 tot0.2 uvB0.3 XA0.3a uvB1.3 urB0.3 RA0.4a uxB0.3 bA0.4 markA0.4 XB0.3a laA0.4 nameB0.3 nameB1.3 yA1.4a urB1.3 laA2.4v uxB1.3 nameB2.3 urB2.3 ggB1.4a absA2.4 ggB0.4v nameB3.3a expB1.3 yA0.4v puB0.4 puB1.4 sumA0.3 lb0.4 expB0.3 absA3.4 absA0.4 absA1.4 bA1.4 laA1.4 bA2.4 lb1.4 RB0.4a laB0.4 lb2.4 markB0.4 holdA0.4a holdA1.4 bB0.4 laA3.4 holdA2.4 sgA0.4 holdA3.4 swapA0.4 sgA1.4v puB2.4 yB1.4a yB0.4a laB1.4 absB0.4 holdA4.4 lb3.4a sumB0.3 sumB1.3 sumB2.3v uxA0.4 laB2.4v uxA1.4 absB1.4 absB2.4 bB1.4 sgA2.4 sumA1.3 fin0.4 expA0.4 sumA2.3v expA1.4 laB4.4 laB3.4 absB3.4 bB2.4 tot0.3 sumA0.4 laA4.4 sumA1.4 fin1.4 swapA1.4 swapA2.4 swapA3.4 uvA0.4 holdB0.4a holdB2.4 uvA1.4 holdB1.4 urA0.4 holdB3.4 holdB4.4 XA0.4a swapB0.4 uxB0.4 uxB1.4 expB0.4 fin2.4 swapB1.4 expB1.4 XA1.4v sumA2.4 oldA0.4 swapB2.4 urA1.4 ZA0.4a swapB3.4 oldB0.4 uvB0.4 ZA1.4v urB0.4 urB1.4 uvB1.4 sumB4.4 sumB0.4 sumB3.4 ZB0.4v sumB7.4 ZB1.4a yr0.4 sumB2.4 XB1.4a XB0.4v wall4.4a wall7.4a wall6.4v wall5.4v yw3.4 wall0.4a wall3.4a sumB1.4 wall2.4v wall1.4v yr1.4v yw4.4v yr2.4 yw0.4 yw1.4a sumB5.4 sumB6.4 yw5.4 tot0.4a yw2.4 tot1.4
"""]


def overlap(hist, reads, writes):
    for regs, wr in ((reads, False), (writes, True)):
        for name, lo, hi in regs:
            for x in hist.get(name, []):
                if x[0] < hi and lo < x[1] and (wr or x[3]):
                    yield x[2]


def note(hist, key, reads, writes, keep=False):
    for name, lo, hi in writes:
        hist[name] = [x for x in hist.get(name, []) if keep or not (lo <= x[0] and x[1] <= hi)] + [(lo, hi, key, True)]
    for name, lo, hi in reads:
        hist.setdefault(name, []).append((lo, hi, key, False))


def banks(o):
    return set((nm, b) for nm, lo, hi in o["r"] + o["w"] if SCRATCH[nm][0] == "psum" for b in range(lo // 512, (hi + 511) // 512))


def graph(ops):
    hist, pred, sent = {}, [], {}
    for i, o in enumerate(ops):
        grp = o.get("group")
        pred.append(set(p for p in overlap(hist, o["r"] + o.get("after", []), o["w"]) if grp is None or ops[p].get("group") != grp))
        note(hist, i, o["r"], o["w"], grp is not None)
        if o["kind"] == "land":
            pred[i].add(i - 1)
        if o["kind"] == "send" and o["sem"] != "an":
            pred[i].add(ORDER["first"])
        if o["name"] in ("load4", "dnt0"):
            pred[i].add(ORDER["first"] + 2)
    return pred


def ways(ops, est):
    out = []
    for o in ops:
        w = []
        for e, cost in o["cost"].items():
            busy, lat = cost(est)
            use = [(e, 0.0, busy)] if e != "-" else []
            use += [(b, 0.0, busy + est["wake"]) for b in banks(o)]
            if o["kind"] == "dma":
                use.append(("dma", busy + 0.6 * est["dfix"], busy + lat - 0.4 * est["dfix"]))
            if o["kind"] == "send":
                use.append((("link", o["via"] is None), busy + est["rfix"] / 2, busy + est["rfix"] / 2 + lat))
                lat += est["rfix"] / 2
            if o["kind"] == "land":
                way = est["rfix"] / 2
                if o["via"] is not None:
                    way += (est["first"] if o["sem"] in ("l200", "l210") else 0) + est["riss"] + est["rfix"] + (est["dfix"] + 1.0) * o["via"] * (o["d"] == 1)
                    use.append(("port", way, way + lat))
                    way += lat
                lat = way
            w.append((e, busy + lat + (est["wake"] if o["kind"] != "send" else 0.0), use))
        out.append(w)
    return out


def place(prio, pred, succ, way, pick):
    n = len(prio)
    line, end, got = {}, [0.0] * n, [None] * n
    left = [len(p) for p in pred]
    ready = [i for i in range(n) if not left[i]]
    while ready:
        i = min(ready, key=lambda k: (prio[k], k))
        ready.remove(i)
        t0 = max([end[p] for p in pred[i]] + [0.0])
        best = None
        for e, d, use in way[i]:
            if len(way[i]) > 1 and pick[i] in "va" and pick[i] != e:
                continue
            t, moved = t0, True
            while moved:
                moved = False
                for r, a, b in use:
                    ln = line.get(r, ())
                    k = len(ln)
                    while k and ln[k - 1][1] > t + a + 1e-9:
                        k -= 1
                    while k < len(ln) and ln[k][0] < t + b - 1e-9:
                        t, moved = ln[k][1] - a, True
                        k += 1
            score = t + d + (0.5 if e == "v" else 0.0)
            if best is None or score < best[4]:
                best = (t + d, t, e, use, score)
        end[i], got[i] = best[0], (best[1], best[2])
        for r, a, b in best[3]:
            line.setdefault(r, []).append((best[1] + a, best[1] + b))
            line[r].sort()
        for s in succ[i]:
            left[s] -= 1
            if not left[s]:
                ready.append(s)
    return end, got


def arrange(ops):
    n = len(ops)
    if PLAN[0]:
        ix = {o["name"] + (".%d" % o["t"] if o["t"] else ""): i for i, o in enumerate(ops) if o["name"]}
        out = []
        for w in PLAN[0].split():
            i = ix[w] if w in ix else ix[w[:-1]]
            out.append((i, list(ops[i]["cost"])[0] if w in ix else w[-1]))
            if ops[i]["kind"] == "send":
                out.append((i + 1, "-"))
        assert len(out) == n
        return out
    pred, way = graph(ops), ways(ops, EST)
    succ = [[] for _ in ops]
    for i in range(n):
        for p in pred[i]:
            succ[p].append(i)
    prio, pick = [0.0] * n, ["-"] * n
    for i in reversed(range(n)):
        o = ops[i]
        at = ROUND.get("%s.%d" % (o["name"], o["t"])) or ROUND.get(o["name"])
        if at:
            prio[i], pick[i] = PERIOD * o["t"] + at[0], at[1]
        else:
            prio[i] = min([prio[s] for s in succ[i]] + [200.0]) - min(w[1] for w in way[i])
    end, got = place(prio, pred, succ, way, pick)
    ORDER["ops"], ORDER["end"] = ops, max(end)
    return [(i, got[i][1]) for i in sorted(range(n), key=lambda k: (round(got[k][0], 6), k))]


def rank_program(g, core, T, topo):
    n = len(T.cores)

    def helper(r, h):
        c = T.cores[r % n]
        return [x for x in topo.cores_of(c) if topo.die(x) != topo.die(c)][h]

    rank, role = T.rank_of(core), None
    for r in range(n):
        for h in range(2):
            if helper(r, h) == core:
                rank, role = r, h
    if rank is None:
        return
    Q = {"v": g.vector, "a": g.scalar, "p": g.tensor, "g": g, "s": g.sync}
    ops, label, count = [], ["", 0], {}

    def at(name, t):
        label[:] = [name, t]

    def add(**o):
        k = count[tuple(label)] = count.get(tuple(label), -1) + 1
        ops.append(dict(o, name=label[0] + str(k), t=label[1]))

    def V(name, a=0, b=None, st=1, p=None):
        if b is None:
            b = SCRATCH[name][1][1]
        ps = slice(0, 128) if p is None else slice(*p)
        return (T[name][ps, a:b:st] if st > 1 else T[name][ps, a:b], [(name, a, b)], len(range(a, b, st)), SCRATCH[name][2], SCRATCH[name][0])

    def IND(win, off):
        return (win[0].indirect(off[0]), win[1] + off[1], 16 * off[2], win[3], "ind")

    def X(*at_):
        return (at_, [], 0, "", "dram")

    def ap(x):
        return T[x[0][0]][x[0][1]:x[0][2], x[0][3]:x[0][4]] if x[4] == "dram" else x[0]

    def aps(*xs):
        return [x for x in xs if isinstance(x, tuple)]

    def val(x):
        return x[0] if isinstance(x, tuple) else x

    def cyc(out, ins, k):
        key = "s" if out[4] == "ind" else "g" if ins and ins[0][4] == "ind" else None
        return lambda est: (est["fix"] + max(64, (est[key] if key else k) * out[2]) * est["cyc"], 0.0)

    def half(*xs):
        return 0.5 if all(x[3] in (BF, U16) for x in xs) else 1

    def op(calls, out, ins):
        reads = [r for x in ins for r in x[1]]
        writes = out[1]
        if out[4] == "ind":
            reads, writes = reads + out[1][1:], out[1][:1]
        add(kind="op", r=reads, w=writes, calls=calls, cost={e: cyc(out, ins, k) for e, (c, k) in calls.items()})

    def cp(out, a, both=False):
        calls = {"v": (lambda: g.vector.tensor_copy(out[0], a[0]), half(out, a))}
        if both:
            calls["a"] = (lambda: g.scalar.activation(out[0], a[0], FN.Identity), 1)
        op(calls, out, [a])

    def tt(out, a, b, o):
        op({"v": (lambda: g.vector.tensor_tensor(out[0], a[0], b[0], o), 2 if a[4] == b[4] else 1)}, out, [a, b])

    def ts(out, a, s1, o0, s2=None, o1=None, alt=None):
        if o1 is None:
            calls = {"v": (lambda: g.vector.tensor_scalar(out[0], a[0], val(s1), None, o0), half(out, a))}
        else:
            calls = {"v": (lambda: g.vector.tensor_scalar(out[0], a[0], val(s1), val(s2), o0, o1), half(out, a))}
        if alt:
            calls["a"] = (lambda: g.scalar.activation(out[0], a[0], alt[0], bias=val(alt[2]), scale=val(alt[1])), 1)
        op(calls, out, aps(a, s1, s2))

    def lin(out, a, scale, bias):
        ts(out, a, scale, ALU.mult, bias, ALU.add, alt=(FN.Identity, scale, bias))

    def scan(out, a, b):
        op({"v": (lambda: g.vector.tensor_tensor_scan(out[0], a[0], b[0], 0.0, ALU.mult, ALU.add), 1)}, out, [a, b])

    def fill(out, c):
        op({"v": (lambda: g.vector.memset(out[0], c), half(out))}, out, [])

    def act(out, a, f, scale=1.0):
        op({"a": (lambda: g.scalar.activation(out[0], a[0], f, scale=scale), 1)}, out, [a])

    def gather(buf, a, win, obuf, oa, cnt, ch=None):
        ch = ch or OPT["ch"]
        for c in range(0, cnt, ch):
            m = min(ch, cnt - c)
            cp(V(buf, a + c, a + c + m), IND(win, V(obuf, oa + c // 16, oa + (c + m) // 16)), True)

    def iota(out, pat, cm, base=0):
        if out[3] == I32:
            op({"g": (lambda: g.iota(out[0], pat, base, cm), 2)}, out, [])
        else:
            op({"g": (lambda: g.iota(out[0], pat, base, cm, allow_small_or_imprecise_dtypes=True), 2)}, out, [])

    runs, seen = {}, {}

    def mm(items, group=None, after=()):
        runs[group] = runs.get(group, 0) + 1

        def call():
            seen[group] = seen.get(group, 0) + 1
            start, stop = group is None or seen[group] == 1, group is None or seen[group] == runs[group]
            for i, (o, l, r) in enumerate(items):
                ins = g.tensor.matmul(o[0], l[0], r[0], start and i == 0, stop and i == len(items) - 1)
            return ins
        c = sum(max(64, r[2]) * (4 if r[3] == F32 else 1) for o, l, r in items)
        add(kind="op", r=[r for it in items for x in it[1:] for r in x[1]], calls={"p": (call, 0)}, cost={"p": lambda est: (c * est["pcyc"], 0.0)},
            w=sorted(set(r for it in items for r in it[0][1])), group=group, after=[r for x in after for r in x[1]])

    def wrap(out, s, buf, a, cnt):
        return [(out, V("sel", 144 * s + 15 - k, 144 * s + 143 - k), V(buf, a + k, a + cnt, 16)) for k in range(16)]

    def dma(e, pairs, kb):
        add(kind="dma", r=[r for o, i in pairs for r in i[1]], w=[r for o, i in pairs for r in o[1]], pairs=pairs,
            cost={e: lambda est: (0.1 * len(pairs), est["dfix"] + kb * 1024 / est["dbw"])})

    def rows(buf, a, b, pairs):
        dma("s", [(V(buf, a, b, p=(r, 128, 16)), tile) for r, tile in pairs], (40 + (b - a) // 24) * len(pairs))

    def send(d, out, a, sem, via=None, slot=0):
        by = 128 * a[2] * (4 if a[3] == F32 else 2)
        add(kind="send", r=a[1], w=[], d=d, out=out, a=a, sem=sem, via=via, slot=slot,
            cost={"g": lambda est: (est["riss"] + (est["first"] if sem == "an" else 0), 0.3 + by / est["rbw"] / (1 if via is None else 2))})
        ops.append(dict(kind="land", r=[], w=out[1], d=d, sem=sem, via=via, cost={"-": lambda est: (0.0, by / est["rbw"])}, name="", t=0))

    def LD(t, h):
        return (2 * (t - 2) + h) * LW

    def col(i):
        return V("col", i, i + 1)

    def eq(i):
        return V("eq", i, i + 1)

    DH, DL, QJ, QL = 0, 4, 8, 12
    PL, PH, PJ, PI = 1, 5, 9, 13

    def TG(t):
        return 4 * t - 2

    PT, DS, HP, HN, A15, PQ, S0, NG, PB = 0, 1, 2, 3, 4, 5, 6, 6, 9
    IDB, NID, P2, N2, BIG = 0, 128, 384, 640, 896

    def mat(m):
        return V("idb", m, m + 128)

    def turn(o):
        return V("idf", o, o + 128)

    at("load", 0)
    dma("s", [(V("nmi", 0, 64), X("nm", 0, 128, 0, 64)), (V("nmi", 64, 128, p=(SH, 128)), X("nm", 0, 128 - SH, 64, 128)),
              (V("nmi", 64, 128, p=(0, SH)), X("nm", 128 - SH, 128, 64, 128))], 64)
    dma("a", [(V("dni"), X("dn", 0, 8, 0, W))], 80)
    dma("a", [(V("pli", p=(0, 8)), X("pl", 0, 8, 0, 128))], 20)
    dma("a", [(V("rout", 0, H), X("rc", 0, 128, 0, H))], 256)
    dma("s", [(V("pool", W0, W0 + W), X("wl", 0, 128, 0, W))], 640)
    dma("a", [(V("rout", H, K, p=(SH, 128)), X("rc", 0, 128 - SH, H, K)), (V("rout", H, K, p=(0, SH)), X("rc", 128 - SH, 128, H, K))], 256)

    at("early", 0)
    iota(V("pci", 0, 1), [[0, 1]], 1)
    iota(V("mt"), [[1, 256]], 0)
    fill(V("tab", 0, W), 0.0)
    ts(V("pci", 4, 5), V("pci", 0, 1), 15, ALU.bitwise_and)
    ts(V("pci", 5, 6), V("pci", 0, 1), 2, ALU.arith_shift_right, 3, ALU.bitwise_and)
    cp(V("col", 1, 3), V("pci", 4, 6))
    lin(V("it"), V("mt", 0, 160), 0.0, col(1))
    rows("tab", 0, W, [(PI, V("it")), (PL, V("mt", 0, 160))])
    lin(V("i4", 0, 256), V("mt"), 0.0, col(2))
    ts(V("eq", 0, 16), V("mt", 0, 16), col(1), ALU.is_equal)
    i4, m4 = [V("i4", 256 * u, 256 * u + 256, p=(0, 128, 4)) for u in range(3)], V("mt", p=(0, 128, 4))
    lin(col(20), eq(PH), float(BX(1) // 128), eq(TG(1)))
    fill(V("tab", W, W + H), 0.0)
    lin(V("c0", 0, H), V("tab", W, W + H), 0.0, col(20))
    lin(V("i4", 256, 512), V("i4", 0, 256), 1.0, float(W // 256))
    cp(V("nl", 0, 128), V("nmi"))
    ORDER["first"] = len(ops) - 1
    rows("c0", 0, H, [(PJ, i4[0]), (PL, m4), (QJ, i4[1]), (QL, m4)])
    lin(V("i4", 512, 768), V("i4", 0, 256), 1.0, float(H // 256))
    lin(V("c0", H, K), V("tab", W, W + H), 0.0, col(20))
    rows("c0", H, K, [(PJ, i4[2]), (PL, m4)])
    at("set", 0)
    iota(V("ph"), [[K // 128, NT - 1], [0, 128]], 0, BX(2) // 128)
    iota(V("xi"), [[1, 144]], -1)
    iota(V("xw"), [[0, 2], [1, 128]], -1)
    iota(V("xb"), [[16, 8], [0, 16]], -1)
    iota(V("xf", p=(0, 8)), [[0, 2], [1, 8], [0, 16]], -1)
    act(V("one"), V("mt", 0, 128), FN.Exp, scale=0.0)
    ops[-1]["cost"] = {"a": lambda est: (1.5, 0.0)}
    at("first", 0)
    send(1, V("ui", 0, 128), V("nl", 0, 128), "an")
    cp(V("zb", 0, 160), V("dni"))
    tt(V("zb", 160, 320), V("dni"), V("zb", 0, 160), ALU.subtract)
    send(-1, V("zi"), V("zb"), "ad")
    for h in range(2):
        send(1, V("pool", RP(h), RP(h) + H), V("rout", H * h, H * h + H), "ar%d" % h)
        if h in OPT["hold"]:
            ops[-2]["r"] = ops[-2]["r"] + V("zi")[1]
    at("far", 0)
    s2 = 2 * SH % 128
    dma("s", [(V("rb2", p=(s2, 128)), X("rc", 0, 128 - s2, H, K)), (V("rb2", p=(0, s2)), X("rc", 128 - s2, 128, H, K))], 256)
    for h in range(2):
        send(2, V("land", LD(2, h) + 16, LD(2, h) + 16 + H), V("rb2") if h else V("rout", 0, H), "l2%d0" % h, h, 0)
    at("set", 0)
    count["set", 0] = 5
    cp(V("eo", 129, 384, 2), V("nmi"))
    SG = 256 if OPT["sg"] == 1 else -128
    UO = 256 if OPT["ur"] == 1 else 0
    lin(col(5), col(1), -1.0, 15.0)
    ts(V("sel", 144 * S0, 144 * S0 + 144), V("xi"), col(5), ALU.is_equal)
    lin(col(3), eq(DH), 1.0, eq(DL))
    lin(col(4), eq(PH), 128.0, eq(PL))
    lin(col(6), eq(PJ), 256.0, col(4))
    lin(col(7), eq(PI), 160.0, col(6))
    lin(col(10), eq(15), -0.5, 0.5)
    lin(col(11), eq(15), 0.5, -0.5)
    lin(col(12), eq(15), 16.0, 0.0)
    lin(col(18), eq(QJ), 256.0, eq(QL))
    lin(V("eq", 16, 32), V("eq", 0, 16), -1.0, 0.0)
    for t in range(2, NT + 1):
        lin(col(20 + t), eq(TG(t)), -float(H + BX(t)), col(7))
    for s, c in ([(PT, col(7)), (DS, col(3)), (HP, col(10)), (HN, col(11)), (A15, col(12)), (PQ, col(18))]
                 + [(NG + t, eq(16 + TG(t))) for t in range(1, NT + 1)] + [(PB + t, col(20 + t)) for t in range(2, NT + 1)]):
        lin(V("sel", 144 * s, 144 * s + 144), V("sel", 144 * S0, 144 * S0 + 144), c, 0.0)
    lin(col(15), col(1), -1.0, 0.0)
    lin(col(16), col(1), 1.0, 16.0)
    lin(col(17), col(1), 1.0, 16.0 - H)
    ts(V("idf"), V("xw"), 0.0, ALU.is_equal)
    ts(V("wf", p=(0, 8)), V("xf", p=(0, 8)), 0.0, ALU.is_equal)
    ts(V("plf", p=(0, 8)), V("pli", p=(0, 8)), 1.0 / 128, ALU.max)
    for m, w, c in ((IDB, 128, 1.0), (NID, 256, -1.0), (BIG, 128, 4096.0), (P2, 256, 2.0), (N2, 256, -2.0)):
        lin(V("idb", m, m + w), V("idf", 0, w), c, 0.0)
    for t in range(1, NT + 1):
        o = (-SH * t) % 128
        mm([(V("pn", 128 * (t - 1), 128 * (t - 1) + 64), V("wf", 0, 128, p=(0, 8)), V("plf", 0, 64, p=(0, 8)))])
        mm([(V("pn", 128 * (t - 1) + 64, 128 * t), V("wf", o, o + 128, p=(0, 8)), V("plf", 64, 128, p=(0, 8)))])
    cp(V("fout"), V("pn"), True)
    for t in range(1, NT):
        send(t, V("fin", 128 * (t - 1), 128 * t), V("fout", 128 * (t - 1), 128 * t), "af%d" % t)
    ts(V("blk"), V("xb"), col(15), ALU.is_equal)
    lin(V("c16"), V("mt", 0, 64), 16.0, 0.0)
    lin(V("cc"), V("mt", 0, 64), 1.0 / 64, 1.0)
    for h in range(2):
        fill(V("pool", ZP(h), ZP(h) + 16), 0.0)
    for u in range(6):
        fill(V("land", LW * u, LW * u + 16), 0.0)
    fill(V("c64"), 1.0 / 64)
    for u in range(4):
        fill(V("ab", (H + 16) * u + H, (H + 16) * (u + 1)), 16384.0)
    fill(V("n0"), 0.0)
    fill(V("mk"), 1.0)
    fill(V("mk", 0, 512, 16), 0.0)
    at("dnt", 0)
    dma("s", [(V("dnt", a, min(a + H, W)), V("tab", W, min(W + H, 2 * W - a))) for a in range(0, W, H)], 640)
    rows("dnt", 0, W, [(DH, V("zi", 0, 160)), (DL, V("zi", 160, 320))])

    tab = V("tab", 0, W)

    def index(t):
        last, n0, e0, u0 = t == NT, 128 * (t - 1), 512 * t - 384, 384 * (t - 1)
        for h in range(2):
            c, a, s = 64 * h, H * h, "AB"[h]
            if t > 1:
                at("gg" + s, t)
                gather("gg", a, tab, "nl", n0 + c, H)
                at("pu" + s, t)
                p = V("pa", c, c + 64)
                mm(wrap(p, (PT, PB + t)[h], "gg", a, H))
                ts(V("uo", u0 + 128 + c, u0 + 192 + c), p, float(H * h), ALU.add)
                lo, hi = u0 + 128 + c, u0 + 192 + c
                if OPT["ur"] == h:
                    lo, hi = min(lo, u0 + UO), max(hi, u0 + UO + 128)
                send(1, V("ui", lo, hi), V("uo", lo, hi), ("pa%d", "pb%d")[h] % t)
            elif h:
                at("ggB", t)
                gather("hh", 0, tab, "nl", 64, H)
            if h:
                at("lb", t)
                q = V("pb", 256, 320)
                mm(wrap(q, PQ, "gg" if t > 1 else "hh", a if t > 1 else 0, H))
                tt(V("lq"), q, V("eo", e0 + 129, e0 + 256, 2), ALU.max)
                cp(V("lb"), V("lq"))
                ts(V("eo", e0 + SG + 64, e0 + SG + 128), q, 1.0, ALU.is_lt, alt=(FN.Relu, -1.0, 1.0))
            for q in range(0, H, OPT["sc"]):
                e = q + OPT["sc"]
                mark = IND(V("tab"), V("lb", q // 16, e // 16)) if h else IND(tab, V("nl", n0 + q // 16, n0 + e // 16))
                if h or t == 1 or last:
                    at("mark" + s, t)
                    cp(mark, V("c0", a + q, a + e))
                else:
                    at("src", t)
                    lin(V("src", q, e), V("gg", q, e), col(3), 0.0)
                    at("markA", t)
                    tt(mark, V("src", q, e), V("c0", q, e), ALU.add)
        at("sgA", t)
        mm(wrap(V("pa", 128, 192), NG + t, "tab", W, H))
        lin(V("eo", e0 + SG, e0 + SG + 64), V("pa", 128, 192), 1.0, 1.0)
        if last or OPT["sg"] == 2:
            send(1, V("en", e0 + SG, e0 + SG + 128), V("eo", e0 + SG, e0 + SG + 128), "sg%d" % t)
        if last:
            at("fin", t)
            mm(wrap(V("pa", 192, 352), PT, "tab", 0, W))
            cp(V("uo", 1536, 1696), V("pa", 192, 352))
            send(1, V("ui", 1536, 1696), V("uo", 1536, 1696), "aw")
            return
        for h in range(2):
            c, a, s = 64 * h, H * h, "AB"[h]
            if t == 1:
                at("dn" + s, t)
                gather("gg", a, V("dnt", 0, W), "nl", c, H)
            at("du" + s, t)
            mm(wrap(V("pb", c, c + 64), DS, "gg", a, H))
            cp(V("du", c, c + 64), V("pb", c, c + 64))
            tt(V("dl", c, c + 64), V("pb", c, c + 64), V("eo", e0 + 2 * c + 1, e0 + 2 * c + 128, 2), ALU.subtract)
            at("oo" + s, t)
            gather("oo", a, tab, "du", c, H)
            at("e" + s, t)
            free = V("pb", 128 + c, 192 + c)
            mm([(free, mat(IDB), V("one", 0, 64))] + wrap(free, NG + t, "oo", a, H))
            tt(V("eo", e0 + 2 * c, e0 + 2 * c + 128, 2), free, V("dl", c, c + 64), ALU.mult)
            lo, hi = e0 + 2 * c, e0 + 2 * c + 128
            if OPT["sg"] == h:
                lo, hi = min(lo, e0 + SG), max(hi, e0 + SG + 128)
            send(1, V("en", lo, hi), V("eo", lo, hi), ("na%d", "nb%d")[h] % t)
        at("back", t)
        rows("c0", 0, K, [(PH, V("ph", 128 * t - 128, 128 * t)), (TG(t + 1), V("one"))])
        dma("s", [(V("tab", 0, W, p=(0, 128, 4)), V("dnt", p=(0, 128, 4)))], 330)

    def record(t):
        last, n0, e0, u0 = t == NT, 128 * (t - 1), 512 * t - 384, 384 * (t - 1)
        x0 = K * (t % 2)
        for h in range(2):
            c, R, Y, s = 64 * h, RP(h), YP(h), "AB"[h]
            a0 = (H + 16) * (2 * (t % 2) + h)
            pull = V("fout", 384 + c, 448 + c) if last else V("fin", n0 + c, n0 + c + 64)
            if t > 1:
                at("R" + s, t)
                gather("pool", R, V("land", LD(t, h), LD(t, h) + LW), "ui", u0 + UO + c, H, OPT["rch"])
            at("y" + s, t)
            gather("pool", Y, V("pool", W0 - (H * h if t > 1 else 0), W0 + BX(t)), "ui", u0 + c + (128 if t > 1 else 0), H)
            if not last:
                at("on" + s, t)
                for m in range(1 if t == 1 else 0, 2):
                    a = LD(t + 1, h) + 16 + H * m
                    send(1, V("land", a, a + H), V("pool", R + H * m, R + H * m + H), "l%d%d%d" % (t + 1, h, m), h if h or m else None, 2 * t - 2 + m)
            at("abs" + s, t)
            for q in range(2):
                pd = V("pd", 512 * q, 512 * q + 512)
                mm([(pd, mat(IDB), V("pool", R + 512 * q, R + 512 * q + 512)), (pd, mat(NID), V("pool", Y + 512 * q, Y + 512 * q + 512))])
                act(V("ab", a0 + 512 * q, a0 + 512 * q + 512), pd, FN.Abs)
            bb, nn, pv, gt, dd, nw = [V("pc", 512 * h + 64 * u, 512 * h + 64 * u + 64) for u in range(6)]
            ly, lr = V("pe", 128 + c, 192 + c), V("pe", 256 + c, 320 + c)
            lr_, la, ww, bond = [V(u, c, c + 64) for u in ("lr", "la", "ww", "bond")]
            nh = V("n0", 2 * c + 1, 2 * c + 128, 2)
            at("la" + s, t)
            mm(wrap(lr, A15, "pool", R, H))
            mm([(ly, mat(IDB), V("c64"))] + wrap(ly, A15, "pool", Y, H))
            lin(lr_, lr, 1.0, 1.0 / 64)
            tt(la, ly, lr_, ALU.min)
            tt(dd, ly, lr_, ALU.is_le)
            at("b" + s, t)
            for w, buf, a in ((HP, "pool", R), (HP, "pool", Y), (HN, "ab", a0)):
                mm(wrap(bb, w, buf, a, H), "b%d%d" % (t, h), (nn, nw))
            at("hold" + s, t)
            ts(bond, bb, 0.0, ALU.is_gt, alt=(FN.Sign, 1.0, 0.0))
            mm([(nn, V("blk"), bond)])
            tt(ww, bb, la, ALU.min)
            tt(pv, nn, ww, ALU.mult)
            tt(nh, pv, pull, ALU.is_lt)
            if not last:
                at("name" + s, t)
                e1 = e0 + 512 + 2 * c
                new = V("ln") if h else V("eo", e1, e1 + 128)
                scan(new, V("n0", 2 * c, 2 * c + 128), V("en", e0 + 2 * c, e0 + 2 * c + 128))
                if h:
                    mm([(nw, turn(128 - SH), V("ln", 1, 128, 2))])
                    cp(V("nl", n0 + 192, n0 + 256), nw)
                    cp(V("eo", e1 + 1, e1 + 128, 2), nw, True)
                else:
                    cp(V("nl", n0 + 128, n0 + 192), V("eo", e1 + 1, e1 + 128, 2))
            at("swap" + s, t)
            sw, sd = V("sw", c, c + 64), V("sd", c, c + 64)
            tt(gt, bb, la, ALU.is_gt)
            tt(gt, gt, V("en", e0 + SG + c, e0 + SG + 64 + c), ALU.mult)
            tt(sw, gt, nh, ALU.mult)
            tt(sd, dd, sw, ALU.mult)
            o = 0 if last else (128 - SH) * h
            u, v, x = [V("pn", 128 * k + c, 128 * k + c + 64) for k in range(3)]
            at("ur" + s, t)
            mm([(u, mat(IDB), V("cc")), (u, mat(NID + o), sw), (u, mat(P2 + o), sd)])
            lo = u0 + 384 + c
            ts(V("ur", c, c + 64) if last else V("uo", lo, lo + 64), u, float(H), ALU.mult, col(17), ALU.add)
            if not last:
                send(1, V("ui", lo, lo + 64), V("uo", lo, lo + 64), ("au%d", "av%d")[h] % t)
            at("uv" + s, t)
            mm([(v, mat(IDB), V("cc")), (v, mat(NID), sw), (v, mat(NID), sd)])
            ts(V("uv", c, c + 64), v, float(H), ALU.mult, col(16), ALU.add)
            old = V("pool", ZP(h), ZP(h) + LW)
            ch = OPT["ch"] if last else OPT["big"]
            at("X" + s, t)
            gather("pool", W0 + BX(t) + H * h, old, "uv", c, H, ch)
            if last:
                at("Z" + s, t)
                gather("rout", K + H * h, old, "ur", c, H, ch)
            at("ux" + s, t)
            mm([(x, mat(IDB), V("c16")), (x, mat(BIG), nh)])
            ts(V("ux", c, c + 64), x, col(1), ALU.add, float(H), ALU.min)
            at("exp" + s, t)
            ch = OPT["ch"] if last or h else OPT["big"]
            for q in range(0, H, ch):
                act(V("xx", x0 + H * h + q, x0 + H * h + q + ch), IND(V("ab", a0, a0 + H + 16), V("ux", c + q // 16, c + (q + ch) // 16)), FN.Exp, scale=-1.0 / 64)
        for h in range(2):
            at("sum" + "AB"[h], t)
            out, o, a = V("pe", 64 * h, 64 * h + 64), turn((SH * t * h) % 128), x0 + H * h
            if not last:
                for q in range(0, H, 512):
                    scan(V("xs", H * h + q, H * h + q + 512), V("mk"), V("xx", a + q, a + q + 512))
                cp(V("eout", n0 + 64 * h, n0 + 64 * h + 64), V("xs", H * h + 15, H * h + H, 16), True)
            else:
                if OPT["ls"][h]:
                    for q in range(0, H, 512):
                        scan(V("xs", H * h + q, H * h + q + 512), V("mk"), V("xx", a + q, a + q + 512))
                    mm([(out, o, V("xs", H * h + 15, H * h + H, 16))], "e", [V("pe", 128, 384)])
                for k in range(0, 16 * (1 - OPT["ls"][h]), 2):
                    mm([(out, o, V("xx", a + k + u, a + H, 16)) for u in range(2)], "e", [V("pe", 128, 384)])
                at("old" + "AB"[h], t)
                mm([(out, turn((SH * u * h) % 128), V("ein", 128 * u + 64 * h - 128, 128 * u + 64 * h - 64)) for u in range(1, NT)], "e", [V("pe", 128, 384)])
        at("tot", t)
        if last:
            cp(V("eout", n0, n0 + 128), V("pe", 0, 128), True)
        else:
            send(-t, V("ein", n0, n0 + 128), V("eout", n0, n0 + 128), "ae%d" % t)

    for t in range(1, NT + 1):
        index(t)
        record(t)

    dma("s", [(X("ye", 0, 128, 0, 128), V("eout", 384, 512))], 64)
    for q in range(2):
        at("wall", NT)
        for u in range(4):
            gather("wout", 640 * u + 320 * q, V("pool", W0, NP), "ui", 1536 + 40 * u + 20 * q, 320)
        at("yw", NT)
        out = V("pd", 512 * q, 512 * q + 320)
        mm([(out, mat(m), V("wout", 640 * u + 320 * q, 640 * u + 320 * q + 320)) for u, m in enumerate((IDB, NID, P2, N2))])
        cp(V("ow", 320 * q, 320 * q + 320), out, True)
        dma("s", [(X("yw", 0, 128, 320 * q, 320 * q + 320), V("ow", 320 * q, 320 * q + 320))], 160)
    at("yr", NT)
    o = (SH * NT) % 128
    mm([(V("pb"), mat(m), V("rout", K + 512 * u, K + 512 * u + 512)) for u, m in enumerate((IDB, NID, P2 + o, N2 + o))])
    cp(V("orr"), V("pb"), True)
    dma("s", [(X("yr", 0, 128, 0, 512), V("orr"))], 256)

    if "order" not in ORDER:
        ORDER["order"] = arrange(ops)
    clock = {e: {} for e in Q}
    total, hist, bank, ndma = {}, {}, {}, 0

    def wait(e, tok):
        if clock[e].get(tok[0], 0) < tok[1]:
            Q[e].wait_ge(T.sem[tok[0]], tok[1])
            for s, c in list(tok[2].items()) + [(tok[0], tok[1])]:
                if clock[e].get(s, 0) < c:
                    clock[e][s] = c

    def token(e, sem, c):
        total[sem] = total.get(sem, 0) + c
        return (sem, total[sem], dict(clock.get(e, {})))

    def write(dst, out, a, sem, local, eng):
        rid, pid = topo.addr(dst, core)
        g.remote_dma(out, a, T.sem[sem], T.sem[local], pid, rid, sum(1 << k for k in eng))
        return token("g", local, len(eng))

    nxt = T.cores[(rank + 1) % n]
    spare = [k for k in topo.engines(T.cores[rank], helper(rank, 0)) if k not in topo.engines(T.cores[rank], nxt)]
    for i, e in ORDER["order"]:
        o = ops[i]
        if role is not None:
            if o["kind"] == "send" and o["via"] == role:
                a, b = H * o["slot"], H * o["slot"] + o["a"][2]
                tok = token("-", "h%d" % o["slot"], len(spare))
                lay, nxt = role and o["d"] == 1, T.cores[(rank + o["d"]) % n]
                if lay:
                    wait("s", tok)
                    g.sync.dma_start(T.hq[SH:128, a:b], T.hop[0:128 - SH, a:b]).then_inc(T.sem["d%d" % ndma], 16)
                    g.sync.dma_start(T.hq[0:SH, a:b], T.hop[128 - SH:128, a:b]).then_inc(T.sem["d%d" % ndma], 16)
                    tok = token("s", "d%d" % ndma, 32)
                    ndma += 1
                wait("g", tok)
                write(nxt, o["out"][0], T["hq" if lay else "hop"][:, a:b], o["sem"], "sent", topo.engines(core, nxt))
            continue
        if o["kind"] == "land":
            src = T.cores[(rank - o["d"]) % n] if o["via"] is None else helper(rank - o["d"], o["via"])
            tok = token(e, o["sem"], len(topo.engines(src, core)))
            note(hist, tok, [], o["w"])
            continue
        wr = o["w"]
        if e == "p":
            wr = []
            toks = [k for k in overlap(hist, [], o["w"]) if k[0] != "ep"]
        else:
            toks = []
        toks += list(overlap(hist, o["r"], wr)) + [bank[b][0] for b in banks(o) if b in bank and bank[b][1] != e]
        for tok in sorted(toks, key=lambda k: (-len(k[2]), -k[1])):
            wait(e, tok)
        if o["kind"] == "send":
            if o["via"] is None:
                dst = T.cores[(rank + o["d"]) % n]
                again = o["a"][1][0][0] == "pool"
                tok = write(dst, o["out"][0], o["a"][0], o["sem"], "o0%d" % o["slot"] if again else "sent", topo.engines(core, dst))
                if again:
                    note(hist, tok, o["r"], [])
            else:
                a = H * o["slot"]
                tok = write(helper(rank, o["via"]), T.hop[:, a:a + o["a"][2]], o["a"][0], "h%d" % o["slot"], "o%d%d" % (o["via"], o["slot"]), spare)
                note(hist, tok, o["r"], [])
            continue
        if o["kind"] == "dma":
            sem = "d%d" % ndma
            ndma += 1
            for a, b in o["pairs"]:
                Q[e].dma_start(ap(a), ap(b)).then_inc(T.sem[sem], 16)
            tok = token(e, sem, 16 * len(o["pairs"]))
        else:
            o["calls"][e][0]().then_inc(T.sem["e" + e], 1)
            tok = token(e, "e" + e, 1)
        note(hist, tok, o["r"], o["w"], o.get("group") is not None)
        for b in banks(o):
            bank[b] = (tok, e)
    for sem in sorted(total):
        wait("g", (sem, total[sem], {}))
